import numpy as np
import ml_dtypes


def mxq(x, axis, fmt="e4m3"):
    dtype, down = {"e4m3": (ml_dtypes.float8_e4m3fn, 7), "e5m2": (ml_dtypes.float8_e5m2, 14)}[fmt]
    v = np.moveaxis(np.asarray(x, np.float32).astype(ml_dtypes.bfloat16).astype(np.float64), axis, -1)
    blocks = v.reshape(v.shape[:-1] + (-1, 32))
    amax = np.abs(blocks).max(-1, keepdims=True)
    byte = np.maximum(np.where(amax > 0, np.frexp(amax)[1] - 1 + 127, 0) - down, 1)
    scale = np.exp2(byte - 127.0)
    codes = (blocks / scale).astype(np.float32).astype(dtype).astype(np.float64)
    return np.moveaxis((codes * scale).reshape(v.shape), -1, axis)


WIDE = False


def mx_kscale(k):
    if not WIDE:
        return np.ones(k)
    levels = np.array([10, -10, 5, -5, 0])
    if k % 512:
        return np.exp2(np.random.permutation(np.resize(levels, k // 32))).repeat(32)
    a = np.empty((k // 512, 16))
    for p in range(k // 512):
        a[p, :8] = np.random.permutation(np.resize(levels, 8))
        for g in range(8):
            far = levels[np.abs(levels - a[p, g]) >= 10]
            a[p, g + 8] = far[np.random.randint(len(far))]
    return np.exp2(a.ravel()).repeat(32)


def f64(x):
    return np.asarray(x).astype(np.float64)


def striped(idx):
    return np.tile(idx.reshape(-1, 16).T, (8, 1)).astype(np.uint16)


def unstriped(offs):
    return offs[:16].T.reshape(-1).astype(np.int64)


E2M1 = np.array([0.0, 0.5, 1.0, 1.5, 2.0, 3.0, 4.0, 6.0, -0.0, -0.5, -1.0, -1.5, -2.0, -3.0, -4.0, -6.0])


def pack_weight(w, fmt):
    k, n = w.shape
    w = f64(np.asarray(w, np.float32).astype(ml_dtypes.bfloat16)).reshape(k // 32, 32, n)
    amax = np.abs(w).max(1)
    if fmt == "e4m3":
        byte = np.frexp(amax)[1] - 1 + 127 - 7
    else:
        mant, ex = np.frexp(amax / 6.0)
        byte = np.where(mant > 0.5, ex, ex - 1) + 127
    byte = np.clip(np.where(amax > 0, byte, 1), 1, 254)
    scaled = (w * np.exp2(127.0 - byte)[:, None, :]).reshape(k, n).astype(np.float32)
    by_word = np.ascontiguousarray(scaled.reshape(k // 512, 128, 4, n).transpose(0, 1, 3, 2))
    if fmt == "e4m3":
        words = by_word.astype(ml_dtypes.float8_e4m3fn).view(np.uint8)
    else:
        c = by_word.astype(ml_dtypes.float4_e2m1fn).view(np.uint8) & 0xF
        words = (c[..., 0::2] | (c[..., 1::2] << 4)).reshape(k // 512, 128, 2 * n)
    return np.ascontiguousarray(words), np.ascontiguousarray(byte.astype(np.uint8).reshape(k // 512, 16, n))


def unpack_weight(words, scales, fmt):
    g, _, n = scales.shape
    words = np.ascontiguousarray(words).reshape(g, 128, n, -1)
    if fmt == "e4m3":
        vals = words.view(ml_dtypes.float8_e4m3fn).astype(np.float64)
    else:
        nib = np.empty((g, 128, n, 4), np.uint8)
        nib[..., 0::2] = words & 0xF
        nib[..., 1::2] = words >> 4
        vals = E2M1[nib]
    vals = vals * np.repeat(np.exp2(scales.astype(np.float64) - 127.0), 8, axis=1)[..., None]
    return vals.transpose(0, 1, 3, 2).reshape(g * 512, n)


def silu(v):
    return v / (1.0 + np.exp(-np.maximum(v, -700.0)))


K, T, Q, E, C, D, H = 512, 1024, 768, 8, 256, 256, 0
N = 512


def by_expert(wq, xq, C):
    return np.concatenate([wq[e].T @ xq[:, e * C:(e + 1) * C] for e in range(E)], axis=1)


def setup_inputs():
    n = np.random.standard_normal
    s = mx_kscale(K)
    first = np.random.permutation(np.repeat(np.arange(E), T // E))
    second = (first + 1 + np.random.permutation(np.repeat(np.arange(E - 1), -(-T // (E - 1)))[:T])) % E
    while np.bincount(second, minlength=E).max() != T // E:
        load = np.bincount(second, minlength=E); hi, lo = int(load.argmax()), int(load.argmin())
        t = np.flatnonzero((second == hi) & (first != lo))[0]; second[t] = lo
    slot_token = np.empty(E * C, np.int64); pos = np.empty((2, T), np.int64); fill = np.zeros(E, np.int64)
    place = np.stack([np.random.permutation(C) for _ in range(E)])
    for r, deal in enumerate((first, second)):
        for t in np.random.permutation(T):
            e = deal[t]; j = e * C + place[e, fill[e]]; fill[e] += 1; slot_token[j] = t; pos[r, t] = j
    g = np.random.uniform(0.2, 0.8, T)
    slots2 = np.concatenate([np.random.permutation(Q)[:D] for e in range(E)])
    x = pack_weight(n((K, Q)) * s[:, None], "e4m3")
    return {
        "x_words": x[0],
        "x_scales": x[1],
        "xo": (n((K, T)) * s[:, None]).astype(np.float32),
        "w": (n((E, K, N)) / np.sqrt(K) / s[None, :, None]).astype(np.float32),
        "gate": np.stack([np.tile(g, (128, 1)), np.tile(1.0 - g, (128, 1))]).astype(np.float32),
        "offs": striped(slot_token),
        "pos1": striped(pos[0]),
        "pos2": striped(pos[1]),
        "offs2": striped(slots2),
    }


def reference(x_words, x_scales, xo, w, gate, offs, pos1, pos2, offs2):
    wq = mxq(f64(w), 1, "e4m3")
    idx, idx2 = unstriped(offs), unstriped(offs2)
    xq = mxq(f64(xo)[:, idx], 0, "e4m3")
    rq = unpack_weight(x_words, x_scales, "e4m3")[:, idx2]
    y = silu(by_expert(wq, xq, C))
    z = silu(by_expert(wq, rq, D))
    own = sum(f64(gate[r, :1]) * y[:, unstriped(p)] for r, p in enumerate((pos1, pos2)))
    return np.concatenate([own, z], axis=1)

@@ -1,0 +1,181 @@
+from contextlib import ExitStack
+
+import concourse.mybir as mybir
+
+K, T, Q, E, C, N = 512, 1024, 768, 8, 256, 512
+S = E * C
+FLOPS = 2 * 2 * K * N * S
+
+F32 = mybir.dt.float32
+BF16 = mybir.dt.bfloat16
+I32 = mybir.dt.int32
+U32 = mybir.dt.uint32
+U16 = mybir.dt.uint16
+U8 = mybir.dt.uint8
+FP8X4 = mybir.dt.float8_e4m3fn_x4
+MULT = mybir.AluOpType.mult
+ADD = mybir.AluOpType.add
+SILU = mybir.ActivationFunctionType.Silu
+
+P = 128
+CH = 512
+NCH = S // CH
+HALF = N // 2
+
+
+def tile_moe_loc_lin_silu_kernel(tc, x_words, x_scales, xo, w, gate, offs, pos1, pos2, offs2, out):
+    nc = tc.nc
+    with ExitStack() as ctx:
+        keep = ctx.enter_context(tc.tile_pool(name="keep", bufs=1))
+        ring = ctx.enter_context(tc.tile_pool(name="ring", bufs=3))
+        psum = ctx.enter_context(tc.psum_pool(name="psum", bufs=4))
+
+        offs2_t = keep.tile([P, S // 16], U16, name="offs2_t")
+        offs_t = keep.tile([P, S // 16], U16, name="offs_t")
+        pos_t = [keep.tile([P, T // 16], U16, name=f"pos_t{r}") for r in range(2)]
+        words = keep.tile([P, Q], I32, name="words")
+        sbytes = keep.tile([P, Q], U8, name="sbytes")
+        xo_raw = [ring.tile([P, 2, T], F32, name=f"xo_raw{a}", tag="big") for a in range(2)]
+        w_raw = [keep.tile([P, 4, N], F32, name=f"w_raw{e}") for e in range(E)]
+        gate_t = [keep.tile([P, T], F32, name=f"gate_t{r}") for r in range(2)]
+
+        nc.gpsimd.memset(sbytes[:], 0)
+        nc.sync.dma_start(offs2_t[:], offs2)
+        nc.sync.dma_start(words[:], x_words[0].rearrange("p t d -> p (t d)").bitcast(I32))
+        for q in range(4):
+            nc.scalar.dma_start(sbytes[32 * q : 32 * q + 4, :].bitcast(I32), x_scales[0, 4 * q : 4 * q + 4, :].bitcast(I32))
+        xo_v = xo.rearrange("(p j) t -> p j t", j=4)
+        nc.sync.dma_start(xo_raw[0][:], xo_v[:, 0:2, :])
+        nc.sync.dma_start(offs_t[:], offs)
+        nc.sync.dma_start(xo_raw[1][:], xo_v[:, 2:4, :])
+        for e in range(E):
+            nc.sync.dma_start(w_raw[e][:], w[e].rearrange("(p j) n -> p j n", j=4))
+        nc.sync.dma_start(pos_t[0][:], pos1)
+        nc.sync.dma_start(pos_t[1][:], pos2)
+        for r in range(2):
+            nc.sync.dma_start(gate_t[r][:], gate[r])
+
+        pairs = [keep.tile([P, 2 * T], BF16, name=f"pairs{a}") for a in range(2)]
+        for a in range(2):
+            nc.scalar.copy(pairs[a][:].rearrange("p (t e) -> p t e", e=2), xo_raw[a][:].rearrange("p e t -> p t e"))
+
+        own_codes = [keep.tile([P, CH], U32, name=f"own_codes{c}", align_bytes=64) for c in range(NCH)]
+        own_scales = [keep.tile([P, CH], U8, name=f"own_scales{c}", align_bytes=64) for c in range(NCH)]
+        far_codes = [keep.tile([P, CH], U32, name=f"far_codes{c}", align_bytes=64) for c in range(NCH)]
+        far_scales = [keep.tile([P, CH], U8, name=f"far_scales{c}", align_bytes=64) for c in range(NCH)]
+        planes = {}
+        grouped = {}
+
+        def gather_own(c, a):
+            if a == 0:
+                planes[c] = ring.tile([P, 2, 2 * CH], BF16, name="planes", bufs=2)
+            cols = offs_t[:, c * CH // 16 : (c + 1) * CH // 16]
+            nc.vector.tensor_copy(planes[c][:, a, :].bitcast(U32), pairs[a][:].bitcast(U32).indirect(cols))
+
+        def interleave_own(c):
+            grouped[c] = ring.tile([P, 4 * CH], BF16, name="grouped", align_bytes=64, bufs=2)
+            nc.vector.tensor_copy(
+                grouped[c][:].rearrange("p (s a e) -> p s a e", a=2, e=2),
+                planes[c][:].rearrange("p a (s e) -> p s a e", e=2),
+            )
+
+        def quantize_own(c):
+            nc.vector.quantize_mx(out=own_codes[c][:].bitcast(FP8X4), scales=own_scales[c][:], in_=grouped[c][:])
+
+        for c in range(NCH + 1):
+            if c < NCH:
+                gather_own(c, 0)
+            if c > 0:
+                interleave_own(c - 1)
+            if c < NCH:
+                gather_own(c, 1)
+            if c > 0:
+                quantize_own(c - 1)
+
+        w_codes = {}
+        w_scales = {}
+
+        def quantize_w(e, h):
+            wg = ring.tile([P, 4 * HALF], BF16, name="wg", align_bytes=64, bufs=8)
+            nc.scalar.copy(
+                wg[:].rearrange("p (c i j) -> p c j i", i=4, j=4),
+                w_raw[e][:, :, h * HALF : (h + 1) * HALF].rearrange("p j (c i) -> p c j i", i=4),
+            )
+            w_codes[e, h] = keep.tile([P, HALF], U32, name=f"w_codes{e}_{h}", align_bytes=64)
+            w_scales[e, h] = keep.tile([P, HALF], U8, name=f"w_scales{e}_{h}", align_bytes=64)
+            nc.vector.quantize_mx(out=w_codes[e, h][:].bitcast(FP8X4), scales=w_scales[e, h][:], in_=wg[:])
+
+        def experts(c, nt, codes, scales, dest, tag):
+            bank = psum.tile([P, CH], F32, name=tag)
+            h, m0 = divmod(nt * P, HALF)
+            for u in range(2):
+                e = 2 * c + u
+                nc.tensor.matmul_mx(
+                    out=bank[:, u * C : (u + 1) * C],
+                    lhsT=w_codes[e, h][:, m0 : m0 + P].bitcast(FP8X4),
+                    lhsT_scale=w_scales[e, h][:, m0 : m0 + P],
+                    rhs=codes[c][:, u * C : (u + 1) * C].bitcast(FP8X4),
+                    rhs_scale=scales[c][:, u * C : (u + 1) * C],
+                    start=True,
+                    stop=True,
+                )
+            nc.scalar.activation(dest, bank[:], SILU)
+
+        y = [keep.tile([P, S], F32, name=f"y{nt}") for nt in range(4)]
+
+        def own_tile(c, nt):
+            experts(c, nt, own_codes, own_scales, y[nt][:, c * CH : (c + 1) * CH], "ybank")
+
+        def far_tile(nt):
+            z = ring.tile([P, 2, 2 * CH], F32, name="z", tag="big")
+            for cc in range(2):
+                for u in range(2):
+                    experts(2 * cc + u, nt, far_codes, far_scales, z[:, cc, u * CH : (u + 1) * CH], "zbank")
+                nc.sync.dma_start(out[nt * P : (nt + 1) * P, T + cc * 2 * CH : T + (cc + 1) * 2 * CH], z[:, cc, :])
+
+        for c in range(NCH):
+            quantize_w(2 * c, 0)
+            quantize_w(2 * c + 1, 0)
+            own_tile(c, 0)
+            own_tile(c, 1)
+        for c in range(NCH):
+            cols = offs2_t[:, c * CH // 16 : (c + 1) * CH // 16]
+            nc.vector.tensor_copy(far_codes[c][:], words[:].bitcast(U32).indirect(cols))
+            nc.vector.tensor_copy(far_scales[c][:], sbytes[:].indirect(cols))
+
+
+        for c in range(NCH):
+            quantize_w(2 * c, 1)
+            quantize_w(2 * c + 1, 1)
+            own_tile(c, 2)
+        far_tile(0)
+        for c in range(NCH):
+            own_tile(c, 3)
+
+        TH = 512
+        steps = [(nt, t0) for nt in range(4) for t0 in range(0, T, TH)]
+        prods = {}
+
+        def weigh(i, r):
+            nt, t0 = steps[i]
+            prods[i, r] = ring.tile([P, TH], F32, name=f"prod{r}")
+            nc.vector.tensor_tensor(
+                prods[i, r][:], y[nt][:].indirect(pos_t[r][:, t0 // 16 : (t0 + TH) // 16]), gate_t[r][:, t0 : t0 + TH], MULT
+            )
+
+        def add_store(i):
+            nt, t0 = steps[i]
+            o = ring.tile([P, TH], F32, name="o")
+            nc.vector.tensor_tensor(o[:], prods[i, 0][:], prods[i, 1][:], ADD)
+            nc.sync.dma_start(out[nt * P : (nt + 1) * P, t0 : t0 + TH], o[:])
+
+        for i in range(len(steps) + 1):
+            if i < len(steps):
+                weigh(i, 0)
+            if i > 0:
+                add_store(i - 1)
+            if i < len(steps):
+                weigh(i, 1)
+
+        for nt in range(1, 4):
+            far_tile(nt)

@@ -28,28 +28,31 @@ def tile_moe_loc_lin_silu_kernel(tc, x_words, x_scales, xo, w, gate, offs, pos1,
     with ExitStack() as ctx:
         keep = ctx.enter_context(tc.tile_pool(name="keep", bufs=1))
         ring = ctx.enter_context(tc.tile_pool(name="ring", bufs=3))
-        psum = ctx.enter_context(tc.psum_pool(name="psum", bufs=4))
+        psum = ctx.enter_context(tc.psum_pool(name="psum", bufs=1))
 
         offs2_t = keep.tile([P, S // 16], U16, name="offs2_t")
         offs_t = keep.tile([P, S // 16], U16, name="offs_t")
         pos_t = [keep.tile([P, T // 16], U16, name=f"pos_t{r}") for r in range(2)]
         words = keep.tile([P, Q], I32, name="words")
-        sbytes = keep.tile([P, Q], U8, name="sbytes")
-        xo_raw = [ring.tile([P, 2, T], F32, name=f"xo_raw{a}", tag="big") for a in range(2)]
-        w_raw = [keep.tile([P, 4, N], F32, name=f"w_raw{e}") for e in range(E)]
+        sbytes = keep.tile([P, Q // 4], I32, name="sbytes")
+        xo_raw = [keep.tile([P, 2, T], F32, name=f"xo_raw{a}") for a in range(2)]
+        w_raw = [keep.tile([P, 4, N], F32, name=f"w_raw{e}", tag=f"big{e}") for e in range(E)]
         gate_t = [keep.tile([P, T], F32, name=f"gate_t{r}") for r in range(2)]
 
-        nc.gpsimd.memset(sbytes[:], 0)
+        warm = keep.tile([P, 16], F32, name="warm")
+        nc.vector.memset(warm[:, 0:8], 0.0)
+        nc.scalar.activation(warm[:, 8:16], warm[:, 0:8], SILU)
+        nc.vector.memset(sbytes[:], 0)
         nc.sync.dma_start(offs2_t[:], offs2)
         nc.sync.dma_start(words[:], x_words[0].rearrange("p t d -> p (t d)").bitcast(I32))
-        for q in range(4):
-            nc.scalar.dma_start(sbytes[32 * q : 32 * q + 4, :].bitcast(I32), x_scales[0, 4 * q : 4 * q + 4, :].bitcast(I32))
         xo_v = xo.rearrange("(p j) t -> p j t", j=4)
         nc.sync.dma_start(xo_raw[0][:], xo_v[:, 0:2, :])
         nc.sync.dma_start(offs_t[:], offs)
         nc.sync.dma_start(xo_raw[1][:], xo_v[:, 2:4, :])
         for e in range(E):
             nc.sync.dma_start(w_raw[e][:], w[e].rearrange("(p j) n -> p j n", j=4))
+        for q in range(4):
+            nc.sync.dma_start(sbytes[32 * q : 32 * q + 4, :], x_scales[0, 4 * q : 4 * q + 4, :].bitcast(I32))
         nc.sync.dma_start(pos_t[0][:], pos1)
         nc.sync.dma_start(pos_t[1][:], pos2)
         for r in range(2):
@@ -82,38 +85,26 @@ def tile_moe_loc_lin_silu_kernel(tc, x_words, x_scales, xo, w, gate, offs, pos1,
         def quantize_own(c):
             nc.vector.quantize_mx(out=own_codes[c][:].bitcast(FP8X4), scales=own_scales[c][:], in_=grouped[c][:])
 
-        for c in range(NCH + 1):
-            if c < NCH:
-                gather_own(c, 0)
-            if c > 0:
-                interleave_own(c - 1)
-            if c < NCH:
-                gather_own(c, 1)
-            if c > 0:
-                quantize_own(c - 1)
+        w_codes = [keep.tile([P, N], U32, name=f"w_codes{e}", align_bytes=64) for e in range(E)]
+        w_scales = [keep.tile([P, N], U8, name=f"w_scales{e}", align_bytes=64) for e in range(E)]
 
-        w_codes = {}
-        w_scales = {}
-
-        def quantize_w(e, h):
-            wg = ring.tile([P, 4 * HALF], BF16, name="wg", align_bytes=64, bufs=8)
+        def quantize_w(e):
+            wg = keep.tile([P, 4 * N], BF16, name=f"wg{e}", align_bytes=64)
             nc.scalar.copy(
                 wg[:].rearrange("p (c i j) -> p c j i", i=4, j=4),
-                w_raw[e][:, :, h * HALF : (h + 1) * HALF].rearrange("p j (c i) -> p c j i", i=4),
+                w_raw[e][:].rearrange("p j (c i) -> p c j i", i=4),
             )
-            w_codes[e, h] = keep.tile([P, HALF], U32, name=f"w_codes{e}_{h}", align_bytes=64)
-            w_scales[e, h] = keep.tile([P, HALF], U8, name=f"w_scales{e}_{h}", align_bytes=64)
-            nc.vector.quantize_mx(out=w_codes[e, h][:].bitcast(FP8X4), scales=w_scales[e, h][:], in_=wg[:])
+            nc.vector.quantize_mx(out=w_codes[e][:].bitcast(FP8X4), scales=w_scales[e][:], in_=wg[:])
 
-        def experts(c, nt, codes, scales, dest, tag):
-            bank = psum.tile([P, CH], F32, name=tag)
-            h, m0 = divmod(nt * P, HALF)
+        def experts(c, nt, codes, scales, dest):
+            bank = psum.tile([P, CH], F32, name=f"bank{c}")
+            m0 = nt * P
             for u in range(2):
                 e = 2 * c + u
                 nc.tensor.matmul_mx(
                     out=bank[:, u * C : (u + 1) * C],
-                    lhsT=w_codes[e, h][:, m0 : m0 + P].bitcast(FP8X4),
-                    lhsT_scale=w_scales[e, h][:, m0 : m0 + P],
+                    lhsT=w_codes[e][:, m0 : m0 + P].bitcast(FP8X4),
+                    lhsT_scale=w_scales[e][:, m0 : m0 + P],
                     rhs=codes[c][:, u * C : (u + 1) * C].bitcast(FP8X4),
                     rhs_scale=scales[c][:, u * C : (u + 1) * C],
                     start=True,
@@ -121,36 +112,39 @@ def tile_moe_loc_lin_silu_kernel(tc, x_words, x_scales, xo, w, gate, offs, pos1,
                 )
             nc.scalar.activation(dest, bank[:], SILU)
 
-        y = [keep.tile([P, S], F32, name=f"y{nt}") for nt in range(4)]
-
-        def own_tile(c, nt):
-            experts(c, nt, own_codes, own_scales, y[nt][:, c * CH : (c + 1) * CH], "ybank")
-
-        def far_tile(nt):
-            z = ring.tile([P, 2, 2 * CH], F32, name="z", tag="big")
-            for cc in range(2):
-                for u in range(2):
-                    experts(2 * cc + u, nt, far_codes, far_scales, z[:, cc, u * CH : (u + 1) * CH], "zbank")
-                nc.sync.dma_start(out[nt * P : (nt + 1) * P, T + cc * 2 * CH : T + (cc + 1) * 2 * CH], z[:, cc, :])
+        def far_cols(c):
+            return offs2_t[:, c * CH // 16 : (c + 1) * CH // 16]
 
         for c in range(NCH):
-            quantize_w(2 * c, 0)
-            quantize_w(2 * c + 1, 0)
-            own_tile(c, 0)
-            own_tile(c, 1)
-        for c in range(NCH):
-            cols = offs2_t[:, c * CH // 16 : (c + 1) * CH // 16]
-            nc.vector.tensor_copy(far_codes[c][:], words[:].bitcast(U32).indirect(cols))
-            nc.vector.tensor_copy(far_scales[c][:], sbytes[:].indirect(cols))
+            nc.vector.tensor_copy(far_codes[c][:], words[:].bitcast(U32).indirect(far_cols(c)))
 
+        gather_own(0, 0)
+        gather_own(0, 1)
+        for c in range(NCH):
+            interleave_own(c)
+            quantize_w(2 * c)
+            quantize_own(c)
+            quantize_w(2 * c + 1)
+            if c + 1 < NCH:
+                gather_own(c + 1, 0)
+                gather_own(c + 1, 1)
 
         for c in range(NCH):
-            quantize_w(2 * c, 1)
-            quantize_w(2 * c + 1, 1)
-            own_tile(c, 2)
-        far_tile(0)
-        for c in range(NCH):
-            own_tile(c, 3)
+            nc.vector.tensor_copy(far_scales[c][:], sbytes[:].bitcast(U8).indirect(far_cols(c)))
+
+        y = []
+        for nt in range(4):
+            y.append(keep.tile([P, S], F32, name=f"y{nt}", tag=f"big{E - 1 - nt}"))
+            for c in range(NCH):
+                experts(c, nt, own_codes, own_scales, y[nt][:, c * CH : (c + 1) * CH])
+
+        for nt in range(4):
+            z = keep.tile([P, S], F32, name=f"z{nt}", tag=f"big{nt}")
+            for c in range(NCH):
+                experts(c, nt, far_codes, far_scales, z[:, c * CH : (c + 1) * CH])
+                if c % 2:
+                    cols = slice((c - 1) * CH, (c + 1) * CH)
+                    nc.gpsimd.dma_start(out[nt * P : (nt + 1) * P, T + cols.start : T + cols.stop], z[:, cols])
 
         TH = 512
         steps = [(nt, t0) for nt in range(4) for t0 in range(0, T, TH)]
@@ -176,6 +170,3 @@ def tile_moe_loc_lin_silu_kernel(tc, x_words, x_scales, xo, w, gate, offs, pos1,
                 add_store(i - 1)
             if i < len(steps):
                 weigh(i, 1)
-
-        for nt in range(1, 4):
-            far_tile(nt)

@@ -1,6 +1,7 @@
 from contextlib import ExitStack
 
 import concourse.mybir as mybir
+from concourse.masks import make_identity
 
 K, T, Q, E, C, N = 512, 1024, 768, 8, 256, 512
 S = E * C
@@ -21,6 +22,13 @@ P = 128
 CH = 512
 NCH = S // CH
 HALF = N // 2
+WHOLE = 4
+ON_SCALAR = ()
+PB = 3
+ZG = 0
+PHASES = "y0 y1 L z0 y2 z1 y3 z2 z3".split()
+ON_PE = 2
+TAIL = "e0 e1 e2 e3 e4 e5 e6 g1 e7 s l4 p l5 l6 l7 g0".split()
 
 
 def tile_moe_loc_lin_silu_kernel(tc, x_words, x_scales, xo, w, gate, offs, pos1, pos2, offs2, out):
@@ -36,7 +44,15 @@ def tile_moe_loc_lin_silu_kernel(tc, x_words, x_scales, xo, w, gate, offs, pos1,
         words = keep.tile([P, Q], I32, name="words")
         sbytes = keep.tile([P, Q // 4], I32, name="sbytes")
         xo_raw = [keep.tile([P, 2, T], F32, name=f"xo_raw{a}") for a in range(2)]
-        w_raw = [keep.tile([P, 4, N], F32, name=f"w_raw{e}", tag=f"big{e}") for e in range(E)]
+        early = [(e, 0, N) for e in range(WHOLE)] + [(e, 0, HALF) for e in range(WHOLE, E)]
+        late = [(e, HALF, HALF) for e in range(WHOLE, E)]
+        w_raw = {}
+
+        def load_w(piece):
+            e, n0, width = piece
+            w_raw[piece] = keep.tile([P, 4, width], F32, name=f"w_raw{e}_{n0}", tag=f"big{e}" if n0 == 0 else f"late{e}")
+            nc.sync.dma_start(w_raw[piece][:], w[e].rearrange("(p j) n -> p j n", j=4)[:, :, n0 : n0 + width])
+
         gate_t = [keep.tile([P, T], F32, name=f"gate_t{r}") for r in range(2)]
 
         warm = keep.tile([P, 16], F32, name="warm")
@@ -49,14 +65,19 @@ def tile_moe_loc_lin_silu_kernel(tc, x_words, x_scales, xo, w, gate, offs, pos1,
         nc.sync.dma_start(xo_raw[0][:], xo_v[:, 0:2, :])
         nc.sync.dma_start(offs_t[:], offs)
         nc.sync.dma_start(xo_raw[1][:], xo_v[:, 2:4, :])
-        for e in range(E):
-            nc.sync.dma_start(w_raw[e][:], w[e].rearrange("(p j) n -> p j n", j=4))
-        for q in range(4):
-            nc.sync.dma_start(sbytes[32 * q : 32 * q + 4, :], x_scales[0, 4 * q : 4 * q + 4, :].bitcast(I32))
-        nc.sync.dma_start(pos_t[0][:], pos1)
-        nc.sync.dma_start(pos_t[1][:], pos2)
-        for r in range(2):
-            nc.sync.dma_start(gate_t[r][:], gate[r])
+        for item in TAIL:
+            if item == "s":
+                for q in range(4):
+                    nc.sync.dma_start(sbytes[32 * q : 32 * q + 4, :], x_scales[0, 4 * q : 4 * q + 4, :].bitcast(I32))
+            elif item == "p":
+                nc.sync.dma_start(pos_t[0][:], pos1)
+                nc.sync.dma_start(pos_t[1][:], pos2)
+            elif item[0] == "g":
+                nc.sync.dma_start(gate_t[int(item[1])][:], gate[int(item[1])])
+            elif item[0] == "e":
+                load_w(early[int(item[1])])
+            else:
+                load_w(late[int(item[1]) - WHOLE])
 
         pairs = [keep.tile([P, 2 * T], BF16, name=f"pairs{a}") for a in range(2)]
         for a in range(2):
@@ -71,13 +92,14 @@ def tile_moe_loc_lin_silu_kernel(tc, x_words, x_scales, xo, w, gate, offs, pos1,
 
         def gather_own(c, a):
             if a == 0:
-                planes[c] = ring.tile([P, 2, 2 * CH], BF16, name="planes", bufs=2)
+                planes[c] = ring.tile([P, 2, 2 * CH], BF16, name="planes", bufs=PB)
             cols = offs_t[:, c * CH // 16 : (c + 1) * CH // 16]
             nc.vector.tensor_copy(planes[c][:, a, :].bitcast(U32), pairs[a][:].bitcast(U32).indirect(cols))
 
         def interleave_own(c):
             grouped[c] = ring.tile([P, 4 * CH], BF16, name="grouped", align_bytes=64, bufs=2)
-            nc.vector.tensor_copy(
+            copy = nc.scalar.copy if c in ON_SCALAR else nc.vector.tensor_copy
+            copy(
                 grouped[c][:].rearrange("p (s a e) -> p s a e", a=2, e=2),
                 planes[c][:].rearrange("p a (s e) -> p s a e", e=2),
             )
@@ -88,13 +110,15 @@ def tile_moe_loc_lin_silu_kernel(tc, x_words, x_scales, xo, w, gate, offs, pos1,
         w_codes = [keep.tile([P, N], U32, name=f"w_codes{e}", align_bytes=64) for e in range(E)]
         w_scales = [keep.tile([P, N], U8, name=f"w_scales{e}", align_bytes=64) for e in range(E)]
 
-        def quantize_w(e):
-            wg = keep.tile([P, 4 * N], BF16, name=f"wg{e}", align_bytes=64)
+        def quantize_w(piece):
+            e, n0, width = piece
+            wg = keep.tile([P, 4 * width], BF16, name=f"wg{e}_{n0}", align_bytes=64)
             nc.scalar.copy(
                 wg[:].rearrange("p (c i j) -> p c j i", i=4, j=4),
-                w_raw[e][:].rearrange("p j (c i) -> p c j i", i=4),
+                w_raw[piece][:].rearrange("p j (c i) -> p c j i", i=4),
             )
-            nc.vector.quantize_mx(out=w_codes[e][:].bitcast(FP8X4), scales=w_scales[e][:], in_=wg[:])
+            cols = slice(n0, n0 + width)
+            nc.vector.quantize_mx(out=w_codes[e][:, cols].bitcast(FP8X4), scales=w_scales[e][:, cols], in_=wg[:])
 
         def experts(c, nt, codes, scales, dest):
             bank = psum.tile([P, CH], F32, name=f"bank{c}")
@@ -122,9 +146,9 @@ def tile_moe_loc_lin_silu_kernel(tc, x_words, x_scales, xo, w, gate, offs, pos1,
         gather_own(0, 1)
         for c in range(NCH):
             interleave_own(c)
-            quantize_w(2 * c)
+            quantize_w(early[2 * c])
             quantize_own(c)
-            quantize_w(2 * c + 1)
+            quantize_w(early[2 * c + 1])
             if c + 1 < NCH:
                 gather_own(c + 1, 0)
                 gather_own(c + 1, 1)
@@ -132,33 +156,43 @@ def tile_moe_loc_lin_silu_kernel(tc, x_words, x_scales, xo, w, gate, offs, pos1,
         for c in range(NCH):
             nc.vector.tensor_copy(far_scales[c][:], sbytes[:].bitcast(U8).indirect(far_cols(c)))
 
-        y = []
-        for nt in range(4):
-            y.append(keep.tile([P, S], F32, name=f"y{nt}", tag=f"big{E - 1 - nt}"))
-            for c in range(NCH):
-                experts(c, nt, own_codes, own_scales, y[nt][:, c * CH : (c + 1) * CH])
+        y = {}
+        for item in PHASES:
+            if item == "L":
+                for piece in late:
+                    quantize_w(piece)
+                continue
+            nt = int(item[1])
+            if item[0] == "y":
+                y[nt] = keep.tile([P, S], F32, name=f"y{nt}", tag=f"big{E - 1 - nt}")
+                for c in range(NCH):
+                    experts(c, nt, own_codes, own_scales, y[nt][:, c * CH : (c + 1) * CH])
+            else:
+                z = keep.tile([P, S], F32, name=f"z{nt}", tag=f"big{nt}")
+                for c in range(NCH):
+                    experts(c, nt, far_codes, far_scales, z[:, c * CH : (c + 1) * CH])
+                    if c % 2:
+                        cols = slice((c - 1) * CH, (c + 1) * CH)
+                        queue = nc.gpsimd if nt < ZG else nc.scalar
+                        queue.dma_start(out[nt * P : (nt + 1) * P, T + cols.start : T + cols.stop], z[:, cols])
 
-        for nt in range(4):
-            z = keep.tile([P, S], F32, name=f"z{nt}", tag=f"big{nt}")
-            for c in range(NCH):
-                experts(c, nt, far_codes, far_scales, z[:, c * CH : (c + 1) * CH])
-                if c % 2:
-                    cols = slice((c - 1) * CH, (c + 1) * CH)
-                    nc.gpsimd.dma_start(out[nt * P : (nt + 1) * P, T + cols.start : T + cols.stop], z[:, cols])
-
-        TH = 512
-        steps = [(nt, t0) for nt in range(4) for t0 in range(0, T, TH)]
+        steps = [(nt, t0, 512) for nt in range(4) for t0 in range(0, T, 512)][:-1] + [(3, 512, 256), (3, 768, 256)]
+        ident = keep.tile([P, P], F32, name="ident")
+        make_identity(nc, ident[:])
         prods = {}
 
         def weigh(i, r):
-            nt, t0 = steps[i]
-            prods[i, r] = ring.tile([P, TH], F32, name=f"prod{r}")
+            nt, t0, TH = steps[i]
+            if i < ON_PE:
+                prods[i, r] = keep.tile([P, TH], F32, name=f"kept{i}_{r}", tag=f"wg{i + WHOLE * r}_0", align_bytes=64)
+            else:
+                prods[i, r] = ring.tile([P, TH], F32, name=f"prod{r}")
             nc.vector.tensor_tensor(
                 prods[i, r][:], y[nt][:].indirect(pos_t[r][:, t0 // 16 : (t0 + TH) // 16]), gate_t[r][:, t0 : t0 + TH], MULT
             )
 
         def add_store(i):
-            nt, t0 = steps[i]
+            nt, t0, TH = steps[i]
             o = ring.tile([P, TH], F32, name="o")
             nc.vector.tensor_tensor(o[:], prods[i, 0][:], prods[i, 1][:], ADD)
             nc.sync.dma_start(out[nt * P : (nt + 1) * P, t0 : t0 + TH], o[:])
@@ -166,7 +200,34 @@ def tile_moe_loc_lin_silu_kernel(tc, x_words, x_scales, xo, w, gate, offs, pos1,
         for i in range(len(steps) + 1):
             if i < len(steps):
                 weigh(i, 0)
-            if i > 0:
+            if i > ON_PE:
                 add_store(i - 1)
             if i < len(steps):
                 weigh(i, 1)
+
+        turned = {}
+
+        def add_turned(i):
+            nt, t0, TH = steps[i]
+            bank = psum.tile([P, TH], F32, name=f"bank{i % NCH}")
+            for b in range(0, TH, P):
+                for r in range(2):
+                    nc.tensor.matmul(
+                        bank[:, b : b + P], prods[i, r][:, b : b + P], ident[:], start=r == 0, stop=r == 1, is_transpose=True
+                    )
+            turned[i] = keep.tile([P, TH], F32, name=f"turned{i}", tag=f"late{WHOLE + i}")
+            nc.scalar.copy(turned[i][:], bank[:])
+
+        def turn_back(i):
+            nt, t0, TH = steps[i]
+            bank = psum.tile([P, TH], F32, name="back", bufs=3)
+            for b in range(0, TH, P):
+                nc.tensor.transpose(bank[:, b : b + P], turned[i][:, b : b + P], ident[:])
+            o = keep.tile([P, TH], F32, name=f"back{i}", tag=f"wg{WHOLE + i}_{HALF}", align_bytes=64)
+            nc.scalar.copy(o[:], bank[:])
+            nc.scalar.dma_start(out[nt * P : (nt + 1) * P, t0 : t0 + TH], o[:])
+
+        for i in range(ON_PE):
+            add_turned(i)
+        for i in range(ON_PE):
+            turn_back(i)

@@ -23,26 +23,27 @@ CH = 512
 NCH = S // CH
 HALF = N // 2
 WHOLE = 4
-ON_SCALAR = ()
 PB = 3
-ZG = 0
-PHASES = "y0 y1 L z0 y2 z1 y3 z2 z3".split()
+FG = 512
+QW = 768
+TAIL = "e0 e1 e2 e3 e4 e5 e6 e7 s l4 g1 l5 p l6 l7 g0".split()
+PHASES = "y0 y1 z0 L z1 y2 y3 z2 z3".split()
+ZQ = "yyyy"
+STEPS = [(0, 0, 1024), (1, 0, 512), (1, 512, 512), (2, 0, 1024), (3, 0, 512), (3, 512, 256), (3, 768, 256)]
 ON_PE = 2
-TAIL = "e0 e1 e2 e3 e4 e5 e6 g1 e7 s l4 p l5 l6 l7 g0".split()
 
 
 def tile_moe_loc_lin_silu_kernel(tc, x_words, x_scales, xo, w, gate, offs, pos1, pos2, offs2, out):
     nc = tc.nc
     with ExitStack() as ctx:
         keep = ctx.enter_context(tc.tile_pool(name="keep", bufs=1))
-        ring = ctx.enter_context(tc.tile_pool(name="ring", bufs=3))
         psum = ctx.enter_context(tc.psum_pool(name="psum", bufs=1))
 
         offs2_t = keep.tile([P, S // 16], U16, name="offs2_t")
         offs_t = keep.tile([P, S // 16], U16, name="offs_t")
         pos_t = [keep.tile([P, T // 16], U16, name=f"pos_t{r}") for r in range(2)]
-        words = keep.tile([P, Q], I32, name="words")
-        sbytes = keep.tile([P, Q // 4], I32, name="sbytes")
+        words = keep.tile([P, QW], I32, name="words")
+        sbytes = keep.tile([P, QW // 4], I32, name="sbytes")
         xo_raw = [keep.tile([P, 2, T], F32, name=f"xo_raw{a}") for a in range(2)]
         early = [(e, 0, N) for e in range(WHOLE)] + [(e, 0, HALF) for e in range(WHOLE, E)]
         late = [(e, HALF, HALF) for e in range(WHOLE, E)]
@@ -59,8 +60,10 @@ def tile_moe_loc_lin_silu_kernel(tc, x_words, x_scales, xo, w, gate, offs, pos1,
         nc.vector.memset(warm[:, 0:8], 0.0)
         nc.scalar.activation(warm[:, 8:16], warm[:, 0:8], SILU)
         nc.vector.memset(sbytes[:], 0)
+        if QW > Q:
+            nc.vector.memset(words[:, Q:], 0)
         nc.sync.dma_start(offs2_t[:], offs2)
-        nc.sync.dma_start(words[:], x_words[0].rearrange("p t d -> p (t d)").bitcast(I32))
+        nc.sync.dma_start(words[:, :Q], x_words[0].rearrange("p t d -> p (t d)").bitcast(I32))
         xo_v = xo.rearrange("(p j) t -> p j t", j=4)
         nc.sync.dma_start(xo_raw[0][:], xo_v[:, 0:2, :])
         nc.sync.dma_start(offs_t[:], offs)
@@ -68,7 +71,7 @@ def tile_moe_loc_lin_silu_kernel(tc, x_words, x_scales, xo, w, gate, offs, pos1,
         for item in TAIL:
             if item == "s":
                 for q in range(4):
-                    nc.sync.dma_start(sbytes[32 * q : 32 * q + 4, :], x_scales[0, 4 * q : 4 * q + 4, :].bitcast(I32))
+                    nc.sync.dma_start(sbytes[32 * q : 32 * q + 4, : Q // 4], x_scales[0, 4 * q : 4 * q + 4, :].bitcast(I32))
             elif item == "p":
                 nc.sync.dma_start(pos_t[0][:], pos1)
                 nc.sync.dma_start(pos_t[1][:], pos2)
@@ -83,29 +86,29 @@ def tile_moe_loc_lin_silu_kernel(tc, x_words, x_scales, xo, w, gate, offs, pos1,
         for a in range(2):
             nc.scalar.copy(pairs[a][:].rearrange("p (t e) -> p t e", e=2), xo_raw[a][:].rearrange("p e t -> p t e"))
 
-        own_codes = [keep.tile([P, CH], U32, name=f"own_codes{c}", align_bytes=64) for c in range(NCH)]
-        own_scales = [keep.tile([P, CH], U8, name=f"own_scales{c}", align_bytes=64) for c in range(NCH)]
-        far_codes = [keep.tile([P, CH], U32, name=f"far_codes{c}", align_bytes=64) for c in range(NCH)]
-        far_scales = [keep.tile([P, CH], U8, name=f"far_scales{c}", align_bytes=64) for c in range(NCH)]
+        own_codes = keep.tile([P, S], U32, name="own_codes", align_bytes=64)
+        own_scales = keep.tile([P, S], U8, name="own_scales", align_bytes=64)
+        far_codes = keep.tile([P, S], U32, name="far_codes", align_bytes=64)
+        far_scales = keep.tile([P, S], U8, name="far_scales", align_bytes=64)
         planes = {}
         grouped = {}
 
         def gather_own(c, a):
             if a == 0:
-                planes[c] = ring.tile([P, 2, 2 * CH], BF16, name="planes", bufs=PB)
+                planes[c] = keep.tile([P, 2, 2 * CH], BF16, name="planes", bufs=PB)
             cols = offs_t[:, c * CH // 16 : (c + 1) * CH // 16]
             nc.vector.tensor_copy(planes[c][:, a, :].bitcast(U32), pairs[a][:].bitcast(U32).indirect(cols))
 
         def interleave_own(c):
-            grouped[c] = ring.tile([P, 4 * CH], BF16, name="grouped", align_bytes=64, bufs=2)
-            copy = nc.scalar.copy if c in ON_SCALAR else nc.vector.tensor_copy
-            copy(
-                grouped[c][:].rearrange("p (s a e) -> p s a e", a=2, e=2),
-                planes[c][:].rearrange("p a (s e) -> p s a e", e=2),
+            grouped[c] = keep.tile([P, 4 * CH], BF16, name="grouped", align_bytes=64, bufs=2)
+            nc.vector.tensor_copy(
+                grouped[c][:].bitcast(I32).rearrange("p (s a) -> p s a", a=2),
+                planes[c][:].bitcast(I32).rearrange("p a s -> p s a"),
             )
 
         def quantize_own(c):
-            nc.vector.quantize_mx(out=own_codes[c][:].bitcast(FP8X4), scales=own_scales[c][:], in_=grouped[c][:])
+            cols = slice(c * CH, (c + 1) * CH)
+            nc.vector.quantize_mx(out=own_codes[:, cols].bitcast(FP8X4), scales=own_scales[:, cols], in_=grouped[c][:])
 
         w_codes = [keep.tile([P, N], U32, name=f"w_codes{e}", align_bytes=64) for e in range(E)]
         w_scales = [keep.tile([P, N], U8, name=f"w_scales{e}", align_bytes=64) for e in range(E)]
@@ -129,18 +132,15 @@ def tile_moe_loc_lin_silu_kernel(tc, x_words, x_scales, xo, w, gate, offs, pos1,
                     out=bank[:, u * C : (u + 1) * C],
                     lhsT=w_codes[e][:, m0 : m0 + P].bitcast(FP8X4),
                     lhsT_scale=w_scales[e][:, m0 : m0 + P],
-                    rhs=codes[c][:, u * C : (u + 1) * C].bitcast(FP8X4),
-                    rhs_scale=scales[c][:, u * C : (u + 1) * C],
+                    rhs=codes[:, e * C : (e + 1) * C].bitcast(FP8X4),
+                    rhs_scale=scales[:, e * C : (e + 1) * C],
                     start=True,
                     stop=True,
                 )
             nc.scalar.activation(dest, bank[:], SILU)
 
-        def far_cols(c):
-            return offs2_t[:, c * CH // 16 : (c + 1) * CH // 16]
-
-        for c in range(NCH):
-            nc.vector.tensor_copy(far_codes[c][:], words[:].bitcast(U32).indirect(far_cols(c)))
+        for s0 in range(0, S, FG):
+            nc.vector.tensor_copy(far_codes[:, s0 : s0 + FG], words[:].bitcast(U32).indirect(offs2_t[:, s0 // 16 : (s0 + FG) // 16]))
 
         gather_own(0, 0)
         gather_own(0, 1)
@@ -153,9 +153,10 @@ def tile_moe_loc_lin_silu_kernel(tc, x_words, x_scales, xo, w, gate, offs, pos1,
                 gather_own(c + 1, 0)
                 gather_own(c + 1, 1)
 
-        for c in range(NCH):
-            nc.vector.tensor_copy(far_scales[c][:], sbytes[:].bitcast(U8).indirect(far_cols(c)))
+        for s0 in range(0, S, FG):
+            nc.vector.tensor_copy(far_scales[:, s0 : s0 + FG], sbytes[:].bitcast(U8).indirect(offs2_t[:, s0 // 16 : (s0 + FG) // 16]))
 
+        queues = {"g": nc.gpsimd, "s": nc.scalar, "y": nc.sync}
         y = {}
         for item in PHASES:
             if item == "L":
@@ -173,61 +174,52 @@ def tile_moe_loc_lin_silu_kernel(tc, x_words, x_scales, xo, w, gate, offs, pos1,
                     experts(c, nt, far_codes, far_scales, z[:, c * CH : (c + 1) * CH])
                     if c % 2:
                         cols = slice((c - 1) * CH, (c + 1) * CH)
-                        queue = nc.gpsimd if nt < ZG else nc.scalar
-                        queue.dma_start(out[nt * P : (nt + 1) * P, T + cols.start : T + cols.stop], z[:, cols])
+                        queues[ZQ[nt]].dma_start(out[nt * P : (nt + 1) * P, T + cols.start : T + cols.stop], z[:, cols])
 
-        steps = [(nt, t0, 512) for nt in range(4) for t0 in range(0, T, 512)][:-1] + [(3, 512, 256), (3, 768, 256)]
         ident = keep.tile([P, P], F32, name="ident")
         make_identity(nc, ident[:])
         prods = {}
 
         def weigh(i, r):
-            nt, t0, TH = steps[i]
+            nt, t0, width = STEPS[i]
             if i < ON_PE:
-                prods[i, r] = keep.tile([P, TH], F32, name=f"kept{i}_{r}", tag=f"wg{i + WHOLE * r}_0", align_bytes=64)
+                prods[i, r] = keep.tile([P, width], F32, name=f"kept{i}_{r}", tag=f"wg{2 * i + r}_0", align_bytes=64)
             else:
-                prods[i, r] = ring.tile([P, TH], F32, name=f"prod{r}")
+                prods[i, r] = keep.tile([P, width], F32, name=f"prod{r}", bufs=2)
             nc.vector.tensor_tensor(
-                prods[i, r][:], y[nt][:].indirect(pos_t[r][:, t0 // 16 : (t0 + TH) // 16]), gate_t[r][:, t0 : t0 + TH], MULT
+                prods[i, r][:], y[nt][:].indirect(pos_t[r][:, t0 // 16 : (t0 + width) // 16]), gate_t[r][:, t0 : t0 + width], MULT
             )
 
         def add_store(i):
-            nt, t0, TH = steps[i]
-            o = ring.tile([P, TH], F32, name="o")
+            nt, t0, width = STEPS[i]
+            o = keep.tile([P, width], F32, name="o", tag="planes", bufs=PB)
             nc.vector.tensor_tensor(o[:], prods[i, 0][:], prods[i, 1][:], ADD)
-            nc.sync.dma_start(out[nt * P : (nt + 1) * P, t0 : t0 + TH], o[:])
+            nc.sync.dma_start(out[nt * P : (nt + 1) * P, t0 : t0 + width], o[:])
 
-        for i in range(len(steps) + 1):
-            if i < len(steps):
+        for i in range(len(STEPS) + 1):
+            if i < len(STEPS):
                 weigh(i, 0)
             if i > ON_PE:
                 add_store(i - 1)
-            if i < len(steps):
+            if i < len(STEPS):
                 weigh(i, 1)
 
+        blocks = [(i, b0) for i in range(ON_PE) for b0 in range(0, STEPS[i][2], CH)]
         turned = {}
-
-        def add_turned(i):
-            nt, t0, TH = steps[i]
-            bank = psum.tile([P, TH], F32, name=f"bank{i % NCH}")
-            for b in range(0, TH, P):
+        for k, (i, b0) in enumerate(blocks):
+            bank = psum.tile([P, CH], F32, name=f"bank{k % NCH}")
+            for b in range(0, CH, P):
                 for r in range(2):
                     nc.tensor.matmul(
-                        bank[:, b : b + P], prods[i, r][:, b : b + P], ident[:], start=r == 0, stop=r == 1, is_transpose=True
+                        bank[:, b : b + P], prods[i, r][:, b0 + b : b0 + b + P], ident[:], start=r == 0, stop=r == 1, is_transpose=True
                     )
-            turned[i] = keep.tile([P, TH], F32, name=f"turned{i}", tag=f"late{WHOLE + i}")
-            nc.scalar.copy(turned[i][:], bank[:])
-
-        def turn_back(i):
-            nt, t0, TH = steps[i]
-            bank = psum.tile([P, TH], F32, name="back", bufs=3)
-            for b in range(0, TH, P):
-                nc.tensor.transpose(bank[:, b : b + P], turned[i][:, b : b + P], ident[:])
-            o = keep.tile([P, TH], F32, name=f"back{i}", tag=f"wg{WHOLE + i}_{HALF}", align_bytes=64)
+            turned[k] = keep.tile([P, CH], F32, name=f"turned{k}", tag=f"late{WHOLE + k}")
+            nc.scalar.copy(turned[k][:], bank[:])
+        for k, (i, b0) in enumerate(blocks):
+            nt, t0, width = STEPS[i]
+            bank = psum.tile([P, CH], F32, name="back", bufs=4)
+            for b in range(0, CH, P):
+                nc.tensor.transpose(bank[:, b : b + P], turned[k][:, b : b + P], ident[:])
+            o = keep.tile([P, CH], F32, name=f"back{k}", tag=f"wg{WHOLE + k}_{HALF}", align_bytes=64)
             nc.scalar.copy(o[:], bank[:])
-            nc.scalar.dma_start(out[nt * P : (nt + 1) * P, t0 : t0 + TH], o[:])
-
-        for i in range(ON_PE):
-            add_turned(i)
-        for i in range(ON_PE):
-            turn_back(i)
+            nc.scalar.dma_start(out[nt * P : (nt + 1) * P, t0 + b0 : t0 + b0 + CH], o[:])

@@ -19,207 +19,218 @@ ADD = mybir.AluOpType.add
 SILU = mybir.ActivationFunctionType.Silu
 
 P = 128
-CH = 512
-NCH = S // CH
+ROW_TILES = N // P
+PER_COLUMN = 16
+CHUNK = 512
+CHUNKS = S // CHUNK
 HALF = N // 2
-WHOLE = 4
-PB = 3
-FG = 512
-QW = 768
-TAIL = "e0 e1 e2 e3 e4 e5 e6 e7 s l4 g1 l5 p l6 l7 g0".split()
-PHASES = "y0 y1 z0 L z1 y2 y3 z2 z3".split()
-ZQ = "yyyy"
+
+WHOLE = 3
+GPSIMD_CHUNKS = 3
+EARLY_SCALE_CHUNKS = 2
 STEPS = [(0, 0, 1024), (1, 0, 512), (1, 512, 512), (2, 0, 1024), (3, 0, 512), (3, 512, 256), (3, 768, 256)]
-ON_PE = 2
+TENSOR_STEPS = 2
+
+
+def list_columns(list_tile, first, count):
+    return list_tile[:, first // PER_COLUMN : (first + count) // PER_COLUMN]
 
 
 def tile_moe_loc_lin_silu_kernel(tc, x_words, x_scales, xo, w, gate, offs, pos1, pos2, offs2, out):
     nc = tc.nc
     with ExitStack() as ctx:
-        keep = ctx.enter_context(tc.tile_pool(name="keep", bufs=1))
+        sbuf = ctx.enter_context(tc.tile_pool(name="sbuf", bufs=1))
         psum = ctx.enter_context(tc.psum_pool(name="psum", bufs=1))
 
-        offs2_t = keep.tile([P, S // 16], U16, name="offs2_t")
-        offs_t = keep.tile([P, S // 16], U16, name="offs_t")
-        pos_t = [keep.tile([P, T // 16], U16, name=f"pos_t{r}") for r in range(2)]
-        words = keep.tile([P, QW], I32, name="words")
-        sbytes = keep.tile([P, QW // 4], I32, name="sbytes")
-        xo_raw = [keep.tile([P, 2, T], F32, name=f"xo_raw{a}") for a in range(2)]
-        early = [(e, 0, N) for e in range(WHOLE)] + [(e, 0, HALF) for e in range(WHOLE, E)]
+        offs2_t = sbuf.tile([P, S // PER_COLUMN], U16, name="offs2_t")
+        offs_t = sbuf.tile([P, S // PER_COLUMN], U16, name="offs_t")
+        pos_t = [sbuf.tile([P, T // PER_COLUMN], U16, name=f"pos_t{r}") for r in range(2)]
+        gate_t = [sbuf.tile([P, T], F32, name=f"gate_t{r}") for r in range(2)]
+        token_words = sbuf.tile([P, Q], I32, name="token_words")
+        token_scales = sbuf.tile([P, Q // 4], I32, name="token_scales")
+        xo_raw = [sbuf.tile([P, 2, T], F32, name=f"xo_raw{a}", align_bytes=64) for a in range(2)]
+
+        warm = sbuf.tile([P, 16], F32, name="warm")
+        nc.vector.memset(warm[:, 0:8], 0.0)
+        nc.scalar.activation(warm[:, 8:16], warm[:, 0:8], SILU)
+        nc.vector.memset(token_scales[:], 0)
+
+        early = [(e, 0, N if e < WHOLE else HALF) for e in range(E)]
         late = [(e, HALF, HALF) for e in range(WHOLE, E)]
         w_raw = {}
 
         def load_w(piece):
             e, n0, width = piece
-            w_raw[piece] = keep.tile([P, 4, width], F32, name=f"w_raw{e}_{n0}", tag=f"big{e}" if n0 == 0 else f"late{e}")
+            tag = f"early{e}" if n0 == 0 else f"late{e}"
+            w_raw[piece] = sbuf.tile([P, 4, width], F32, name=f"w_raw{e}_{n0}", tag=tag)
             nc.sync.dma_start(w_raw[piece][:], w[e].rearrange("(p j) n -> p j n", j=4)[:, :, n0 : n0 + width])
 
-        gate_t = [keep.tile([P, T], F32, name=f"gate_t{r}") for r in range(2)]
-
-        warm = keep.tile([P, 16], F32, name="warm")
-        nc.vector.memset(warm[:, 0:8], 0.0)
-        nc.scalar.activation(warm[:, 8:16], warm[:, 0:8], SILU)
-        nc.vector.memset(sbytes[:], 0)
-        if QW > Q:
-            nc.vector.memset(words[:, Q:], 0)
+        xo_rows = xo.rearrange("(p j) t -> p j t", j=4)
         nc.sync.dma_start(offs2_t[:], offs2)
-        nc.sync.dma_start(words[:, :Q], x_words[0].rearrange("p t d -> p (t d)").bitcast(I32))
-        xo_v = xo.rearrange("(p j) t -> p j t", j=4)
-        nc.sync.dma_start(xo_raw[0][:], xo_v[:, 0:2, :])
+        nc.sync.dma_start(token_words[:], x_words[0].rearrange("p t d -> p (t d)").bitcast(I32))
+        nc.sync.dma_start(xo_raw[0][:], xo_rows[:, 0:2, :])
         nc.sync.dma_start(offs_t[:], offs)
-        nc.sync.dma_start(xo_raw[1][:], xo_v[:, 2:4, :])
-        for item in TAIL:
-            if item == "s":
-                for q in range(4):
-                    nc.sync.dma_start(sbytes[32 * q : 32 * q + 4, : Q // 4], x_scales[0, 4 * q : 4 * q + 4, :].bitcast(I32))
-            elif item == "p":
-                nc.sync.dma_start(pos_t[0][:], pos1)
-                nc.sync.dma_start(pos_t[1][:], pos2)
-            elif item[0] == "g":
-                nc.sync.dma_start(gate_t[int(item[1])][:], gate[int(item[1])])
-            elif item[0] == "e":
-                load_w(early[int(item[1])])
-            else:
-                load_w(late[int(item[1]) - WHOLE])
+        nc.sync.dma_start(xo_raw[1][:], xo_rows[:, 2:4, :])
+        for q in range(4):
+            nc.sync.dma_start(token_scales[32 * q : 32 * q + 4, :], x_scales[0, 4 * q : 4 * q + 4, :].bitcast(I32))
+        for piece in early + late[:1]:
+            load_w(piece)
+        nc.sync.dma_start(gate_t[1][:], gate[1])
+        nc.sync.dma_start(pos_t[0][:], pos1)
+        nc.sync.dma_start(pos_t[1][:], pos2)
+        for piece in late[1:]:
+            load_w(piece)
+        nc.sync.dma_start(gate_t[0][:], gate[0])
 
-        pairs = [keep.tile([P, 2 * T], BF16, name=f"pairs{a}") for a in range(2)]
+        pairs = [sbuf.tile([P, 2 * T], BF16, name=f"pairs{a}") for a in range(2)]
         for a in range(2):
-            nc.scalar.copy(pairs[a][:].rearrange("p (t e) -> p t e", e=2), xo_raw[a][:].rearrange("p e t -> p t e"))
+            nc.scalar.copy(pairs[a][:].rearrange("p (t i) -> p t i", i=2), xo_raw[a][:].rearrange("p i t -> p t i"))
 
-        own_codes = keep.tile([P, S], U32, name="own_codes", align_bytes=64)
-        own_scales = keep.tile([P, S], U8, name="own_scales", align_bytes=64)
-        far_codes = keep.tile([P, S], U32, name="far_codes", align_bytes=64)
-        far_scales = keep.tile([P, S], U8, name="far_scales", align_bytes=64)
-        planes = {}
-        grouped = {}
+        own_codes = sbuf.tile([P, S], U32, name="own_codes", align_bytes=64)
+        own_scales = [sbuf.tile([P, CHUNK], U8, name=f"own_scales{c}", align_bytes=64)[:] for c in range(CHUNKS)]
+        far_codes = sbuf.tile([P, S], U32, name="far_codes", align_bytes=64)
+        far_scales = {}
+        w_codes = [sbuf.tile([P, N], U32, name=f"w_codes{e}", align_bytes=64) for e in range(E)]
+        w_scales = [sbuf.tile([P, N], U8, name=f"w_scales{e}", align_bytes=64) for e in range(E)]
 
-        def gather_own(c, a):
-            if a == 0:
-                planes[c] = keep.tile([P, 2, 2 * CH], BF16, name="planes", bufs=PB)
-            cols = offs_t[:, c * CH // 16 : (c + 1) * CH // 16]
-            nc.vector.tensor_copy(planes[c][:, a, :].bitcast(U32), pairs[a][:].bitcast(U32).indirect(cols))
-
-        def interleave_own(c):
-            grouped[c] = keep.tile([P, 4 * CH], BF16, name="grouped", align_bytes=64, bufs=2)
+        for c in range(CHUNKS):
             nc.vector.tensor_copy(
-                grouped[c][:].bitcast(I32).rearrange("p (s a) -> p s a", a=2),
-                planes[c][:].bitcast(I32).rearrange("p a s -> p s a"),
+                far_codes[:, c * CHUNK : (c + 1) * CHUNK],
+                token_words[:].bitcast(U32).indirect(list_columns(offs2_t, c * CHUNK, CHUNK)),
             )
 
-        def quantize_own(c):
-            cols = slice(c * CH, (c + 1) * CH)
-            nc.vector.quantize_mx(out=own_codes[:, cols].bitcast(FP8X4), scales=own_scales[:, cols], in_=grouped[c][:])
+        def gather_far_scales(chunks, tag):
+            gathered = sbuf.tile([P, len(chunks) * CHUNK], U8, name=f"far_scales{chunks[0]}", tag=tag, align_bytes=64)
+            for place, c in enumerate(chunks):
+                far_scales[c] = gathered[:, place * CHUNK : (place + 1) * CHUNK]
+                nc.vector.tensor_copy(
+                    far_scales[c], token_scales[:].bitcast(U8).indirect(list_columns(offs2_t, c * CHUNK, CHUNK))
+                )
 
-        w_codes = [keep.tile([P, N], U32, name=f"w_codes{e}", align_bytes=64) for e in range(E)]
-        w_scales = [keep.tile([P, N], U8, name=f"w_scales{e}", align_bytes=64) for e in range(E)]
+        grouped = []
+        for c in range(CHUNKS):
+            picked = sbuf.tile([P, 2, 2 * CHUNK], BF16, name="picked", bufs=3)
+            for a in range(2):
+                nc.vector.tensor_copy(
+                    picked[:, a, :].bitcast(U32), pairs[a][:].bitcast(U32).indirect(list_columns(offs_t, c * CHUNK, CHUNK))
+                )
+            grouped.append(sbuf.tile([P, 4 * CHUNK], BF16, name="grouped", align_bytes=64, bufs=3))
+            engine = nc.gpsimd if c < GPSIMD_CHUNKS else nc.vector
+            engine.tensor_copy(
+                grouped[c][:].bitcast(I32).rearrange("p (s a) -> p s a", a=2),
+                picked[:].bitcast(I32).rearrange("p a s -> p s a"),
+            )
 
         def quantize_w(piece):
             e, n0, width = piece
-            wg = keep.tile([P, 4 * width], BF16, name=f"wg{e}_{n0}", align_bytes=64)
+            w_grouped = sbuf.tile([P, 4 * width], BF16, name=f"w_grouped{e}_{n0}", align_bytes=64)
             nc.scalar.copy(
-                wg[:].rearrange("p (c i j) -> p c j i", i=4, j=4),
-                w_raw[piece][:].rearrange("p j (c i) -> p c j i", i=4),
+                w_grouped[:].rearrange("p (g i j) -> p g j i", i=4, j=4),
+                w_raw[piece][:].rearrange("p j (g i) -> p g j i", i=4),
             )
             cols = slice(n0, n0 + width)
-            nc.vector.quantize_mx(out=w_codes[e][:, cols].bitcast(FP8X4), scales=w_scales[e][:, cols], in_=wg[:])
+            nc.vector.quantize_mx(out=w_codes[e][:, cols].bitcast(FP8X4), scales=w_scales[e][:, cols], in_=w_grouped[:])
+
+        gather_far_scales(range(EARLY_SCALE_CHUNKS), "xo_raw1")
+        for c in range(CHUNKS):
+            nc.vector.quantize_mx(
+                out=own_codes[:, c * CHUNK : (c + 1) * CHUNK].bitcast(FP8X4), scales=own_scales[c], in_=grouped[c][:]
+            )
+            quantize_w(early[2 * c])
+            quantize_w(early[2 * c + 1])
+        gather_far_scales(range(EARLY_SCALE_CHUNKS, CHUNKS), f"w_grouped{E - 1}_0")
 
         def experts(c, nt, codes, scales, dest):
-            bank = psum.tile([P, CH], F32, name=f"bank{c}")
-            m0 = nt * P
+            bank = psum.tile([P, CHUNK], F32, name=f"bank{c}")
+            rows = slice(nt * P, (nt + 1) * P)
             for u in range(2):
                 e = 2 * c + u
                 nc.tensor.matmul_mx(
                     out=bank[:, u * C : (u + 1) * C],
-                    lhsT=w_codes[e][:, m0 : m0 + P].bitcast(FP8X4),
-                    lhsT_scale=w_scales[e][:, m0 : m0 + P],
+                    lhsT=w_codes[e][:, rows].bitcast(FP8X4),
+                    lhsT_scale=w_scales[e][:, rows],
                     rhs=codes[:, e * C : (e + 1) * C].bitcast(FP8X4),
-                    rhs_scale=scales[:, e * C : (e + 1) * C],
+                    rhs_scale=scales[c][:, u * C : (u + 1) * C],
                     start=True,
                     stop=True,
                 )
             nc.scalar.activation(dest, bank[:], SILU)
 
-        for s0 in range(0, S, FG):
-            nc.vector.tensor_copy(far_codes[:, s0 : s0 + FG], words[:].bitcast(U32).indirect(offs2_t[:, s0 // 16 : (s0 + FG) // 16]))
-
-        gather_own(0, 0)
-        gather_own(0, 1)
-        for c in range(NCH):
-            interleave_own(c)
-            quantize_w(early[2 * c])
-            quantize_own(c)
-            quantize_w(early[2 * c + 1])
-            if c + 1 < NCH:
-                gather_own(c + 1, 0)
-                gather_own(c + 1, 1)
-
-        for s0 in range(0, S, FG):
-            nc.vector.tensor_copy(far_scales[:, s0 : s0 + FG], sbytes[:].bitcast(U8).indirect(offs2_t[:, s0 // 16 : (s0 + FG) // 16]))
-
-        queues = {"g": nc.gpsimd, "s": nc.scalar, "y": nc.sync}
         y = {}
-        for item in PHASES:
-            if item == "L":
-                for piece in late:
-                    quantize_w(piece)
-                continue
-            nt = int(item[1])
-            if item[0] == "y":
-                y[nt] = keep.tile([P, S], F32, name=f"y{nt}", tag=f"big{E - 1 - nt}")
-                for c in range(NCH):
-                    experts(c, nt, own_codes, own_scales, y[nt][:, c * CH : (c + 1) * CH])
-            else:
-                z = keep.tile([P, S], F32, name=f"z{nt}", tag=f"big{nt}")
-                for c in range(NCH):
-                    experts(c, nt, far_codes, far_scales, z[:, c * CH : (c + 1) * CH])
-                    if c % 2:
-                        cols = slice((c - 1) * CH, (c + 1) * CH)
-                        queues[ZQ[nt]].dma_start(out[nt * P : (nt + 1) * P, T + cols.start : T + cols.stop], z[:, cols])
 
-        ident = keep.tile([P, P], F32, name="ident")
-        make_identity(nc, ident[:])
-        prods = {}
+        def own_tile(nt):
+            y[nt] = sbuf.tile([P, S], F32, name=f"y{nt}", tag=f"early{E - 1 - nt}")
+            for c in range(CHUNKS):
+                experts(c, nt, own_codes, own_scales, y[nt][:, c * CHUNK : (c + 1) * CHUNK])
 
-        def weigh(i, r):
-            nt, t0, width = STEPS[i]
-            if i < ON_PE:
-                prods[i, r] = keep.tile([P, width], F32, name=f"kept{i}_{r}", tag=f"wg{2 * i + r}_0", align_bytes=64)
+        def far_tile(nt):
+            z = sbuf.tile([P, S], F32, name=f"z{nt}", tag=f"early{nt}")
+            for s0 in range(0, S, 2 * CHUNK):
+                for c in (s0 // CHUNK, s0 // CHUNK + 1):
+                    experts(c, nt, far_codes, far_scales, z[:, c * CHUNK : (c + 1) * CHUNK])
+                nc.sync.dma_start(out[nt * P : (nt + 1) * P, T + s0 : T + s0 + 2 * CHUNK], z[:, s0 : s0 + 2 * CHUNK])
+
+        own_tile(0)
+        own_tile(1)
+        far_tile(0)
+        for piece in late:
+            quantize_w(piece)
+        far_tile(1)
+        for nt in range(2, ROW_TILES):
+            own_tile(nt)
+        for nt in range(2, ROW_TILES):
+            far_tile(nt)
+
+        identity = sbuf.tile([P, P], F32, name="identity")
+        make_identity(nc, identity[:])
+        products = {}
+
+        def weigh(step, r):
+            nt, t0, width = STEPS[step]
+            if step < TENSOR_STEPS:
+                tag = f"w_grouped{2 * step + r}_0"
+                products[step, r] = sbuf.tile([P, width], F32, name=f"kept{step}_{r}", tag=tag, align_bytes=64)
             else:
-                prods[i, r] = keep.tile([P, width], F32, name=f"prod{r}", bufs=2)
+                products[step, r] = sbuf.tile([P, width], F32, name=f"product{r}", bufs=2)
             nc.vector.tensor_tensor(
-                prods[i, r][:], y[nt][:].indirect(pos_t[r][:, t0 // 16 : (t0 + width) // 16]), gate_t[r][:, t0 : t0 + width], MULT
+                products[step, r][:], y[nt][:].indirect(list_columns(pos_t[r], t0, width)), gate_t[r][:, t0 : t0 + width], MULT
             )
 
-        def add_store(i):
-            nt, t0, width = STEPS[i]
-            o = keep.tile([P, width], F32, name="o", tag="planes", bufs=PB)
-            nc.vector.tensor_tensor(o[:], prods[i, 0][:], prods[i, 1][:], ADD)
-            nc.sync.dma_start(out[nt * P : (nt + 1) * P, t0 : t0 + width], o[:])
+        def add_and_store(step):
+            nt, t0, width = STEPS[step]
+            total = sbuf.tile([P, width], F32, name="total", tag="picked", bufs=3)
+            nc.vector.tensor_tensor(total[:], products[step, 0][:], products[step, 1][:], ADD)
+            nc.sync.dma_start(out[nt * P : (nt + 1) * P, t0 : t0 + width], total[:])
 
-        for i in range(len(STEPS) + 1):
-            if i < len(STEPS):
-                weigh(i, 0)
-            if i > ON_PE:
-                add_store(i - 1)
-            if i < len(STEPS):
-                weigh(i, 1)
+        for step in range(len(STEPS)):
+            weigh(step, 0)
+            if step > TENSOR_STEPS:
+                add_and_store(step - 1)
+            weigh(step, 1)
+        add_and_store(len(STEPS) - 1)
 
-        blocks = [(i, b0) for i in range(ON_PE) for b0 in range(0, STEPS[i][2], CH)]
-        turned = {}
-        for k, (i, b0) in enumerate(blocks):
-            bank = psum.tile([P, CH], F32, name=f"bank{k % NCH}")
-            for b in range(0, CH, P):
+        spans = [(step, b0) for step in range(TENSOR_STEPS) for b0 in range(0, STEPS[step][2], CHUNK)]
+        turned = []
+        for index, (step, b0) in enumerate(spans):
+            bank = psum.tile([P, CHUNK], F32, name=f"bank{index}")
+            for b in range(0, CHUNK, P):
                 for r in range(2):
                     nc.tensor.matmul(
-                        bank[:, b : b + P], prods[i, r][:, b0 + b : b0 + b + P], ident[:], start=r == 0, stop=r == 1, is_transpose=True
+                        bank[:, b : b + P],
+                        products[step, r][:, b0 + b : b0 + b + P],
+                        identity[:],
+                        start=r == 0,
+                        stop=r == 1,
+                        is_transpose=True,
                     )
-            turned[k] = keep.tile([P, CH], F32, name=f"turned{k}", tag=f"late{WHOLE + k}")
-            nc.scalar.copy(turned[k][:], bank[:])
-        for k, (i, b0) in enumerate(blocks):
-            nt, t0, width = STEPS[i]
-            bank = psum.tile([P, CH], F32, name="back", bufs=4)
-            for b in range(0, CH, P):
-                nc.tensor.transpose(bank[:, b : b + P], turned[k][:, b : b + P], ident[:])
-            o = keep.tile([P, CH], F32, name=f"back{k}", tag=f"wg{WHOLE + k}_{HALF}", align_bytes=64)
-            nc.scalar.copy(o[:], bank[:])
-            nc.scalar.dma_start(out[nt * P : (nt + 1) * P, t0 + b0 : t0 + b0 + CH], o[:])
+            turned.append(sbuf.tile([P, CHUNK], F32, name=f"turned{index}", tag=f"late{WHOLE + index}"))
+            nc.scalar.copy(turned[index][:], bank[:])
+        for index, (step, b0) in enumerate(spans):
+            nt, t0, width = STEPS[step]
+            bank = psum.tile([P, CHUNK], F32, name="back_bank", bufs=4)
+            for b in range(0, CHUNK, P):
+                nc.tensor.transpose(bank[:, b : b + P], turned[index][:, b : b + P], identity[:])
+            tag = f"w_grouped{WHOLE + index}_{HALF}"
+            summed = sbuf.tile([P, CHUNK], F32, name=f"summed{index}", tag=tag, align_bytes=64)
+            nc.scalar.copy(summed[:], bank[:])
+            nc.scalar.dma_start(out[nt * P : (nt + 1) * P, t0 + b0 : t0 + b0 + CHUNK], summed[:])

@@ -25,11 +25,9 @@ CHUNK = 512
 CHUNKS = S // CHUNK
 HALF = N // 2
 
-WHOLE = 3
-GPSIMD_CHUNKS = 3
-EARLY_SCALE_CHUNKS = 2
-STEPS = [(0, 0, 1024), (1, 0, 512), (1, 512, 512), (2, 0, 1024), (3, 0, 512), (3, 512, 256), (3, 768, 256)]
-TENSOR_STEPS = 2
+WHOLE = 7
+STEPS = [(0, 0, 1024), (1, 0, 1024), (2, 0, 512), (2, 512, 512), (3, 0, 512), (3, 512, 256), (3, 768, 256)]
+TENSOR_STEPS = 3
 
 
 def list_columns(list_tile, first, count):
@@ -48,50 +46,49 @@ def tile_moe_loc_lin_silu_kernel(tc, x_words, x_scales, xo, w, gate, offs, pos1,
         gate_t = [sbuf.tile([P, T], F32, name=f"gate_t{r}") for r in range(2)]
         token_words = sbuf.tile([P, Q], I32, name="token_words")
         token_scales = sbuf.tile([P, Q // 4], I32, name="token_scales")
-        xo_raw = [sbuf.tile([P, 2, T], F32, name=f"xo_raw{a}", align_bytes=64) for a in range(2)]
+        xo_raw = {
+            (a, h): sbuf.tile([P, 2, T // 2], F32, name=f"xo_raw{a}{h}", align_bytes=64) for a in range(2) for h in range(2)
+        }
 
         warm = sbuf.tile([P, 16], F32, name="warm")
         nc.vector.memset(warm[:, 0:8], 0.0)
         nc.scalar.activation(warm[:, 8:16], warm[:, 0:8], SILU)
         nc.vector.memset(token_scales[:], 0)
 
-        early = [(e, 0, N if e < WHOLE else HALF) for e in range(E)]
-        late = [(e, HALF, HALF) for e in range(WHOLE, E)]
+        pieces = [(e, 0, N) for e in range(WHOLE)] + [(e, n0, HALF) for n0 in (0, HALF) for e in range(WHOLE, E)]
         w_raw = {}
 
-        def load_w(piece):
-            e, n0, width = piece
-            tag = f"early{e}" if n0 == 0 else f"late{e}"
-            w_raw[piece] = sbuf.tile([P, 4, width], F32, name=f"w_raw{e}_{n0}", tag=tag)
-            nc.sync.dma_start(w_raw[piece][:], w[e].rearrange("(p j) n -> p j n", j=4)[:, :, n0 : n0 + width])
-
         xo_rows = xo.rearrange("(p j) t -> p j t", j=4)
+
+        def load_xo(a):
+            for h in range(2):
+                nc.sync.dma_start(xo_raw[a, h][:], xo_rows[:, 2 * a : 2 * a + 2, h * T // 2 : (h + 1) * T // 2])
+
         nc.sync.dma_start(offs2_t[:], offs2)
         nc.sync.dma_start(token_words[:], x_words[0].rearrange("p t d -> p (t d)").bitcast(I32))
-        nc.sync.dma_start(xo_raw[0][:], xo_rows[:, 0:2, :])
+        load_xo(0)
         nc.sync.dma_start(offs_t[:], offs)
-        nc.sync.dma_start(xo_raw[1][:], xo_rows[:, 2:4, :])
+        load_xo(1)
         for q in range(4):
             nc.sync.dma_start(token_scales[32 * q : 32 * q + 4, :], x_scales[0, 4 * q : 4 * q + 4, :].bitcast(I32))
-        for piece in early + late[:1]:
-            load_w(piece)
-        nc.sync.dma_start(gate_t[1][:], gate[1])
-        nc.sync.dma_start(pos_t[0][:], pos1)
-        nc.sync.dma_start(pos_t[1][:], pos2)
-        for piece in late[1:]:
-            load_w(piece)
-        nc.sync.dma_start(gate_t[0][:], gate[0])
+        for e, n0, width in pieces:
+            w_raw[e, n0] = sbuf.tile([P, 4, width], F32, name=f"w_raw{e}_{n0}", align_bytes=64)
+            nc.sync.dma_start(w_raw[e, n0][:], w[e].rearrange("(p j) n -> p j n", j=4)[:, :, n0 : n0 + width])
+        for r, pos in enumerate((pos1, pos2)):
+            nc.sync.dma_start(pos_t[r][:], pos)
+            nc.sync.dma_start(gate_t[r][:], gate[r])
 
         pairs = [sbuf.tile([P, 2 * T], BF16, name=f"pairs{a}") for a in range(2)]
         for a in range(2):
-            nc.scalar.copy(pairs[a][:].rearrange("p (t i) -> p t i", i=2), xo_raw[a][:].rearrange("p i t -> p t i"))
+            for h in range(2):
+                nc.scalar.copy(
+                    pairs[a][:, h * T : (h + 1) * T].rearrange("p (t i) -> p t i", i=2),
+                    xo_raw[a, h][:].rearrange("p i t -> p t i"),
+                )
 
         own_codes = sbuf.tile([P, S], U32, name="own_codes", align_bytes=64)
-        own_scales = [sbuf.tile([P, CHUNK], U8, name=f"own_scales{c}", align_bytes=64)[:] for c in range(CHUNKS)]
+        own_scales = sbuf.tile([P, S], U8, name="own_scales", align_bytes=64)
         far_codes = sbuf.tile([P, S], U32, name="far_codes", align_bytes=64)
-        far_scales = {}
-        w_codes = [sbuf.tile([P, N], U32, name=f"w_codes{e}", align_bytes=64) for e in range(E)]
-        w_scales = [sbuf.tile([P, N], U8, name=f"w_scales{e}", align_bytes=64) for e in range(E)]
 
         for c in range(CHUNKS):
             nc.vector.tensor_copy(
@@ -99,58 +96,71 @@ def tile_moe_loc_lin_silu_kernel(tc, x_words, x_scales, xo, w, gate, offs, pos1,
                 token_words[:].bitcast(U32).indirect(list_columns(offs2_t, c * CHUNK, CHUNK)),
             )
 
-        def gather_far_scales(chunks, tag):
-            gathered = sbuf.tile([P, len(chunks) * CHUNK], U8, name=f"far_scales{chunks[0]}", tag=tag, align_bytes=64)
-            for place, c in enumerate(chunks):
-                far_scales[c] = gathered[:, place * CHUNK : (place + 1) * CHUNK]
-                nc.vector.tensor_copy(
-                    far_scales[c], token_scales[:].bitcast(U8).indirect(list_columns(offs2_t, c * CHUNK, CHUNK))
-                )
-
         grouped = []
         for c in range(CHUNKS):
-            picked = sbuf.tile([P, 2, 2 * CHUNK], BF16, name="picked", bufs=3)
+            picked = sbuf.tile([P, 2, 2 * CHUNK], BF16, name="picked", bufs=CHUNKS)
             for a in range(2):
                 nc.vector.tensor_copy(
                     picked[:, a, :].bitcast(U32), pairs[a][:].bitcast(U32).indirect(list_columns(offs_t, c * CHUNK, CHUNK))
                 )
-            grouped.append(sbuf.tile([P, 4 * CHUNK], BF16, name="grouped", align_bytes=64, bufs=3))
-            engine = nc.gpsimd if c < GPSIMD_CHUNKS else nc.vector
-            engine.tensor_copy(
+            grouped.append(sbuf.tile([P, 4 * CHUNK], BF16, name="grouped", align_bytes=64, bufs=CHUNKS))
+            nc.gpsimd.tensor_copy(
                 grouped[c][:].bitcast(I32).rearrange("p (s a) -> p s a", a=2),
                 picked[:].bitcast(I32).rearrange("p a s -> p s a"),
             )
 
-        def quantize_w(piece):
-            e, n0, width = piece
-            w_grouped = sbuf.tile([P, 4 * width], BF16, name=f"w_grouped{e}_{n0}", align_bytes=64)
-            nc.scalar.copy(
-                w_grouped[:].rearrange("p (g i j) -> p g j i", i=4, j=4),
-                w_raw[piece][:].rearrange("p j (g i) -> p g j i", i=4),
-            )
-            cols = slice(n0, n0 + width)
-            nc.vector.quantize_mx(out=w_codes[e][:, cols].bitcast(FP8X4), scales=w_scales[e][:, cols], in_=w_grouped[:])
-
-        gather_far_scales(range(EARLY_SCALE_CHUNKS), "xo_raw1")
+        far_scales = sbuf.tile([P, S], U8, name="far_scales", tag="xo_raw11", align_bytes=64)
         for c in range(CHUNKS):
-            nc.vector.quantize_mx(
-                out=own_codes[:, c * CHUNK : (c + 1) * CHUNK].bitcast(FP8X4), scales=own_scales[c], in_=grouped[c][:]
+            nc.vector.tensor_copy(
+                far_scales[:, c * CHUNK : (c + 1) * CHUNK],
+                token_scales[:].bitcast(U8).indirect(list_columns(offs2_t, c * CHUNK, CHUNK)),
             )
-            quantize_w(early[2 * c])
-            quantize_w(early[2 * c + 1])
-        gather_far_scales(range(EARLY_SCALE_CHUNKS, CHUNKS), f"w_grouped{E - 1}_0")
 
-        def experts(c, nt, codes, scales, dest):
-            bank = psum.tile([P, CHUNK], F32, name=f"bank{c}")
-            rows = slice(nt * P, (nt + 1) * P)
+        w_grouped = {}
+
+        def round_w(piece):
+            e, n0, width = piece
+            rounded = sbuf.tile([P, 4 * width], BF16, name=f"w_grouped{e}_{n0}", align_bytes=64)
+            nc.scalar.copy(
+                rounded[:].rearrange("p (g i j) -> p g j i", i=4, j=4),
+                w_raw[e, n0][:].rearrange("p j (g i) -> p g j i", i=4),
+            )
+            for m0 in range(0, width, HALF):
+                w_grouped[e, (n0 + m0) // HALF] = rounded[:, 4 * m0 : 4 * (m0 + HALF)]
+
+        for piece in pieces[:-1]:
+            round_w(piece)
+
+        w_codes = [sbuf.tile([P, E * HALF], U32, name=f"w_codes{half}", align_bytes=64) for half in range(2)]
+        w_scales = [sbuf.tile([P, E * HALF], U8, name="w_scales0", align_bytes=64)]
+
+        def quantize_w(e, half):
+            cols = slice(e * HALF, (e + 1) * HALF)
+            nc.vector.quantize_mx(
+                out=w_codes[half][:, cols].bitcast(FP8X4), scales=w_scales[half][:, cols], in_=w_grouped[e, half]
+            )
+
+        for c in range(CHUNKS):
+            slots = slice(c * CHUNK, (c + 1) * CHUNK)
+            nc.vector.quantize_mx(out=own_codes[:, slots].bitcast(FP8X4), scales=own_scales[:, slots], in_=grouped[c][:])
+            quantize_w(2 * c, 0)
+            quantize_w(2 * c + 1, 0)
+        w_scales.append(sbuf.tile([P, E * HALF], U8, name="w_scales1", tag=f"w_grouped{E - 1}_0", align_bytes=64))
+        for e in range(E - 1):
+            quantize_w(e, 1)
+
+        def experts(c, nt, codes, scales, dest, bank_index):
+            bank = psum.tile([P, CHUNK], F32, name=f"bank{bank_index}")
+            half, row0 = divmod(nt * P, HALF)
             for u in range(2):
                 e = 2 * c + u
+                rows = slice(e * HALF + row0, e * HALF + row0 + P)
                 nc.tensor.matmul_mx(
                     out=bank[:, u * C : (u + 1) * C],
-                    lhsT=w_codes[e][:, rows].bitcast(FP8X4),
-                    lhsT_scale=w_scales[e][:, rows],
+                    lhsT=w_codes[half][:, rows].bitcast(FP8X4),
+                    lhsT_scale=w_scales[half][:, rows],
                     rhs=codes[:, e * C : (e + 1) * C].bitcast(FP8X4),
-                    rhs_scale=scales[c][:, u * C : (u + 1) * C],
+                    rhs_scale=scales[:, e * C : (e + 1) * C],
                     start=True,
                     stop=True,
                 )
@@ -158,28 +168,29 @@ def tile_moe_loc_lin_silu_kernel(tc, x_words, x_scales, xo, w, gate, offs, pos1,
 
         y = {}
 
-        def own_tile(nt):
-            y[nt] = sbuf.tile([P, S], F32, name=f"y{nt}", tag=f"early{E - 1 - nt}")
+        def own_tile(nt, tag, bank0):
+            y[nt] = sbuf.tile([P, S], F32, name=f"y{nt}", tag=tag, align_bytes=64)
             for c in range(CHUNKS):
-                experts(c, nt, own_codes, own_scales, y[nt][:, c * CHUNK : (c + 1) * CHUNK])
+                experts(c, nt, own_codes, own_scales, y[nt][:, c * CHUNK : (c + 1) * CHUNK], bank0 + c)
 
-        def far_tile(nt):
-            z = sbuf.tile([P, S], F32, name=f"z{nt}", tag=f"early{nt}")
+        def far_tile(nt, bank0):
+            z = sbuf.tile([P, S], F32, name=f"z{nt}", tag=f"w_raw{nt}_0", align_bytes=64)
             for s0 in range(0, S, 2 * CHUNK):
                 for c in (s0 // CHUNK, s0 // CHUNK + 1):
-                    experts(c, nt, far_codes, far_scales, z[:, c * CHUNK : (c + 1) * CHUNK])
-                nc.sync.dma_start(out[nt * P : (nt + 1) * P, T + s0 : T + s0 + 2 * CHUNK], z[:, s0 : s0 + 2 * CHUNK])
+                    experts(c, nt, far_codes, far_scales, z[:, c * CHUNK : (c + 1) * CHUNK], bank0 + c)
+                queue = nc.scalar if nt == ROW_TILES - 1 else nc.sync
+                queue.dma_start(out[nt * P : (nt + 1) * P, T + s0 : T + s0 + 2 * CHUNK], z[:, s0 : s0 + 2 * CHUNK])
 
-        own_tile(0)
-        own_tile(1)
-        far_tile(0)
-        for piece in late:
-            quantize_w(piece)
-        far_tile(1)
-        for nt in range(2, ROW_TILES):
-            own_tile(nt)
-        for nt in range(2, ROW_TILES):
-            far_tile(nt)
+        own_tile(0, f"w_raw{E - 1}_0", 0)
+        round_w(pieces[-1])
+        quantize_w(E - 1, 1)
+        own_tile(1, f"w_raw{E - 1}_{HALF}", CHUNKS)
+        far_tile(0, 0)
+        far_tile(1, CHUNKS)
+        own_tile(2, "w_raw4_0", 0)
+        far_tile(2, CHUNKS)
+        own_tile(3, "w_raw5_0", 0)
+        far_tile(3, CHUNKS)
 
         identity = sbuf.tile([P, P], F32, name="identity")
         make_identity(nc, identity[:])
@@ -198,7 +209,10 @@ def tile_moe_loc_lin_silu_kernel(tc, x_words, x_scales, xo, w, gate, offs, pos1,
 
         def add_and_store(step):
             nt, t0, width = STEPS[step]
-            total = sbuf.tile([P, width], F32, name="total", tag="picked", bufs=3)
+            if nt < ROW_TILES - 1:
+                total = sbuf.tile([P, width], F32, name=f"total{step}", tag=f"w_raw{nt}_0", align_bytes=64)
+            else:
+                total = sbuf.tile([P, width], F32, name="total", tag="picked", bufs=CHUNKS)
             nc.vector.tensor_tensor(total[:], products[step, 0][:], products[step, 1][:], ADD)
             nc.sync.dma_start(out[nt * P : (nt + 1) * P, t0 : t0 + width], total[:])
 
@@ -210,9 +224,11 @@ def tile_moe_loc_lin_silu_kernel(tc, x_words, x_scales, xo, w, gate, offs, pos1,
         add_and_store(len(STEPS) - 1)
 
         spans = [(step, b0) for step in range(TENSOR_STEPS) for b0 in range(0, STEPS[step][2], CHUNK)]
-        turned = []
-        for index, (step, b0) in enumerate(spans):
-            bank = psum.tile([P, CHUNK], F32, name=f"bank{index}")
+        turned = {}
+
+        def turn(index):
+            step, b0 = spans[index]
+            bank = psum.tile([P, CHUNK], F32, name=f"bank{index % CHUNKS}")
             for b in range(0, CHUNK, P):
                 for r in range(2):
                     nc.tensor.matmul(
@@ -223,14 +239,22 @@ def tile_moe_loc_lin_silu_kernel(tc, x_words, x_scales, xo, w, gate, offs, pos1,
                         stop=r == 1,
                         is_transpose=True,
                     )
-            turned.append(sbuf.tile([P, CHUNK], F32, name=f"turned{index}", tag=f"late{WHOLE + index}"))
+            turned[index] = sbuf.tile([P, CHUNK], F32, name="turned", tag="grouped", align_bytes=64, bufs=CHUNKS)
             nc.scalar.copy(turned[index][:], bank[:])
-        for index, (step, b0) in enumerate(spans):
+
+        def turn_back(index):
+            step, b0 = spans[index]
             nt, t0, width = STEPS[step]
-            bank = psum.tile([P, CHUNK], F32, name="back_bank", bufs=4)
+            bank = psum.tile([P, CHUNK], F32, name=f"bank{CHUNKS + index % CHUNKS}")
             for b in range(0, CHUNK, P):
                 nc.tensor.transpose(bank[:, b : b + P], turned[index][:, b : b + P], identity[:])
-            tag = f"w_grouped{WHOLE + index}_{HALF}"
-            summed = sbuf.tile([P, CHUNK], F32, name=f"summed{index}", tag=tag, align_bytes=64)
+            summed = sbuf.tile([P, CHUNK], F32, name=f"summed{index}")
             nc.scalar.copy(summed[:], bank[:])
             nc.scalar.dma_start(out[nt * P : (nt + 1) * P, t0 + b0 : t0 + b0 + CHUNK], summed[:])
+
+        LAG = 2
+        for index in range(len(spans) + LAG):
+            if index < len(spans):
+                turn(index)
+            if index >= LAG:
+                turn_back(index - LAG)

@@ -25,9 +25,11 @@ CHUNK = 512
 CHUNKS = S // CHUNK
 HALF = N // 2
 
-WHOLE = 7
-STEPS = [(0, 0, 1024), (1, 0, 1024), (2, 0, 512), (2, 512, 512), (3, 0, 512), (3, 512, 256), (3, 768, 256)]
-TENSOR_STEPS = 3
+WHOLE = 5
+STEPS = [(0, 0, 1024), (1, 0, 1024), (2, 0, 1024), (3, 0, 512), (3, 512, 256), (3, 768, 256)]
+TENSOR_STEPS = (1, 2)
+KEPT_STEPS = 3
+EARLY_SCALE_CHUNKS = 2
 
 
 def list_columns(list_tile, first, count):
@@ -71,19 +73,26 @@ def tile_moe_loc_lin_silu_kernel(tc, x_words, x_scales, xo, w, gate, offs, pos1,
         load_xo(1)
         for q in range(4):
             nc.sync.dma_start(token_scales[32 * q : 32 * q + 4, :], x_scales[0, 4 * q : 4 * q + 4, :].bitcast(I32))
-        for e, n0, width in pieces:
+
+        def load_w(piece):
+            e, n0, width = piece
             w_raw[e, n0] = sbuf.tile([P, 4, width], F32, name=f"w_raw{e}_{n0}", align_bytes=64)
             nc.sync.dma_start(w_raw[e, n0][:], w[e].rearrange("(p j) n -> p j n", j=4)[:, :, n0 : n0 + width])
+
+        for piece in pieces[:E]:
+            load_w(piece)
         for r, pos in enumerate((pos1, pos2)):
             nc.sync.dma_start(pos_t[r][:], pos)
             nc.sync.dma_start(gate_t[r][:], gate[r])
+        for piece in pieces[E:]:
+            load_w(piece)
 
-        pairs = [sbuf.tile([P, 2 * T], BF16, name=f"pairs{a}") for a in range(2)]
+        pairs = [sbuf.tile([P, 2 * T], BF16, name=f"pairs{a}", align_bytes=64) for a in range(2)]
         for a in range(2):
             for h in range(2):
                 nc.scalar.copy(
-                    pairs[a][:, h * T : (h + 1) * T].rearrange("p (t i) -> p t i", i=2),
-                    xo_raw[a, h][:].rearrange("p i t -> p t i"),
+                    pairs[a][:, h * T : (h + 1) * T].rearrange("p (g t i) -> p g i t", t=4, i=2),
+                    xo_raw[a, h][:].rearrange("p i (g t) -> p g i t", t=4),
                 )
 
         own_codes = sbuf.tile([P, S], U32, name="own_codes", align_bytes=64)
@@ -103,18 +112,23 @@ def tile_moe_loc_lin_silu_kernel(tc, x_words, x_scales, xo, w, gate, offs, pos1,
                 nc.vector.tensor_copy(
                     picked[:, a, :].bitcast(U32), pairs[a][:].bitcast(U32).indirect(list_columns(offs_t, c * CHUNK, CHUNK))
                 )
-            grouped.append(sbuf.tile([P, 4 * CHUNK], BF16, name="grouped", align_bytes=64, bufs=CHUNKS))
+            grouped.append(sbuf.tile([P, 4 * CHUNK], BF16, name=f"grouped{c}", align_bytes=64))
             nc.gpsimd.tensor_copy(
                 grouped[c][:].bitcast(I32).rearrange("p (s a) -> p s a", a=2),
                 picked[:].bitcast(I32).rearrange("p a s -> p s a"),
             )
 
-        far_scales = sbuf.tile([P, S], U8, name="far_scales", tag="xo_raw11", align_bytes=64)
-        for c in range(CHUNKS):
-            nc.vector.tensor_copy(
-                far_scales[:, c * CHUNK : (c + 1) * CHUNK],
-                token_scales[:].bitcast(U8).indirect(list_columns(offs2_t, c * CHUNK, CHUNK)),
-            )
+        far_scales = {}
+
+        def gather_far_scales(chunks, tag):
+            gathered = sbuf.tile([P, len(chunks) * CHUNK], U8, name=f"far_scales{chunks[0]}", tag=tag, align_bytes=64)
+            for place, c in enumerate(chunks):
+                far_scales[c] = gathered[:, place * CHUNK : (place + 1) * CHUNK]
+                nc.vector.tensor_copy(
+                    far_scales[c], token_scales[:].bitcast(U8).indirect(list_columns(offs2_t, c * CHUNK, CHUNK))
+                )
+
+        gather_far_scales(range(EARLY_SCALE_CHUNKS), "xo_raw11")
 
         w_grouped = {}
 
@@ -122,13 +136,13 @@ def tile_moe_loc_lin_silu_kernel(tc, x_words, x_scales, xo, w, gate, offs, pos1,
             e, n0, width = piece
             rounded = sbuf.tile([P, 4 * width], BF16, name=f"w_grouped{e}_{n0}", align_bytes=64)
             nc.scalar.copy(
-                rounded[:].rearrange("p (g i j) -> p g j i", i=4, j=4),
-                w_raw[e, n0][:].rearrange("p j (g i) -> p g j i", i=4),
+                rounded[:].rearrange("p (g i j) -> p g j i", i=2, j=4),
+                w_raw[e, n0][:].rearrange("p j (g i) -> p g j i", i=2),
             )
             for m0 in range(0, width, HALF):
                 w_grouped[e, (n0 + m0) // HALF] = rounded[:, 4 * m0 : 4 * (m0 + HALF)]
 
-        for piece in pieces[:-1]:
+        for piece in pieces[:E]:
             round_w(piece)
 
         w_codes = [sbuf.tile([P, E * HALF], U32, name=f"w_codes{half}", align_bytes=64) for half in range(2)]
@@ -146,11 +160,11 @@ def tile_moe_loc_lin_silu_kernel(tc, x_words, x_scales, xo, w, gate, offs, pos1,
             quantize_w(2 * c, 0)
             quantize_w(2 * c + 1, 0)
         w_scales.append(sbuf.tile([P, E * HALF], U8, name="w_scales1", tag=f"w_grouped{E - 1}_0", align_bytes=64))
-        for e in range(E - 1):
+        for e in range(WHOLE):
             quantize_w(e, 1)
 
-        def experts(c, nt, codes, scales, dest, bank_index):
-            bank = psum.tile([P, CHUNK], F32, name=f"bank{bank_index}")
+        def experts(c, nt, codes, scales, dest):
+            bank = psum.tile([P, CHUNK], F32, name="bank", bufs=CHUNKS)
             half, row0 = divmod(nt * P, HALF)
             for u in range(2):
                 e = 2 * c + u
@@ -160,7 +174,7 @@ def tile_moe_loc_lin_silu_kernel(tc, x_words, x_scales, xo, w, gate, offs, pos1,
                     lhsT=w_codes[half][:, rows].bitcast(FP8X4),
                     lhsT_scale=w_scales[half][:, rows],
                     rhs=codes[:, e * C : (e + 1) * C].bitcast(FP8X4),
-                    rhs_scale=scales[:, e * C : (e + 1) * C],
+                    rhs_scale=scales[:, u * C : (u + 1) * C],
                     start=True,
                     stop=True,
                 )
@@ -168,29 +182,20 @@ def tile_moe_loc_lin_silu_kernel(tc, x_words, x_scales, xo, w, gate, offs, pos1,
 
         y = {}
 
-        def own_tile(nt, tag, bank0):
+        def own_tile(nt, tag):
             y[nt] = sbuf.tile([P, S], F32, name=f"y{nt}", tag=tag, align_bytes=64)
             for c in range(CHUNKS):
-                experts(c, nt, own_codes, own_scales, y[nt][:, c * CHUNK : (c + 1) * CHUNK], bank0 + c)
+                experts(c, nt, own_codes, own_scales[:, c * CHUNK : (c + 1) * CHUNK], y[nt][:, c * CHUNK : (c + 1) * CHUNK])
 
-        def far_tile(nt, bank0):
-            z = sbuf.tile([P, S], F32, name=f"z{nt}", tag=f"w_raw{nt}_0", align_bytes=64)
-            for s0 in range(0, S, 2 * CHUNK):
-                for c in (s0 // CHUNK, s0 // CHUNK + 1):
-                    experts(c, nt, far_codes, far_scales, z[:, c * CHUNK : (c + 1) * CHUNK], bank0 + c)
-                queue = nc.scalar if nt == ROW_TILES - 1 else nc.sync
-                queue.dma_start(out[nt * P : (nt + 1) * P, T + s0 : T + s0 + 2 * CHUNK], z[:, s0 : s0 + 2 * CHUNK])
+        z_tags = ["xo_raw01", "xo_raw10", "pairs0", "pairs1", "w_raw5_0", "w_raw6_0", "w_raw5_256", "w_raw6_256"]
 
-        own_tile(0, f"w_raw{E - 1}_0", 0)
-        round_w(pieces[-1])
-        quantize_w(E - 1, 1)
-        own_tile(1, f"w_raw{E - 1}_{HALF}", CHUNKS)
-        far_tile(0, 0)
-        far_tile(1, CHUNKS)
-        own_tile(2, "w_raw4_0", 0)
-        far_tile(2, CHUNKS)
-        own_tile(3, "w_raw5_0", 0)
-        far_tile(3, CHUNKS)
+        def far_part(nt, part):
+            z = sbuf.tile([P, 2 * CHUNK], F32, name=f"z{nt}{part}", tag=z_tags[2 * nt + part], align_bytes=64)
+            for u in range(2):
+                c = 2 * part + u
+                experts(c, nt, far_codes, far_scales[c], z[:, u * CHUNK : (u + 1) * CHUNK])
+            s0 = T + 2 * part * CHUNK
+            nc.sync.dma_start(out[nt * P : (nt + 1) * P, s0 : s0 + 2 * CHUNK], z[:])
 
         identity = sbuf.tile([P, P], F32, name="identity")
         make_identity(nc, identity[:])
@@ -198,7 +203,7 @@ def tile_moe_loc_lin_silu_kernel(tc, x_words, x_scales, xo, w, gate, offs, pos1,
 
         def weigh(step, r):
             nt, t0, width = STEPS[step]
-            if step < TENSOR_STEPS:
+            if step < KEPT_STEPS:
                 tag = f"w_grouped{2 * step + r}_0"
                 products[step, r] = sbuf.tile([P, width], F32, name=f"kept{step}_{r}", tag=tag, align_bytes=64)
             else:
@@ -209,26 +214,41 @@ def tile_moe_loc_lin_silu_kernel(tc, x_words, x_scales, xo, w, gate, offs, pos1,
 
         def add_and_store(step):
             nt, t0, width = STEPS[step]
-            if nt < ROW_TILES - 1:
-                total = sbuf.tile([P, width], F32, name=f"total{step}", tag=f"w_raw{nt}_0", align_bytes=64)
-            else:
-                total = sbuf.tile([P, width], F32, name="total", tag="picked", bufs=CHUNKS)
+            total = sbuf.tile([P, width], F32, name=f"total{step}", tag=f"grouped{step - KEPT_STEPS + 1}", align_bytes=64)
             nc.vector.tensor_tensor(total[:], products[step, 0][:], products[step, 1][:], ADD)
             nc.sync.dma_start(out[nt * P : (nt + 1) * P, t0 : t0 + width], total[:])
 
-        for step in range(len(STEPS)):
-            weigh(step, 0)
-            if step > TENSOR_STEPS:
-                add_and_store(step - 1)
-            weigh(step, 1)
-        add_and_store(len(STEPS) - 1)
+        own_tile(0, f"w_raw{E - 1}_0")
+        weigh(0, 0)
+        weigh(0, 1)
+        gather_far_scales(range(EARLY_SCALE_CHUNKS, CHUNKS), f"w_raw{E - 1}_0")
+        first_sum = sbuf.tile([P, T], F32, name="first_sum", tag="xo_raw00", align_bytes=64)
+        nc.gpsimd.tensor_tensor(first_sum[:], products[0, 0][:], products[0, 1][:], ADD)
+        nc.sync.dma_start(out[0:P, 0:T], first_sum[:])
+        for piece in pieces[E:]:
+            round_w(piece)
+            quantize_w(piece[0], 1)
+        own_tile(1, f"w_raw{E - 1}_{HALF}")
+        far_part(0, 0)
+        far_part(1, 0)
+        own_tile(2, "w_raw0_0")
+        far_part(0, 1)
+        far_part(1, 1)
+        own_tile(3, "w_raw1_0")
+        for nt in range(2, ROW_TILES):
+            for part in range(2):
+                far_part(nt, part)
 
-        spans = [(step, b0) for step in range(TENSOR_STEPS) for b0 in range(0, STEPS[step][2], CHUNK)]
+        for step in TENSOR_STEPS:
+            weigh(step, 0)
+            weigh(step, 1)
+
+        spans = [(step, b0) for step in TENSOR_STEPS for b0 in range(0, STEPS[step][2], CHUNK)]
         turned = {}
 
         def turn(index):
             step, b0 = spans[index]
-            bank = psum.tile([P, CHUNK], F32, name=f"bank{index % CHUNKS}")
+            bank = psum.tile([P, CHUNK], F32, name="bank", bufs=CHUNKS)
             for b in range(0, CHUNK, P):
                 for r in range(2):
                     nc.tensor.matmul(
@@ -239,18 +259,18 @@ def tile_moe_loc_lin_silu_kernel(tc, x_words, x_scales, xo, w, gate, offs, pos1,
                         stop=r == 1,
                         is_transpose=True,
                     )
-            turned[index] = sbuf.tile([P, CHUNK], F32, name="turned", tag="grouped", align_bytes=64, bufs=CHUNKS)
+            turned[index] = sbuf.tile([P, CHUNK], F32, name=f"turned{index}", tag=f"grouped{index}", align_bytes=64)
             nc.scalar.copy(turned[index][:], bank[:])
 
         def turn_back(index):
             step, b0 = spans[index]
             nt, t0, width = STEPS[step]
-            bank = psum.tile([P, CHUNK], F32, name=f"bank{CHUNKS + index % CHUNKS}")
+            bank = psum.tile([P, CHUNK], F32, name="back_bank", bufs=CHUNKS)
             for b in range(0, CHUNK, P):
                 nc.tensor.transpose(bank[:, b : b + P], turned[index][:, b : b + P], identity[:])
-            summed = sbuf.tile([P, CHUNK], F32, name=f"summed{index}")
+            summed = sbuf.tile([P, CHUNK], F32, name=f"summed{index}", tag=f"w_grouped{5 + index % 2}_{HALF * (1 - index // 2)}" if index != 2 else "w_raw2_0", align_bytes=64)
             nc.scalar.copy(summed[:], bank[:])
-            nc.scalar.dma_start(out[nt * P : (nt + 1) * P, t0 + b0 : t0 + b0 + CHUNK], summed[:])
+            nc.sync.dma_start(out[nt * P : (nt + 1) * P, t0 + b0 : t0 + b0 + CHUNK], summed[:])
 
         LAG = 2
         for index in range(len(spans) + LAG):
@@ -258,3 +278,10 @@ def tile_moe_loc_lin_silu_kernel(tc, x_words, x_scales, xo, w, gate, offs, pos1,
                 turn(index)
             if index >= LAG:
                 turn_back(index - LAG)
+
+        for step in range(KEPT_STEPS, len(STEPS)):
+            weigh(step, 0)
+            if step > KEPT_STEPS:
+                add_and_store(step - 1)
+            weigh(step, 1)
+        add_and_store(len(STEPS) - 1)

@@ -28,8 +28,9 @@ HALF = N // 2
 WHOLE = 5
 STEPS = [(0, 0, 1024), (1, 0, 1024), (2, 0, 1024), (3, 0, 512), (3, 512, 256), (3, 768, 256)]
 TENSOR_STEPS = (1, 2)
-KEPT_STEPS = 3
+FIRST_VECTOR_STEP = 3
 EARLY_SCALE_CHUNKS = 2
+TURN_LAG = 2
 
 
 def list_columns(list_tile, first, count):
@@ -106,16 +107,20 @@ def tile_moe_loc_lin_silu_kernel(tc, x_words, x_scales, xo, w, gate, offs, pos1,
             )
 
         grouped = []
+        two_chunks = [
+            sbuf.tile([P, 4 * CHUNK], I32, name="picked0"),
+            sbuf.tile([P, 4 * CHUNK], I32, name="picked1", tag="xo_raw11", align_bytes=64),
+        ]
         for c in range(CHUNKS):
-            picked = sbuf.tile([P, 2, 2 * CHUNK], BF16, name="picked", bufs=CHUNKS)
+            picked = two_chunks[c // 2][:, c % 2 * 2 * CHUNK : (c % 2 + 1) * 2 * CHUNK]
             for a in range(2):
                 nc.vector.tensor_copy(
-                    picked[:, a, :].bitcast(U32), pairs[a][:].bitcast(U32).indirect(list_columns(offs_t, c * CHUNK, CHUNK))
+                    picked[:, a * CHUNK : (a + 1) * CHUNK].bitcast(U32), pairs[a][:].bitcast(U32).indirect(list_columns(offs_t, c * CHUNK, CHUNK))
                 )
             grouped.append(sbuf.tile([P, 4 * CHUNK], BF16, name=f"grouped{c}", align_bytes=64))
             nc.gpsimd.tensor_copy(
                 grouped[c][:].bitcast(I32).rearrange("p (s a) -> p s a", a=2),
-                picked[:].bitcast(I32).rearrange("p a s -> p s a"),
+                picked.rearrange("p (a s) -> p s a", a=2),
             )
 
         far_scales = {}
@@ -128,7 +133,7 @@ def tile_moe_loc_lin_silu_kernel(tc, x_words, x_scales, xo, w, gate, offs, pos1,
                     far_scales[c], token_scales[:].bitcast(U8).indirect(list_columns(offs2_t, c * CHUNK, CHUNK))
                 )
 
-        gather_far_scales(range(EARLY_SCALE_CHUNKS), "xo_raw11")
+        gather_far_scales(range(EARLY_SCALE_CHUNKS), "pairs1")
 
         w_grouped = {}
 
@@ -187,7 +192,7 @@ def tile_moe_loc_lin_silu_kernel(tc, x_words, x_scales, xo, w, gate, offs, pos1,
             for c in range(CHUNKS):
                 experts(c, nt, own_codes, own_scales[:, c * CHUNK : (c + 1) * CHUNK], y[nt][:, c * CHUNK : (c + 1) * CHUNK])
 
-        z_tags = ["xo_raw01", "xo_raw10", "pairs0", "pairs1", "w_raw5_0", "w_raw6_0", "w_raw5_256", "w_raw6_256"]
+        z_tags = ["xo_raw01", "xo_raw10", "pairs0", "xo_raw11", "w_raw5_0", "w_raw6_0", "w_raw5_256", "w_raw6_256"]
 
         def far_part(nt, part):
             z = sbuf.tile([P, 2 * CHUNK], F32, name=f"z{nt}{part}", tag=z_tags[2 * nt + part], align_bytes=64)
@@ -203,7 +208,7 @@ def tile_moe_loc_lin_silu_kernel(tc, x_words, x_scales, xo, w, gate, offs, pos1,
 
         def weigh(step, r):
             nt, t0, width = STEPS[step]
-            if step < KEPT_STEPS:
+            if step < FIRST_VECTOR_STEP:
                 tag = f"w_grouped{2 * step + r}_0"
                 products[step, r] = sbuf.tile([P, width], F32, name=f"kept{step}_{r}", tag=tag, align_bytes=64)
             else:
@@ -214,7 +219,8 @@ def tile_moe_loc_lin_silu_kernel(tc, x_words, x_scales, xo, w, gate, offs, pos1,
 
         def add_and_store(step):
             nt, t0, width = STEPS[step]
-            total = sbuf.tile([P, width], F32, name=f"total{step}", tag=f"grouped{step - KEPT_STEPS + 1}", align_bytes=64)
+            tag = f"grouped{step - FIRST_VECTOR_STEP + 1}"
+            total = sbuf.tile([P, width], F32, name=f"total{step}", tag=tag, align_bytes=64)
             nc.vector.tensor_tensor(total[:], products[step, 0][:], products[step, 1][:], ADD)
             nc.sync.dma_start(out[nt * P : (nt + 1) * P, t0 : t0 + width], total[:])
 
@@ -245,6 +251,7 @@ def tile_moe_loc_lin_silu_kernel(tc, x_words, x_scales, xo, w, gate, offs, pos1,
 
         spans = [(step, b0) for step in TENSOR_STEPS for b0 in range(0, STEPS[step][2], CHUNK)]
         turned = {}
+        summed_tags = [f"w_grouped5_{HALF}", f"w_grouped6_{HALF}", "w_raw2_0", "w_grouped6_0"]
 
         def turn(index):
             step, b0 = spans[index]
@@ -264,24 +271,23 @@ def tile_moe_loc_lin_silu_kernel(tc, x_words, x_scales, xo, w, gate, offs, pos1,
 
         def turn_back(index):
             step, b0 = spans[index]
-            nt, t0, width = STEPS[step]
+            nt, t0 = STEPS[step][:2]
             bank = psum.tile([P, CHUNK], F32, name="back_bank", bufs=CHUNKS)
             for b in range(0, CHUNK, P):
                 nc.tensor.transpose(bank[:, b : b + P], turned[index][:, b : b + P], identity[:])
-            summed = sbuf.tile([P, CHUNK], F32, name=f"summed{index}", tag=f"w_grouped{5 + index % 2}_{HALF * (1 - index // 2)}" if index != 2 else "w_raw2_0", align_bytes=64)
+            summed = sbuf.tile([P, CHUNK], F32, name=f"summed{index}", tag=summed_tags[index], align_bytes=64)
             nc.scalar.copy(summed[:], bank[:])
             nc.sync.dma_start(out[nt * P : (nt + 1) * P, t0 + b0 : t0 + b0 + CHUNK], summed[:])
 
-        LAG = 2
-        for index in range(len(spans) + LAG):
+        for index in range(len(spans) + TURN_LAG):
             if index < len(spans):
                 turn(index)
-            if index >= LAG:
-                turn_back(index - LAG)
+            if index >= TURN_LAG:
+                turn_back(index - TURN_LAG)
 
-        for step in range(KEPT_STEPS, len(STEPS)):
+        for step in range(FIRST_VECTOR_STEP, len(STEPS)):
             weigh(step, 0)
-            if step > KEPT_STEPS:
+            if step > FIRST_VECTOR_STEP:
                 add_and_store(step - 1)
             weigh(step, 1)
         add_and_store(len(STEPS) - 1)

@@ -25,11 +25,12 @@ CHUNK = 512
 CHUNKS = S // CHUNK
 HALF = N // 2
 
-WHOLE = 5
+WHOLE = 4
+LAST_RAW = 4 * S - CHUNK
 STEPS = [(0, 0, 1024), (1, 0, 1024), (2, 0, 1024), (3, 0, 512), (3, 512, 256), (3, 768, 256)]
 TENSOR_STEPS = (1, 2)
 FIRST_VECTOR_STEP = 3
-EARLY_SCALE_CHUNKS = 2
+PIECES = [(0, 512), (512, 512), (1024, 512), (1536, 256), (1792, 256)]
 TURN_LAG = 2
 
 
@@ -41,6 +42,7 @@ def tile_moe_loc_lin_silu_kernel(tc, x_words, x_scales, xo, w, gate, offs, pos1,
     nc = tc.nc
     with ExitStack() as ctx:
         sbuf = ctx.enter_context(tc.tile_pool(name="sbuf", bufs=1))
+        shared = ctx.enter_context(tc.tile_pool(name="shared", bufs=1))
         psum = ctx.enter_context(tc.psum_pool(name="psum", bufs=1))
 
         offs2_t = sbuf.tile([P, S // PER_COLUMN], U16, name="offs2_t")
@@ -48,10 +50,8 @@ def tile_moe_loc_lin_silu_kernel(tc, x_words, x_scales, xo, w, gate, offs, pos1,
         pos_t = [sbuf.tile([P, T // PER_COLUMN], U16, name=f"pos_t{r}") for r in range(2)]
         gate_t = [sbuf.tile([P, T], F32, name=f"gate_t{r}") for r in range(2)]
         token_words = sbuf.tile([P, Q], I32, name="token_words")
-        token_scales = sbuf.tile([P, Q // 4], I32, name="token_scales")
-        xo_raw = {
-            (a, h): sbuf.tile([P, 2, T // 2], F32, name=f"xo_raw{a}{h}", align_bytes=64) for a in range(2) for h in range(2)
-        }
+        token_scales = sbuf.tile([P, Q // 4], I32, name="token_scales", align_bytes=64)
+        xo_raw = [sbuf.tile([P, 2, T], F32, name=f"xo_raw{a}", align_bytes=64) for a in range(2)]
 
         warm = sbuf.tile([P, 16], F32, name="warm")
         nc.vector.memset(warm[:, 0:8], 0.0)
@@ -64,8 +64,7 @@ def tile_moe_loc_lin_silu_kernel(tc, x_words, x_scales, xo, w, gate, offs, pos1,
         xo_rows = xo.rearrange("(p j) t -> p j t", j=4)
 
         def load_xo(a):
-            for h in range(2):
-                nc.sync.dma_start(xo_raw[a, h][:], xo_rows[:, 2 * a : 2 * a + 2, h * T // 2 : (h + 1) * T // 2])
+            nc.sync.dma_start(xo_raw[a][:], xo_rows[:, 2 * a : 2 * a + 2, :])
 
         nc.sync.dma_start(offs2_t[:], offs2)
         nc.sync.dma_start(token_words[:], x_words[0].rearrange("p t d -> p (t d)").bitcast(I32))
@@ -77,7 +76,10 @@ def tile_moe_loc_lin_silu_kernel(tc, x_words, x_scales, xo, w, gate, offs, pos1,
 
         def load_w(piece):
             e, n0, width = piece
-            w_raw[e, n0] = sbuf.tile([P, 4, width], F32, name=f"w_raw{e}_{n0}", align_bytes=64)
+            if (e, n0) == (E - 1, 0):
+                w_raw[e, n0] = shared.tile([P, 4, width], F32, name="w_raw_last", align_bytes=64, offset=LAST_RAW)
+            else:
+                w_raw[e, n0] = sbuf.tile([P, 4, width], F32, name=f"w_raw{e}_{n0}", align_bytes=64)
             nc.sync.dma_start(w_raw[e, n0][:], w[e].rearrange("(p j) n -> p j n", j=4)[:, :, n0 : n0 + width])
 
         for piece in pieces[:E]:
@@ -90,11 +92,10 @@ def tile_moe_loc_lin_silu_kernel(tc, x_words, x_scales, xo, w, gate, offs, pos1,
 
         pairs = [sbuf.tile([P, 2 * T], BF16, name=f"pairs{a}", align_bytes=64) for a in range(2)]
         for a in range(2):
-            for h in range(2):
-                nc.scalar.copy(
-                    pairs[a][:, h * T : (h + 1) * T].rearrange("p (g t i) -> p g i t", t=4, i=2),
-                    xo_raw[a, h][:].rearrange("p i (g t) -> p g i t", t=4),
-                )
+            nc.scalar.copy(
+                pairs[a][:].rearrange("p (g t i) -> p g i t", t=4, i=2),
+                xo_raw[a][:].rearrange("p i (g t) -> p g i t", t=4),
+            )
 
         own_codes = sbuf.tile([P, S], U32, name="own_codes", align_bytes=64)
         own_scales = sbuf.tile([P, S], U8, name="own_scales", align_bytes=64)
@@ -106,78 +107,90 @@ def tile_moe_loc_lin_silu_kernel(tc, x_words, x_scales, xo, w, gate, offs, pos1,
                 token_words[:].bitcast(U32).indirect(list_columns(offs2_t, c * CHUNK, CHUNK)),
             )
 
-        grouped = []
         two_chunks = [
-            sbuf.tile([P, 4 * CHUNK], I32, name="picked0"),
-            sbuf.tile([P, 4 * CHUNK], I32, name="picked1", tag="xo_raw11", align_bytes=64),
+            sbuf.tile([P, 4 * CHUNK], I32, name="picked0", align_bytes=64),
+            sbuf.tile([P, 4 * CHUNK], I32, name="picked1", tag="xo_raw1", align_bytes=64),
         ]
-        for c in range(CHUNKS):
-            picked = two_chunks[c // 2][:, c % 2 * 2 * CHUNK : (c % 2 + 1) * 2 * CHUNK]
+        grouped = [sbuf.tile([P, 4 * CHUNK], BF16, name=f"grouped{c}", align_bytes=64) for c in range(CHUNKS)]
+        for s0, count in PIECES:
+            c, place = divmod(s0, CHUNK)
+            first = 2 * (s0 % (2 * CHUNK))
+            picked = two_chunks[c // 2][:, first : first + 2 * count]
             for a in range(2):
                 nc.vector.tensor_copy(
-                    picked[:, a * CHUNK : (a + 1) * CHUNK].bitcast(U32), pairs[a][:].bitcast(U32).indirect(list_columns(offs_t, c * CHUNK, CHUNK))
+                    picked[:, a * count : (a + 1) * count].bitcast(U32), pairs[a][:].bitcast(U32).indirect(list_columns(offs_t, s0, count))
                 )
-            grouped.append(sbuf.tile([P, 4 * CHUNK], BF16, name=f"grouped{c}", align_bytes=64))
             nc.gpsimd.tensor_copy(
-                grouped[c][:].bitcast(I32).rearrange("p (s a) -> p s a", a=2),
+                grouped[c][:, 4 * place : 4 * (place + count)].bitcast(I32).rearrange("p (s a) -> p s a", a=2),
                 picked.rearrange("p (a s) -> p s a", a=2),
             )
 
         far_scales = {}
 
-        def gather_far_scales(chunks, tag):
-            gathered = sbuf.tile([P, len(chunks) * CHUNK], U8, name=f"far_scales{chunks[0]}", tag=tag, align_bytes=64)
+        def behind(name, width, dtype, tag):
+            return sbuf.tile([P, width], dtype, name=name, tag=tag, align_bytes=64)
+
+        def behind_last_raw(name, place):
+            return shared.tile([P, CHUNK], U8, name=name, align_bytes=64, offset=LAST_RAW + (1 + place) * CHUNK)
+
+        def gather_far_scales(chunks, gathered):
             for place, c in enumerate(chunks):
                 far_scales[c] = gathered[:, place * CHUNK : (place + 1) * CHUNK]
                 nc.vector.tensor_copy(
                     far_scales[c], token_scales[:].bitcast(U8).indirect(list_columns(offs2_t, c * CHUNK, CHUNK))
                 )
 
-        gather_far_scales(range(EARLY_SCALE_CHUNKS), "pairs1")
+        gather_far_scales([0], behind("far_scales0", CHUNK, U8, "pairs0"))
 
         w_grouped = {}
 
-        def round_w(piece):
-            e, n0, width = piece
-            rounded = sbuf.tile([P, 4 * width], BF16, name=f"w_grouped{e}_{n0}", align_bytes=64)
+        def round_w(e, half):
+            c, u = divmod(e, 2)
+            if u == 0:
+                w_grouped[c, half] = sbuf.tile([P, 8 * HALF], BF16, name=f"w_grouped{c}_{half}", align_bytes=64)
+            raw = w_raw[e, 0][:, :, half * HALF : (half + 1) * HALF] if e < WHOLE else w_raw[e, half * HALF][:]
             nc.scalar.copy(
-                rounded[:].rearrange("p (g i j) -> p g j i", i=2, j=4),
-                w_raw[e, n0][:].rearrange("p j (g i) -> p g j i", i=2),
+                w_grouped[c, half][:, u * 4 * HALF : (u + 1) * 4 * HALF].rearrange("p (g i j) -> p g j i", i=2, j=4),
+                raw.rearrange("p j (g i) -> p g j i", i=2),
             )
-            for m0 in range(0, width, HALF):
-                w_grouped[e, (n0 + m0) // HALF] = rounded[:, 4 * m0 : 4 * (m0 + HALF)]
 
-        for piece in pieces[:E]:
-            round_w(piece)
+        for e in range(E):
+            for half in range(2 if e < WHOLE else 1):
+                round_w(e, half)
 
-        w_codes = [sbuf.tile([P, E * HALF], U32, name=f"w_codes{half}", align_bytes=64) for half in range(2)]
-        w_scales = [sbuf.tile([P, E * HALF], U8, name="w_scales0", align_bytes=64)]
+        w_codes, w_scales = {}, {}
 
-        def quantize_w(e, half):
-            cols = slice(e * HALF, (e + 1) * HALF)
-            nc.vector.quantize_mx(
-                out=w_codes[half][:, cols].bitcast(FP8X4), scales=w_scales[half][:, cols], in_=w_grouped[e, half]
-            )
+        def quantize_w(c, half, calls=1, scales=None):
+            w_codes[c, half] = sbuf.tile([P, 2 * HALF], U32, name=f"w_codes{c}_{half}", align_bytes=64)
+            if scales is None:
+                scales = sbuf.tile([P, 2 * HALF], U8, name=f"w_scales{c}_{half}", align_bytes=64)
+            w_scales[c, half] = scales
+            width = 2 * HALF // calls
+            for m0 in range(0, 2 * HALF, width):
+                nc.vector.quantize_mx(
+                    out=w_codes[c, half][:, m0 : m0 + width].bitcast(FP8X4),
+                    scales=w_scales[c, half][:, m0 : m0 + width],
+                    in_=w_grouped[c, half][:, 4 * m0 : 4 * (m0 + width)],
+                )
 
         for c in range(CHUNKS):
             slots = slice(c * CHUNK, (c + 1) * CHUNK)
             nc.vector.quantize_mx(out=own_codes[:, slots].bitcast(FP8X4), scales=own_scales[:, slots], in_=grouped[c][:])
-            quantize_w(2 * c, 0)
-            quantize_w(2 * c + 1, 0)
-        w_scales.append(sbuf.tile([P, E * HALF], U8, name="w_scales1", tag=f"w_grouped{E - 1}_0", align_bytes=64))
-        for e in range(WHOLE):
-            quantize_w(e, 1)
+            quantize_w(c, 0, calls=2 if c == CHUNKS - 1 else 1)
+        quantize_w(0, 1, scales=behind_last_raw("w_scales0_1", 0))
+        quantize_w(1, 1, scales=behind_last_raw("w_scales1_1", 1))
+        gather_far_scales([1], behind_last_raw("far_scales1", 2))
 
         def experts(c, nt, codes, scales, dest):
             bank = psum.tile([P, CHUNK], F32, name="bank", bufs=CHUNKS)
             half, row0 = divmod(nt * P, HALF)
             for u in range(2):
                 e = 2 * c + u
-                rows = slice(e * HALF + row0, e * HALF + row0 + P)
+                rows = slice(u * HALF + row0, u * HALF + row0 + P)
                 nc.tensor.matmul_mx(
                     out=bank[:, u * C : (u + 1) * C],
-                    lhsT=w_codes[half][:, rows].bitcast(FP8X4),
-                    lhsT_scale=w_scales[half][:, rows],
+                    lhsT=w_codes[c, half][:, rows].bitcast(FP8X4),
+                    lhsT_scale=w_scales[c, half][:, rows],
                     rhs=codes[:, e * C : (e + 1) * C].bitcast(FP8X4),
                     rhs_scale=scales[:, u * C : (u + 1) * C],
                     start=True,
@@ -187,12 +200,15 @@ def tile_moe_loc_lin_silu_kernel(tc, x_words, x_scales, xo, w, gate, offs, pos1,
 
         y = {}
 
-        def own_tile(nt, tag):
-            y[nt] = sbuf.tile([P, S], F32, name=f"y{nt}", tag=tag, align_bytes=64)
-            for c in range(CHUNKS):
+        def own_tile(nt, tag, chunks=range(CHUNKS)):
+            if nt == 0:
+                y[nt] = shared.tile([P, S], F32, name="y0", align_bytes=64, offset=0)
+            elif nt not in y:
+                y[nt] = behind(f"y{nt}", S, F32, tag)
+            for c in chunks:
                 experts(c, nt, own_codes, own_scales[:, c * CHUNK : (c + 1) * CHUNK], y[nt][:, c * CHUNK : (c + 1) * CHUNK])
 
-        z_tags = ["xo_raw01", "xo_raw10", "pairs0", "xo_raw11", "w_raw5_0", "w_raw6_0", "w_raw5_256", "w_raw6_256"]
+        z_tags = ["w_raw2_0", "w_grouped0_1", "pairs1", "w_grouped1_1", "w_raw4_0", "xo_raw1", "w_raw5_0", "w_raw6_0"]
 
         def far_part(nt, part):
             z = sbuf.tile([P, 2 * CHUNK], F32, name=f"z{nt}{part}", tag=z_tags[2 * nt + part], align_bytes=64)
@@ -206,52 +222,59 @@ def tile_moe_loc_lin_silu_kernel(tc, x_words, x_scales, xo, w, gate, offs, pos1,
         make_identity(nc, identity[:])
         products = {}
 
-        def weigh(step, r):
-            nt, t0, width = STEPS[step]
-            if step < FIRST_VECTOR_STEP:
-                tag = f"w_grouped{2 * step + r}_0"
-                products[step, r] = sbuf.tile([P, width], F32, name=f"kept{step}_{r}", tag=tag, align_bytes=64)
-            else:
-                products[step, r] = sbuf.tile([P, width], F32, name=f"product{r}", bufs=2)
+        def weigh(step, r, product, first=0):
+            nt, t0 = STEPS[step][:2]
+            width = product.shape[1]
+            for b0 in range(0, width, CHUNK):
+                products[step, r, first + b0] = product[:, b0 : min(b0 + CHUNK, width)]
+            t0 = t0 + first
             nc.vector.tensor_tensor(
-                products[step, r][:], y[nt][:].indirect(list_columns(pos_t[r], t0, width)), gate_t[r][:, t0 : t0 + width], MULT
+                product, y[nt][:].indirect(list_columns(pos_t[r], t0, width)), gate_t[r][:, t0 : t0 + width], MULT
             )
+
+        def kept(name, width, tag):
+            return behind(name, width, F32, tag)
 
         def add_and_store(step):
             nt, t0, width = STEPS[step]
             tag = f"grouped{step - FIRST_VECTOR_STEP + 1}"
             total = sbuf.tile([P, width], F32, name=f"total{step}", tag=tag, align_bytes=64)
-            nc.vector.tensor_tensor(total[:], products[step, 0][:], products[step, 1][:], ADD)
+            nc.vector.tensor_tensor(total[:], products[step, 0, 0], products[step, 1, 0], ADD)
             nc.sync.dma_start(out[nt * P : (nt + 1) * P, t0 : t0 + width], total[:])
 
-        own_tile(0, f"w_raw{E - 1}_0")
-        weigh(0, 0)
-        weigh(0, 1)
-        gather_far_scales(range(EARLY_SCALE_CHUNKS, CHUNKS), f"w_raw{E - 1}_0")
-        first_sum = sbuf.tile([P, T], F32, name="first_sum", tag="xo_raw00", align_bytes=64)
-        nc.gpsimd.tensor_tensor(first_sum[:], products[0, 0][:], products[0, 1][:], ADD)
+        own_tile(0, None)
+        first_products = [kept(f"kept0_{r}", T, f"w_grouped{r}_0") for r in range(2)]
+        for r in range(2):
+            weigh(0, r, first_products[r][:])
+        first_sum = sbuf.tile([P, T], F32, name="first_sum", tag="xo_raw0", align_bytes=64)
+        nc.gpsimd.tensor_tensor(first_sum[:], first_products[0][:], first_products[1][:], ADD)
         nc.sync.dma_start(out[0:P, 0:T], first_sum[:])
-        for piece in pieces[E:]:
-            round_w(piece)
-            quantize_w(piece[0], 1)
-        own_tile(1, f"w_raw{E - 1}_{HALF}")
+        own_tile(1, "w_raw0_0")
         far_part(0, 0)
+        for e in range(WHOLE, E):
+            round_w(e, 1)
+        gather_far_scales(range(2, CHUNKS), behind("far_scales2", 2 * CHUNK, U8, f"w_raw4_{HALF}"))
+        quantize_w(2, 1)
+        weigh(1, 0, kept("kept1_early", CHUNK, f"w_raw5_{HALF}")[:])
+        quantize_w(3, 1)
+        late_products = kept("kept1_late", 3 * CHUNK, f"w_raw7_{HALF}")
+        weigh(1, 0, late_products[:, 0:CHUNK], CHUNK)
+        weigh(1, 1, late_products[:, CHUNK:])
         far_part(1, 0)
-        own_tile(2, "w_raw0_0")
+        own_tile(2, f"w_raw6_{HALF}", range(2))
         far_part(0, 1)
+        own_tile(2, None, range(2, CHUNKS))
         far_part(1, 1)
         own_tile(3, "w_raw1_0")
         for nt in range(2, ROW_TILES):
             for part in range(2):
                 far_part(nt, part)
-
-        for step in TENSOR_STEPS:
-            weigh(step, 0)
-            weigh(step, 1)
+        weigh(2, 0, kept("kept2_0", T, "w_grouped2_0")[:])
+        weigh(2, 1, kept("kept2_1", T, "w_raw3_0")[:])
 
         spans = [(step, b0) for step in TENSOR_STEPS for b0 in range(0, STEPS[step][2], CHUNK)]
         turned = {}
-        summed_tags = [f"w_grouped5_{HALF}", f"w_grouped6_{HALF}", "w_raw2_0", "w_grouped6_0"]
+        summed_tags = ["summed0", "summed1", "picked0", "summed3"]
 
         def turn(index):
             step, b0 = spans[index]
@@ -260,7 +283,7 @@ def tile_moe_loc_lin_silu_kernel(tc, x_words, x_scales, xo, w, gate, offs, pos1,
                 for r in range(2):
                     nc.tensor.matmul(
                         bank[:, b : b + P],
-                        products[step, r][:, b0 + b : b0 + b + P],
+                        products[step, r, b0][:, b : b + P],
                         identity[:],
                         start=r == 0,
                         stop=r == 1,
@@ -286,8 +309,8 @@ def tile_moe_loc_lin_silu_kernel(tc, x_words, x_scales, xo, w, gate, offs, pos1,
                 turn_back(index - TURN_LAG)
 
         for step in range(FIRST_VECTOR_STEP, len(STEPS)):
-            weigh(step, 0)
+            weigh(step, 0, sbuf.tile([P, STEPS[step][2]], F32, name="product0", bufs=2)[:])
             if step > FIRST_VECTOR_STEP:
                 add_and_store(step - 1)
-            weigh(step, 1)
+            weigh(step, 1, sbuf.tile([P, STEPS[step][2]], F32, name="product1", bufs=2)[:])
         add_and_store(len(STEPS) - 1)

@@ -25,8 +25,8 @@ CHUNK = 512
 CHUNKS = S // CHUNK
 HALF = N // 2
 
-WHOLE = 4
-LAST_RAW = 4 * S - CHUNK
+WHOLE = 6
+XO_PIECES = [(0, 0, T), (1, 0, T)]
 STEPS = [(0, 0, 1024), (1, 0, 1024), (2, 0, 1024), (3, 0, 512), (3, 512, 256), (3, 768, 256)]
 TENSOR_STEPS = (1, 2)
 FIRST_VECTOR_STEP = 3
@@ -42,7 +42,6 @@ def tile_moe_loc_lin_silu_kernel(tc, x_words, x_scales, xo, w, gate, offs, pos1,
     nc = tc.nc
     with ExitStack() as ctx:
         sbuf = ctx.enter_context(tc.tile_pool(name="sbuf", bufs=1))
-        shared = ctx.enter_context(tc.tile_pool(name="shared", bufs=1))
         psum = ctx.enter_context(tc.psum_pool(name="psum", bufs=1))
 
         offs2_t = sbuf.tile([P, S // PER_COLUMN], U16, name="offs2_t")
@@ -51,35 +50,34 @@ def tile_moe_loc_lin_silu_kernel(tc, x_words, x_scales, xo, w, gate, offs, pos1,
         gate_t = [sbuf.tile([P, T], F32, name=f"gate_t{r}") for r in range(2)]
         token_words = sbuf.tile([P, Q], I32, name="token_words")
         token_scales = sbuf.tile([P, Q // 4], I32, name="token_scales", align_bytes=64)
-        xo_raw = [sbuf.tile([P, 2, T], F32, name=f"xo_raw{a}", align_bytes=64) for a in range(2)]
+        xo_raw = {(a, t0): sbuf.tile([P, 2, width], F32, name=f"xo_raw{a}_{t0}", align_bytes=64) for a, t0, width in XO_PIECES}
+
+        nc.vector.memset(token_scales[:], 0)
+        nc.sync.dma_start(offs2_t[:], offs2)
+        nc.sync.dma_start(token_words[:], x_words[0].rearrange("p t d -> p (t d)").bitcast(I32))
+        for q in range(4):
+            nc.sync.dma_start(token_scales[32 * q : 32 * q + 4, :], x_scales[0, 4 * q : 4 * q + 4, :].bitcast(I32))
 
         warm = sbuf.tile([P, 16], F32, name="warm")
         nc.vector.memset(warm[:, 0:8], 0.0)
         nc.scalar.activation(warm[:, 8:16], warm[:, 0:8], SILU)
-        nc.vector.memset(token_scales[:], 0)
 
         pieces = [(e, 0, N) for e in range(WHOLE)] + [(e, n0, HALF) for n0 in (0, HALF) for e in range(WHOLE, E)]
         w_raw = {}
 
         xo_rows = xo.rearrange("(p j) t -> p j t", j=4)
 
-        def load_xo(a):
-            nc.sync.dma_start(xo_raw[a][:], xo_rows[:, 2 * a : 2 * a + 2, :])
+        def load_xo(piece):
+            a, t0, width = piece
+            nc.sync.dma_start(xo_raw[a, t0][:], xo_rows[:, 2 * a : 2 * a + 2, t0 : t0 + width])
 
-        nc.sync.dma_start(offs2_t[:], offs2)
-        nc.sync.dma_start(token_words[:], x_words[0].rearrange("p t d -> p (t d)").bitcast(I32))
-        load_xo(0)
+        load_xo(XO_PIECES[0])
         nc.sync.dma_start(offs_t[:], offs)
-        load_xo(1)
-        for q in range(4):
-            nc.sync.dma_start(token_scales[32 * q : 32 * q + 4, :], x_scales[0, 4 * q : 4 * q + 4, :].bitcast(I32))
+        load_xo(XO_PIECES[1])
 
         def load_w(piece):
             e, n0, width = piece
-            if (e, n0) == (E - 1, 0):
-                w_raw[e, n0] = shared.tile([P, 4, width], F32, name="w_raw_last", align_bytes=64, offset=LAST_RAW)
-            else:
-                w_raw[e, n0] = sbuf.tile([P, 4, width], F32, name=f"w_raw{e}_{n0}", align_bytes=64)
+            w_raw[e, n0] = sbuf.tile([P, 4, width], F32, name=f"w_raw{e}_{n0}", align_bytes=64)
             nc.sync.dma_start(w_raw[e, n0][:], w[e].rearrange("(p j) n -> p j n", j=4)[:, :, n0 : n0 + width])
 
         for piece in pieces[:E]:
@@ -91,25 +89,36 @@ def tile_moe_loc_lin_silu_kernel(tc, x_words, x_scales, xo, w, gate, offs, pos1,
             load_w(piece)
 
         pairs = [sbuf.tile([P, 2 * T], BF16, name=f"pairs{a}", align_bytes=64) for a in range(2)]
-        for a in range(2):
+        for a, t0, width in XO_PIECES:
             nc.scalar.copy(
-                pairs[a][:].rearrange("p (g t i) -> p g i t", t=4, i=2),
-                xo_raw[a][:].rearrange("p i (g t) -> p g i t", t=4),
+                pairs[a][:, 2 * t0 : 2 * (t0 + width)].rearrange("p (g t i) -> p g i t", t=4, i=2),
+                xo_raw[a, t0][:].rearrange("p i (g t) -> p g i t", t=4),
             )
 
         own_codes = sbuf.tile([P, S], U32, name="own_codes", align_bytes=64)
         own_scales = sbuf.tile([P, S], U8, name="own_scales", align_bytes=64)
-        far_codes = sbuf.tile([P, S], U32, name="far_codes", align_bytes=64)
+        far_codes, far_scales = {}, {}
 
-        for c in range(CHUNKS):
-            nc.vector.tensor_copy(
-                far_codes[:, c * CHUNK : (c + 1) * CHUNK],
-                token_words[:].bitcast(U32).indirect(list_columns(offs2_t, c * CHUNK, CHUNK)),
-            )
+        def behind(name, width, dtype, tag):
+            return sbuf.tile([P, width], dtype, name=name, tag=tag, align_bytes=64)
+
+        def gather_far(chunks, gathered, table, found):
+            for place, c in enumerate(chunks):
+                found[c] = gathered[:, place * CHUNK : (place + 1) * CHUNK]
+                nc.vector.tensor_copy(found[c], table.indirect(list_columns(offs2_t, c * CHUNK, CHUNK)))
+
+        def gather_far_scales(chunks, gathered):
+            gather_far(chunks, gathered, token_scales[:].bitcast(U8), far_scales)
+
+        def gather_far_words(chunks, gathered):
+            gather_far(chunks, gathered, token_words[:].bitcast(U32), far_codes)
+
+        gather_far_words(range(3), sbuf.tile([P, 3 * CHUNK], U32, name="far_codes0", align_bytes=64))
+        gather_far_scales([0], sbuf.tile([P, CHUNK], U8, name="far_scales0", align_bytes=64))
 
         two_chunks = [
             sbuf.tile([P, 4 * CHUNK], I32, name="picked0", align_bytes=64),
-            sbuf.tile([P, 4 * CHUNK], I32, name="picked1", tag="xo_raw1", align_bytes=64),
+            sbuf.tile([P, 4 * CHUNK], I32, name="picked1", tag="xo_raw1_0", align_bytes=64),
         ]
         grouped = [sbuf.tile([P, 4 * CHUNK], BF16, name=f"grouped{c}", align_bytes=64) for c in range(CHUNKS)]
         for s0, count in PIECES:
@@ -125,22 +134,7 @@ def tile_moe_loc_lin_silu_kernel(tc, x_words, x_scales, xo, w, gate, offs, pos1,
                 picked.rearrange("p (a s) -> p s a", a=2),
             )
 
-        far_scales = {}
-
-        def behind(name, width, dtype, tag):
-            return sbuf.tile([P, width], dtype, name=name, tag=tag, align_bytes=64)
-
-        def behind_last_raw(name, place):
-            return shared.tile([P, CHUNK], U8, name=name, align_bytes=64, offset=LAST_RAW + (1 + place) * CHUNK)
-
-        def gather_far_scales(chunks, gathered):
-            for place, c in enumerate(chunks):
-                far_scales[c] = gathered[:, place * CHUNK : (place + 1) * CHUNK]
-                nc.vector.tensor_copy(
-                    far_scales[c], token_scales[:].bitcast(U8).indirect(list_columns(offs2_t, c * CHUNK, CHUNK))
-                )
-
-        gather_far_scales([0], behind("far_scales0", CHUNK, U8, "pairs0"))
+        gather_far_words([3], behind("far_codes3", CHUNK, U32, "pairs0"))
 
         w_grouped = {}
 
@@ -160,11 +154,9 @@ def tile_moe_loc_lin_silu_kernel(tc, x_words, x_scales, xo, w, gate, offs, pos1,
 
         w_codes, w_scales = {}, {}
 
-        def quantize_w(c, half, calls=1, scales=None):
+        def quantize_w(c, half, calls=1):
             w_codes[c, half] = sbuf.tile([P, 2 * HALF], U32, name=f"w_codes{c}_{half}", align_bytes=64)
-            if scales is None:
-                scales = sbuf.tile([P, 2 * HALF], U8, name=f"w_scales{c}_{half}", align_bytes=64)
-            w_scales[c, half] = scales
+            w_scales[c, half] = sbuf.tile([P, 2 * HALF], U8, name=f"w_scales{c}_{half}", align_bytes=64)
             width = 2 * HALF // calls
             for m0 in range(0, 2 * HALF, width):
                 nc.vector.quantize_mx(
@@ -177,21 +169,21 @@ def tile_moe_loc_lin_silu_kernel(tc, x_words, x_scales, xo, w, gate, offs, pos1,
             slots = slice(c * CHUNK, (c + 1) * CHUNK)
             nc.vector.quantize_mx(out=own_codes[:, slots].bitcast(FP8X4), scales=own_scales[:, slots], in_=grouped[c][:])
             quantize_w(c, 0, calls=2 if c == CHUNKS - 1 else 1)
-        quantize_w(0, 1, scales=behind_last_raw("w_scales0_1", 0))
-        quantize_w(1, 1, scales=behind_last_raw("w_scales1_1", 1))
-        gather_far_scales([1], behind_last_raw("far_scales1", 2))
+            if c < WHOLE // 2:
+                quantize_w(c, 1)
+        gather_far_scales([1], behind("far_scales1", CHUNK, U8, "w_raw4_0"))
+        gather_far_scales([2, 3], behind("far_scales2", 2 * CHUNK, U8, f"w_raw{E - 1}_0"))
 
         def experts(c, nt, codes, scales, dest):
             bank = psum.tile([P, CHUNK], F32, name="bank", bufs=CHUNKS)
             half, row0 = divmod(nt * P, HALF)
             for u in range(2):
-                e = 2 * c + u
                 rows = slice(u * HALF + row0, u * HALF + row0 + P)
                 nc.tensor.matmul_mx(
                     out=bank[:, u * C : (u + 1) * C],
                     lhsT=w_codes[c, half][:, rows].bitcast(FP8X4),
                     lhsT_scale=w_scales[c, half][:, rows],
-                    rhs=codes[:, e * C : (e + 1) * C].bitcast(FP8X4),
+                    rhs=codes[:, u * C : (u + 1) * C].bitcast(FP8X4),
                     rhs_scale=scales[:, u * C : (u + 1) * C],
                     start=True,
                     stop=True,
@@ -201,20 +193,19 @@ def tile_moe_loc_lin_silu_kernel(tc, x_words, x_scales, xo, w, gate, offs, pos1,
         y = {}
 
         def own_tile(nt, tag, chunks=range(CHUNKS)):
-            if nt == 0:
-                y[nt] = shared.tile([P, S], F32, name="y0", align_bytes=64, offset=0)
-            elif nt not in y:
+            if nt not in y:
                 y[nt] = behind(f"y{nt}", S, F32, tag)
             for c in chunks:
-                experts(c, nt, own_codes, own_scales[:, c * CHUNK : (c + 1) * CHUNK], y[nt][:, c * CHUNK : (c + 1) * CHUNK])
+                slots = slice(c * CHUNK, (c + 1) * CHUNK)
+                experts(c, nt, own_codes[:, slots], own_scales[:, slots], y[nt][:, slots])
 
-        z_tags = ["w_raw2_0", "w_grouped0_1", "pairs1", "w_grouped1_1", "w_raw4_0", "xo_raw1", "w_raw5_0", "w_raw6_0"]
+        z_tags = ["xo_raw0_0", "w_grouped0_1", "pairs1", "w_grouped1_1", "w_grouped2_1", "xo_raw1_0", "w_raw5_0", "w_grouped3_1"]
 
         def far_part(nt, part):
             z = sbuf.tile([P, 2 * CHUNK], F32, name=f"z{nt}{part}", tag=z_tags[2 * nt + part], align_bytes=64)
             for u in range(2):
                 c = 2 * part + u
-                experts(c, nt, far_codes, far_scales[c], z[:, u * CHUNK : (u + 1) * CHUNK])
+                experts(c, nt, far_codes[c], far_scales[c], z[:, u * CHUNK : (u + 1) * CHUNK])
             s0 = T + 2 * part * CHUNK
             nc.sync.dma_start(out[nt * P : (nt + 1) * P, s0 : s0 + 2 * CHUNK], z[:])
 
@@ -242,35 +233,31 @@ def tile_moe_loc_lin_silu_kernel(tc, x_words, x_scales, xo, w, gate, offs, pos1,
             nc.vector.tensor_tensor(total[:], products[step, 0, 0], products[step, 1, 0], ADD)
             nc.sync.dma_start(out[nt * P : (nt + 1) * P, t0 : t0 + width], total[:])
 
-        own_tile(0, None)
+        own_tile(0, "w_raw6_0")
         first_products = [kept(f"kept0_{r}", T, f"w_grouped{r}_0") for r in range(2)]
         for r in range(2):
             weigh(0, r, first_products[r][:])
-        first_sum = sbuf.tile([P, T], F32, name="first_sum", tag="xo_raw0", align_bytes=64)
-        nc.gpsimd.tensor_tensor(first_sum[:], first_products[0][:], first_products[1][:], ADD)
-        nc.sync.dma_start(out[0:P, 0:T], first_sum[:])
         own_tile(1, "w_raw0_0")
+        weigh(1, 0, kept("kept1_0", T, "w_grouped2_0")[:])
         far_part(0, 0)
         for e in range(WHOLE, E):
             round_w(e, 1)
-        gather_far_scales(range(2, CHUNKS), behind("far_scales2", 2 * CHUNK, U8, f"w_raw4_{HALF}"))
-        quantize_w(2, 1)
-        weigh(1, 0, kept("kept1_early", CHUNK, f"w_raw5_{HALF}")[:])
         quantize_w(3, 1)
-        late_products = kept("kept1_late", 3 * CHUNK, f"w_raw7_{HALF}")
-        weigh(1, 0, late_products[:, 0:CHUNK], CHUNK)
-        weigh(1, 1, late_products[:, CHUNK:])
+        after_casts = kept("after_casts", 2 * T, f"w_raw7_{HALF}")
+        nc.vector.tensor_tensor(after_casts[:, 0:T], first_products[0][:], first_products[1][:], ADD)
+        nc.sync.dma_start(out[0:P, 0:T], after_casts[:, 0:T])
+        weigh(1, 1, after_casts[:, T:])
         far_part(1, 0)
-        own_tile(2, f"w_raw6_{HALF}", range(2))
+        own_tile(2, "w_raw2_0", range(3))
         far_part(0, 1)
-        own_tile(2, None, range(2, CHUNKS))
+        own_tile(2, None, range(3, CHUNKS))
         far_part(1, 1)
+        far_part(2, 0)
         own_tile(3, "w_raw1_0")
-        for nt in range(2, ROW_TILES):
-            for part in range(2):
-                far_part(nt, part)
-        weigh(2, 0, kept("kept2_0", T, "w_grouped2_0")[:])
-        weigh(2, 1, kept("kept2_1", T, "w_raw3_0")[:])
+        last_kept = [kept("kept2_0", T, "w_grouped3_0"), kept("kept2_1", T, "w_raw3_0")]
+        for b0 in range(0, T, CHUNK):
+            for r in range(2):
+                weigh(2, r, last_kept[r][:, b0 : b0 + CHUNK], b0)
 
         spans = [(step, b0) for step in TENSOR_STEPS for b0 in range(0, STEPS[step][2], CHUNK)]
         turned = {}
@@ -302,11 +289,16 @@ def tile_moe_loc_lin_silu_kernel(tc, x_words, x_scales, xo, w, gate, offs, pos1,
             nc.scalar.copy(summed[:], bank[:])
             nc.sync.dma_start(out[nt * P : (nt + 1) * P, t0 + b0 : t0 + b0 + CHUNK], summed[:])
 
-        for index in range(len(spans) + TURN_LAG):
-            if index < len(spans):
-                turn(index)
-            if index >= TURN_LAG:
-                turn_back(index - TURN_LAG)
+        turn(0)
+        turn(1)
+        far_part(2, 1)
+        turn_back(0)
+        turn(2)
+        far_part(3, 0)
+        turn(3)
+        far_part(3, 1)
+        for index in range(1, len(spans)):
+            turn_back(index)
 
         for step in range(FIRST_VECTOR_STEP, len(STEPS)):
             weigh(step, 0, sbuf.tile([P, STEPS[step][2]], F32, name="product0", bufs=2)[:])

@@ -25,12 +25,11 @@ CHUNK = 512
 CHUNKS = S // CHUNK
 HALF = N // 2
 
-WHOLE = 6
+WHOLE = 4
 XO_PIECES = [(0, 0, T), (1, 0, T)]
 STEPS = [(0, 0, 1024), (1, 0, 1024), (2, 0, 1024), (3, 0, 512), (3, 512, 256), (3, 768, 256)]
 TENSOR_STEPS = (1, 2)
 FIRST_VECTOR_STEP = 3
-PIECES = [(0, 512), (512, 512), (1024, 512), (1536, 256), (1792, 256)]
 TURN_LAG = 2
 
 
@@ -55,8 +54,6 @@ def tile_moe_loc_lin_silu_kernel(tc, x_words, x_scales, xo, w, gate, offs, pos1,
         nc.vector.memset(token_scales[:], 0)
         nc.sync.dma_start(offs2_t[:], offs2)
         nc.sync.dma_start(token_words[:], x_words[0].rearrange("p t d -> p (t d)").bitcast(I32))
-        for q in range(4):
-            nc.sync.dma_start(token_scales[32 * q : 32 * q + 4, :], x_scales[0, 4 * q : 4 * q + 4, :].bitcast(I32))
 
         warm = sbuf.tile([P, 16], F32, name="warm")
         nc.vector.memset(warm[:, 0:8], 0.0)
@@ -74,6 +71,8 @@ def tile_moe_loc_lin_silu_kernel(tc, x_words, x_scales, xo, w, gate, offs, pos1,
         load_xo(XO_PIECES[0])
         nc.sync.dma_start(offs_t[:], offs)
         load_xo(XO_PIECES[1])
+        for q in range(4):
+            nc.sync.dma_start(token_scales[32 * q : 32 * q + 4, :], x_scales[0, 4 * q : 4 * q + 4, :].bitcast(I32))
 
         def load_w(piece):
             e, n0, width = piece
@@ -113,28 +112,35 @@ def tile_moe_loc_lin_silu_kernel(tc, x_words, x_scales, xo, w, gate, offs, pos1,
         def gather_far_words(chunks, gathered):
             gather_far(chunks, gathered, token_words[:].bitcast(U32), far_codes)
 
-        gather_far_words(range(3), sbuf.tile([P, 3 * CHUNK], U32, name="far_codes0", align_bytes=64))
-        gather_far_scales([0], sbuf.tile([P, CHUNK], U8, name="far_scales0", align_bytes=64))
+        gather_far_words(range(CHUNKS), sbuf.tile([P, S], U32, name="far_codes", align_bytes=64))
 
         two_chunks = [
             sbuf.tile([P, 4 * CHUNK], I32, name="picked0", align_bytes=64),
             sbuf.tile([P, 4 * CHUNK], I32, name="picked1", tag="xo_raw1_0", align_bytes=64),
         ]
-        grouped = [sbuf.tile([P, 4 * CHUNK], BF16, name=f"grouped{c}", align_bytes=64) for c in range(CHUNKS)]
-        for s0, count in PIECES:
-            c, place = divmod(s0, CHUNK)
-            first = 2 * (s0 % (2 * CHUNK))
-            picked = two_chunks[c // 2][:, first : first + 2 * count]
+        picked = [two_chunks[c // 2][:, c % 2 * 2 * CHUNK : (c % 2 + 1) * 2 * CHUNK] for c in range(CHUNKS)]
+        grouped = {}
+
+        def gather_own(c):
             for a in range(2):
                 nc.vector.tensor_copy(
-                    picked[:, a * count : (a + 1) * count].bitcast(U32), pairs[a][:].bitcast(U32).indirect(list_columns(offs_t, s0, count))
+                    picked[c][:, a * CHUNK : (a + 1) * CHUNK].bitcast(U32),
+                    pairs[a][:].bitcast(U32).indirect(list_columns(offs_t, c * CHUNK, CHUNK)),
                 )
-            nc.gpsimd.tensor_copy(
-                grouped[c][:, 4 * place : 4 * (place + count)].bitcast(I32).rearrange("p (s a) -> p s a", a=2),
-                picked.rearrange("p (a s) -> p s a", a=2),
+
+        def weave(c, copy, dtype, tag):
+            grouped[c] = behind(f"grouped{c}", 4 * CHUNK, BF16, tag)
+            copy(
+                grouped[c][:].bitcast(dtype).rearrange("p (s a) -> p s a", a=2),
+                picked[c].bitcast(dtype).rearrange("p (a s) -> p s a", a=2),
             )
 
-        gather_far_words([3], behind("far_codes3", CHUNK, U32, "pairs0"))
+        gather_own(0)
+        gather_own(1)
+        for c in range(1, CHUNKS):
+            if c + 1 < CHUNKS:
+                gather_own(c + 1)
+            weave(c, nc.vector.tensor_copy, I32, f"grouped{c}")
 
         w_grouped = {}
 
@@ -151,12 +157,16 @@ def tile_moe_loc_lin_silu_kernel(tc, x_words, x_scales, xo, w, gate, offs, pos1,
         for e in range(E):
             for half in range(2 if e < WHOLE else 1):
                 round_w(e, half)
+            if e == 0:
+                weave(0, nc.scalar.copy, U32, "w_raw0_0")
 
         w_codes, w_scales = {}, {}
 
-        def quantize_w(c, half, calls=1):
+        def quantize_w(c, half, calls=1, scales=None):
             w_codes[c, half] = sbuf.tile([P, 2 * HALF], U32, name=f"w_codes{c}_{half}", align_bytes=64)
-            w_scales[c, half] = sbuf.tile([P, 2 * HALF], U8, name=f"w_scales{c}_{half}", align_bytes=64)
+            if scales is None:
+                scales = sbuf.tile([P, 2 * HALF], U8, name=f"w_scales{c}_{half}", align_bytes=64)[:]
+            w_scales[c, half] = scales
             width = 2 * HALF // calls
             for m0 in range(0, 2 * HALF, width):
                 nc.vector.quantize_mx(
@@ -169,10 +179,12 @@ def tile_moe_loc_lin_silu_kernel(tc, x_words, x_scales, xo, w, gate, offs, pos1,
             slots = slice(c * CHUNK, (c + 1) * CHUNK)
             nc.vector.quantize_mx(out=own_codes[:, slots].bitcast(FP8X4), scales=own_scales[:, slots], in_=grouped[c][:])
             quantize_w(c, 0, calls=2 if c == CHUNKS - 1 else 1)
-            if c < WHOLE // 2:
-                quantize_w(c, 1)
-        gather_far_scales([1], behind("far_scales1", CHUNK, U8, "w_raw4_0"))
-        gather_far_scales([2, 3], behind("far_scales2", 2 * CHUNK, U8, f"w_raw{E - 1}_0"))
+            if c == 2:
+                gather_far_scales([0], behind("far_scales0", CHUNK, U8, "w_raw5_0"))
+        held_scales = behind("held_scales", 2 * CHUNK, U8, f"w_raw{E - 1}_0")
+        for c in range(WHOLE // 2):
+            quantize_w(c, 1, scales=held_scales[:, c * CHUNK : (c + 1) * CHUNK])
+        gather_far_scales([1], behind("far_scales1", CHUNK, U8, "w_grouped0_1"))
 
         def experts(c, nt, codes, scales, dest):
             bank = psum.tile([P, CHUNK], F32, name="bank", bufs=CHUNKS)
@@ -199,7 +211,7 @@ def tile_moe_loc_lin_silu_kernel(tc, x_words, x_scales, xo, w, gate, offs, pos1,
                 slots = slice(c * CHUNK, (c + 1) * CHUNK)
                 experts(c, nt, own_codes[:, slots], own_scales[:, slots], y[nt][:, slots])
 
-        z_tags = ["xo_raw0_0", "w_grouped0_1", "pairs1", "w_grouped1_1", "w_grouped2_1", "xo_raw1_0", "w_raw5_0", "w_grouped3_1"]
+        z_tags = ["pairs0", "w_raw4_256", "pairs1", "w_grouped1_1", "w_grouped2_1", "xo_raw1_0", "w_raw4_0", "w_grouped3_1"]
 
         def far_part(nt, part):
             z = sbuf.tile([P, 2 * CHUNK], F32, name=f"z{nt}{part}", tag=z_tags[2 * nt + part], align_bytes=64)
@@ -237,24 +249,27 @@ def tile_moe_loc_lin_silu_kernel(tc, x_words, x_scales, xo, w, gate, offs, pos1,
         first_products = [kept(f"kept0_{r}", T, f"w_grouped{r}_0") for r in range(2)]
         for r in range(2):
             weigh(0, r, first_products[r][:])
-        own_tile(1, "w_raw0_0")
-        weigh(1, 0, kept("kept1_0", T, "w_grouped2_0")[:])
+        gather_far_scales([2, 3], behind("far_scales2", 2 * CHUNK, U8, "w_raw6_0"))
+        first_sum = kept("first_sum", T, "xo_raw0_0")
+        nc.gpsimd.tensor_tensor(first_sum[:], first_products[0][:], first_products[1][:], ADD)
+        nc.sync.dma_start(out[0:P, 0:T], first_sum[:])
+        own_tile(1, "w_raw2_0")
         far_part(0, 0)
         for e in range(WHOLE, E):
             round_w(e, 1)
+        quantize_w(2, 1)
         quantize_w(3, 1)
         after_casts = kept("after_casts", 2 * T, f"w_raw7_{HALF}")
-        nc.vector.tensor_tensor(after_casts[:, 0:T], first_products[0][:], first_products[1][:], ADD)
-        nc.sync.dma_start(out[0:P, 0:T], after_casts[:, 0:T])
-        weigh(1, 1, after_casts[:, T:])
+        for r in range(2):
+            weigh(1, r, after_casts[:, r * T : (r + 1) * T])
         far_part(1, 0)
-        own_tile(2, "w_raw2_0", range(3))
+        own_tile(2, "w_raw3_0", range(2))
         far_part(0, 1)
-        own_tile(2, None, range(3, CHUNKS))
+        own_tile(2, None, range(2, CHUNKS))
         far_part(1, 1)
         far_part(2, 0)
         own_tile(3, "w_raw1_0")
-        last_kept = [kept("kept2_0", T, "w_grouped3_0"), kept("kept2_1", T, "w_raw3_0")]
+        last_kept = [kept("kept2_0", T, "w_grouped3_0"), kept("kept2_1", T, "w_grouped2_0")]
         for b0 in range(0, T, CHUNK):
             for r in range(2):
                 weigh(2, r, last_kept[r][:, b0 : b0 + CHUNK], b0)
@@ -276,7 +291,7 @@ def tile_moe_loc_lin_silu_kernel(tc, x_words, x_scales, xo, w, gate, offs, pos1,
                         stop=r == 1,
                         is_transpose=True,
                     )
-            turned[index] = sbuf.tile([P, CHUNK], F32, name=f"turned{index}", tag=f"grouped{index}", align_bytes=64)
+            turned[index] = sbuf.tile([P, CHUNK], F32, name=f"turned{index}", tag=f"turned{index}" if index == 0 else f"grouped{index}", align_bytes=64)
             nc.scalar.copy(turned[index][:], bank[:])
 
         def turn_back(index):

@@ -25,8 +25,8 @@ CHUNK = 512
 CHUNKS = S // CHUNK
 HALF = N // 2
 
-WHOLE = 4
-XO_PIECES = [(0, 0, T), (1, 0, T)]
+WHOLE = 3
+XO_PIECES = [(a, t0, T // 2) for a in range(2) for t0 in (0, T // 2)]
 STEPS = [(0, 0, 1024), (1, 0, 1024), (2, 0, 1024), (3, 0, 512), (3, 512, 256), (3, 768, 256)]
 TENSOR_STEPS = (1, 2)
 FIRST_VECTOR_STEP = 3
@@ -69,8 +69,10 @@ def tile_moe_loc_lin_silu_kernel(tc, x_words, x_scales, xo, w, gate, offs, pos1,
             nc.sync.dma_start(xo_raw[a, t0][:], xo_rows[:, 2 * a : 2 * a + 2, t0 : t0 + width])
 
         load_xo(XO_PIECES[0])
-        nc.sync.dma_start(offs_t[:], offs)
         load_xo(XO_PIECES[1])
+        nc.sync.dma_start(offs_t[:], offs)
+        load_xo(XO_PIECES[2])
+        load_xo(XO_PIECES[3])
         for q in range(4):
             nc.sync.dma_start(token_scales[32 * q : 32 * q + 4, :], x_scales[0, 4 * q : 4 * q + 4, :].bitcast(I32))
 
@@ -116,7 +118,7 @@ def tile_moe_loc_lin_silu_kernel(tc, x_words, x_scales, xo, w, gate, offs, pos1,
 
         two_chunks = [
             sbuf.tile([P, 4 * CHUNK], I32, name="picked0", align_bytes=64),
-            sbuf.tile([P, 4 * CHUNK], I32, name="picked1", tag="xo_raw1_0", align_bytes=64),
+            sbuf.tile([P, 4 * CHUNK], I32, name="picked1", tag="xo_raw1_512", align_bytes=64),
         ]
         picked = [two_chunks[c // 2][:, c % 2 * 2 * CHUNK : (c % 2 + 1) * 2 * CHUNK] for c in range(CHUNKS)]
         grouped = {}
@@ -135,12 +137,11 @@ def tile_moe_loc_lin_silu_kernel(tc, x_words, x_scales, xo, w, gate, offs, pos1,
                 picked[c].bitcast(dtype).rearrange("p (a s) -> p s a", a=2),
             )
 
-        gather_own(0)
-        gather_own(1)
-        for c in range(1, CHUNKS):
-            if c + 1 < CHUNKS:
-                gather_own(c + 1)
-            weave(c, nc.vector.tensor_copy, I32, f"grouped{c}")
+        for c in range(CHUNKS):
+            gather_own(c)
+            if c < CHUNKS - 1:
+                weave(c, nc.gpsimd.tensor_copy, I32, f"grouped{c}")
+        gather_far_scales([0], behind("far_scales0", CHUNK, U8, "pairs0"))
 
         w_grouped = {}
 
@@ -157,33 +158,35 @@ def tile_moe_loc_lin_silu_kernel(tc, x_words, x_scales, xo, w, gate, offs, pos1,
         for e in range(E):
             for half in range(2 if e < WHOLE else 1):
                 round_w(e, half)
-            if e == 0:
-                weave(0, nc.scalar.copy, U32, "w_raw0_0")
+            if e == WHOLE:
+                weave(CHUNKS - 1, nc.scalar.copy, U32, f"w_raw{WHOLE}_0")
 
         w_codes, w_scales = {}, {}
 
-        def quantize_w(c, half, calls=1, scales=None):
-            w_codes[c, half] = sbuf.tile([P, 2 * HALF], U32, name=f"w_codes{c}_{half}", align_bytes=64)
-            if scales is None:
-                scales = sbuf.tile([P, 2 * HALF], U8, name=f"w_scales{c}_{half}", align_bytes=64)[:]
-            w_scales[c, half] = scales
-            width = 2 * HALF // calls
-            for m0 in range(0, 2 * HALF, width):
-                nc.vector.quantize_mx(
-                    out=w_codes[c, half][:, m0 : m0 + width].bitcast(FP8X4),
-                    scales=w_scales[c, half][:, m0 : m0 + width],
-                    in_=w_grouped[c, half][:, 4 * m0 : 4 * (m0 + width)],
-                )
+        def quantize_w(first, count, half, scales=None):
+            c, u = divmod(first, 2)
+            if (c, half) not in w_codes:
+                w_codes[c, half] = sbuf.tile([P, 2 * HALF], U32, name=f"w_codes{c}_{half}", align_bytes=64)
+                if scales is None:
+                    scales = sbuf.tile([P, 2 * HALF], U8, name=f"w_scales{c}_{half}", align_bytes=64)[:]
+                w_scales[c, half] = scales
+            cols = slice(u * HALF, (u + count) * HALF)
+            nc.vector.quantize_mx(
+                out=w_codes[c, half][:, cols].bitcast(FP8X4),
+                scales=w_scales[c, half][:, cols],
+                in_=w_grouped[c, half][:, 4 * u * HALF : 4 * (u + count) * HALF],
+            )
 
         for c in range(CHUNKS):
             slots = slice(c * CHUNK, (c + 1) * CHUNK)
             nc.vector.quantize_mx(out=own_codes[:, slots].bitcast(FP8X4), scales=own_scales[:, slots], in_=grouped[c][:])
-            quantize_w(c, 0, calls=2 if c == CHUNKS - 1 else 1)
-            if c == 2:
-                gather_far_scales([0], behind("far_scales0", CHUNK, U8, "w_raw5_0"))
+            if c < CHUNKS - 1:
+                quantize_w(2 * c, 2, 0)
+        quantize_w(E - 2, 1, 0)
+        quantize_w(E - 1, 1, 0)
         held_scales = behind("held_scales", 2 * CHUNK, U8, f"w_raw{E - 1}_0")
-        for c in range(WHOLE // 2):
-            quantize_w(c, 1, scales=held_scales[:, c * CHUNK : (c + 1) * CHUNK])
+        quantize_w(0, 2, 1, held_scales[:, 0:CHUNK])
+        quantize_w(2, 1, 1, held_scales[:, CHUNK:])
         gather_far_scales([1], behind("far_scales1", CHUNK, U8, "w_grouped0_1"))
 
         def experts(c, nt, codes, scales, dest):
@@ -211,7 +214,7 @@ def tile_moe_loc_lin_silu_kernel(tc, x_words, x_scales, xo, w, gate, offs, pos1,
                 slots = slice(c * CHUNK, (c + 1) * CHUNK)
                 experts(c, nt, own_codes[:, slots], own_scales[:, slots], y[nt][:, slots])
 
-        z_tags = ["pairs0", "w_raw4_256", "pairs1", "w_grouped1_1", "w_grouped2_1", "xo_raw1_0", "w_raw4_0", "w_grouped3_1"]
+        z_tags = ["xo_raw0_512", "w_raw4_256", "pairs1", "xo_raw1_0", "w_grouped2_1", "xo_raw1_512", "w_raw4_0", "w_grouped3_1"]
 
         def far_part(nt, part):
             z = sbuf.tile([P, 2 * CHUNK], F32, name=f"z{nt}{part}", tag=z_tags[2 * nt + part], align_bytes=64)
@@ -240,7 +243,7 @@ def tile_moe_loc_lin_silu_kernel(tc, x_words, x_scales, xo, w, gate, offs, pos1,
 
         def add_and_store(step):
             nt, t0, width = STEPS[step]
-            tag = f"grouped{step - FIRST_VECTOR_STEP + 1}"
+            tag = f"grouped{(0, 2, 3)[step - FIRST_VECTOR_STEP]}"
             total = sbuf.tile([P, width], F32, name=f"total{step}", tag=tag, align_bytes=64)
             nc.vector.tensor_tensor(total[:], products[step, 0, 0], products[step, 1, 0], ADD)
             nc.sync.dma_start(out[nt * P : (nt + 1) * P, t0 : t0 + width], total[:])
@@ -257,13 +260,13 @@ def tile_moe_loc_lin_silu_kernel(tc, x_words, x_scales, xo, w, gate, offs, pos1,
         far_part(0, 0)
         for e in range(WHOLE, E):
             round_w(e, 1)
-        quantize_w(2, 1)
-        quantize_w(3, 1)
-        after_casts = kept("after_casts", 2 * T, f"w_raw7_{HALF}")
-        for r in range(2):
-            weigh(1, r, after_casts[:, r * T : (r + 1) * T])
+        quantize_w(3, 1, 1)
+        quantize_w(4, 2, 1)
+        weigh(1, 0, kept("kept1_0", T, f"w_raw5_{HALF}")[:])
+        quantize_w(6, 2, 1)
+        weigh(1, 1, kept("kept1_1", T, f"w_raw7_{HALF}")[:])
         far_part(1, 0)
-        own_tile(2, "w_raw3_0", range(2))
+        own_tile(2, "w_raw0_0", range(2))
         far_part(0, 1)
         own_tile(2, None, range(2, CHUNKS))
         far_part(1, 1)
@@ -291,7 +294,7 @@ def tile_moe_loc_lin_silu_kernel(tc, x_words, x_scales, xo, w, gate, offs, pos1,
                         stop=r == 1,
                         is_transpose=True,
                     )
-            turned[index] = sbuf.tile([P, CHUNK], F32, name=f"turned{index}", tag=f"turned{index}" if index == 0 else f"grouped{index}", align_bytes=64)
+            turned[index] = sbuf.tile([P, CHUNK], F32, name=f"turned{index}", tag=f"grouped{index}", align_bytes=64)
             nc.scalar.copy(turned[index][:], bank[:])
 
         def turn_back(index):
@@ -304,14 +307,14 @@ def tile_moe_loc_lin_silu_kernel(tc, x_words, x_scales, xo, w, gate, offs, pos1,
             nc.scalar.copy(summed[:], bank[:])
             nc.sync.dma_start(out[nt * P : (nt + 1) * P, t0 + b0 : t0 + b0 + CHUNK], summed[:])
 
+        far_part(2, 1)
+        far_part(3, 0)
         turn(0)
         turn(1)
-        far_part(2, 1)
-        turn_back(0)
-        turn(2)
-        far_part(3, 0)
-        turn(3)
         far_part(3, 1)
+        turn(2)
+        turn_back(0)
+        turn(3)
         for index in range(1, len(spans)):
             turn_back(index)
 

@@ -19,18 +19,13 @@ ADD = mybir.AluOpType.add
 SILU = mybir.ActivationFunctionType.Silu
 
 P = 128
-ROW_TILES = N // P
 PER_COLUMN = 16
 CHUNK = 512
 CHUNKS = S // CHUNK
 HALF = N // 2
 
 WHOLE = 3
-XO_PIECES = [(a, t0, T // 2) for a in range(2) for t0 in (0, T // 2)]
-STEPS = [(0, 0, 1024), (1, 0, 1024), (2, 0, 1024), (3, 0, 512), (3, 512, 256), (3, 768, 256)]
-TENSOR_STEPS = (1, 2)
-FIRST_VECTOR_STEP = 3
-TURN_LAG = 2
+LAST_STEPS = [(0, 512), (512, 256), (768, 256)]
 
 
 def list_columns(list_tile, first, count):
@@ -43,13 +38,16 @@ def tile_moe_loc_lin_silu_kernel(tc, x_words, x_scales, xo, w, gate, offs, pos1,
         sbuf = ctx.enter_context(tc.tile_pool(name="sbuf", bufs=1))
         psum = ctx.enter_context(tc.psum_pool(name="psum", bufs=1))
 
+        def behind(name, width, dtype, tag):
+            return sbuf.tile([P, width], dtype, name=name, tag=tag, align_bytes=64)
+
         offs2_t = sbuf.tile([P, S // PER_COLUMN], U16, name="offs2_t")
         offs_t = sbuf.tile([P, S // PER_COLUMN], U16, name="offs_t")
         pos_t = [sbuf.tile([P, T // PER_COLUMN], U16, name=f"pos_t{r}") for r in range(2)]
         gate_t = [sbuf.tile([P, T], F32, name=f"gate_t{r}") for r in range(2)]
         token_words = sbuf.tile([P, Q], I32, name="token_words")
         token_scales = sbuf.tile([P, Q // 4], I32, name="token_scales", align_bytes=64)
-        xo_raw = {(a, t0): sbuf.tile([P, 2, width], F32, name=f"xo_raw{a}_{t0}", align_bytes=64) for a, t0, width in XO_PIECES}
+        xo_raw = [sbuf.tile([P, 2, T], F32, name=f"xo_raw{a}", align_bytes=64) for a in range(2)]
 
         nc.vector.memset(token_scales[:], 0)
         nc.sync.dma_start(offs2_t[:], offs2)
@@ -59,67 +57,51 @@ def tile_moe_loc_lin_silu_kernel(tc, x_words, x_scales, xo, w, gate, offs, pos1,
         nc.vector.memset(warm[:, 0:8], 0.0)
         nc.scalar.activation(warm[:, 8:16], warm[:, 0:8], SILU)
 
-        pieces = [(e, 0, N) for e in range(WHOLE)] + [(e, n0, HALF) for n0 in (0, HALF) for e in range(WHOLE, E)]
-        w_raw = {}
-
         xo_rows = xo.rearrange("(p j) t -> p j t", j=4)
-
-        def load_xo(piece):
-            a, t0, width = piece
-            nc.sync.dma_start(xo_raw[a, t0][:], xo_rows[:, 2 * a : 2 * a + 2, t0 : t0 + width])
-
-        load_xo(XO_PIECES[0])
-        load_xo(XO_PIECES[1])
+        nc.sync.dma_start(xo_raw[0][:], xo_rows[:, 0:2, :])
         nc.sync.dma_start(offs_t[:], offs)
-        load_xo(XO_PIECES[2])
-        load_xo(XO_PIECES[3])
+        nc.sync.dma_start(xo_raw[1][:], xo_rows[:, 2:4, :])
         for q in range(4):
             nc.sync.dma_start(token_scales[32 * q : 32 * q + 4, :], x_scales[0, 4 * q : 4 * q + 4, :].bitcast(I32))
 
-        def load_w(piece):
-            e, n0, width = piece
+        w_raw = {}
+
+        def load_w(e, n0, width):
             w_raw[e, n0] = sbuf.tile([P, 4, width], F32, name=f"w_raw{e}_{n0}", align_bytes=64)
             nc.sync.dma_start(w_raw[e, n0][:], w[e].rearrange("(p j) n -> p j n", j=4)[:, :, n0 : n0 + width])
 
-        for piece in pieces[:E]:
-            load_w(piece)
+        for e in range(E):
+            load_w(e, 0, N if e < WHOLE else HALF)
         for r, pos in enumerate((pos1, pos2)):
             nc.sync.dma_start(pos_t[r][:], pos)
             nc.sync.dma_start(gate_t[r][:], gate[r])
-        for piece in pieces[E:]:
-            load_w(piece)
+        for e in range(WHOLE, E):
+            load_w(e, HALF, HALF)
 
         pairs = [sbuf.tile([P, 2 * T], BF16, name=f"pairs{a}", align_bytes=64) for a in range(2)]
-        for a, t0, width in XO_PIECES:
+        for a in range(2):
             nc.scalar.copy(
-                pairs[a][:, 2 * t0 : 2 * (t0 + width)].rearrange("p (g t i) -> p g i t", t=4, i=2),
-                xo_raw[a, t0][:].rearrange("p i (g t) -> p g i t", t=4),
+                pairs[a][:].rearrange("p (g t i) -> p g i t", t=4, i=2),
+                xo_raw[a][:].rearrange("p i (g t) -> p g i t", t=4),
             )
 
         own_codes = sbuf.tile([P, S], U32, name="own_codes", align_bytes=64)
         own_scales = sbuf.tile([P, S], U8, name="own_scales", align_bytes=64)
         far_codes, far_scales = {}, {}
 
-        def behind(name, width, dtype, tag):
-            return sbuf.tile([P, width], dtype, name=name, tag=tag, align_bytes=64)
-
         def gather_far(chunks, gathered, table, found):
             for place, c in enumerate(chunks):
                 found[c] = gathered[:, place * CHUNK : (place + 1) * CHUNK]
                 nc.vector.tensor_copy(found[c], table.indirect(list_columns(offs2_t, c * CHUNK, CHUNK)))
 
-        def gather_far_scales(chunks, gathered):
+        def gather_far_scales(chunks, tag):
+            gathered = behind(f"far_scales{chunks[0]}", len(chunks) * CHUNK, U8, tag)
             gather_far(chunks, gathered, token_scales[:].bitcast(U8), far_scales)
 
-        def gather_far_words(chunks, gathered):
-            gather_far(chunks, gathered, token_words[:].bitcast(U32), far_codes)
+        far_words = sbuf.tile([P, S], U32, name="far_words", align_bytes=64)
+        gather_far(range(CHUNKS), far_words, token_words[:].bitcast(U32), far_codes)
 
-        gather_far_words(range(CHUNKS), sbuf.tile([P, S], U32, name="far_codes", align_bytes=64))
-
-        two_chunks = [
-            sbuf.tile([P, 4 * CHUNK], I32, name="picked0", align_bytes=64),
-            sbuf.tile([P, 4 * CHUNK], I32, name="picked1", tag="xo_raw1_512", align_bytes=64),
-        ]
+        two_chunks = [behind("picked0", 4 * CHUNK, I32, "picked0"), behind("picked1", 4 * CHUNK, I32, "xo_raw1")]
         picked = [two_chunks[c // 2][:, c % 2 * 2 * CHUNK : (c % 2 + 1) * 2 * CHUNK] for c in range(CHUNKS)]
         grouped = {}
 
@@ -130,18 +112,19 @@ def tile_moe_loc_lin_silu_kernel(tc, x_words, x_scales, xo, w, gate, offs, pos1,
                     pairs[a][:].bitcast(U32).indirect(list_columns(offs_t, c * CHUNK, CHUNK)),
                 )
 
-        def weave(c, copy, dtype, tag):
-            grouped[c] = behind(f"grouped{c}", 4 * CHUNK, BF16, tag)
+        def weave(c, copy, dtype, first, count):
             copy(
-                grouped[c][:].bitcast(dtype).rearrange("p (s a) -> p s a", a=2),
-                picked[c].bitcast(dtype).rearrange("p (a s) -> p s a", a=2),
+                grouped[c][:].bitcast(dtype).rearrange("p (s a) -> p s a", a=2)[:, first : first + count, :],
+                picked[c].bitcast(dtype).rearrange("p (a s) -> p s a", a=2)[:, first : first + count, :],
             )
 
         for c in range(CHUNKS):
             gather_own(c)
             if c < CHUNKS - 1:
-                weave(c, nc.gpsimd.tensor_copy, I32, f"grouped{c}")
-        gather_far_scales([0], behind("far_scales0", CHUNK, U8, "pairs0"))
+                grouped[c] = behind(f"grouped{c}", 4 * CHUNK, BF16, f"grouped{c}")
+                weave(c, nc.gpsimd.tensor_copy, I32, 0, CHUNK if c < 2 else CHUNK // 2)
+        gather_far_scales([0], "pairs0")
+        weave(2, nc.vector.tensor_copy, I32, CHUNK // 2, CHUNK // 2)
 
         w_grouped = {}
 
@@ -159,13 +142,14 @@ def tile_moe_loc_lin_silu_kernel(tc, x_words, x_scales, xo, w, gate, offs, pos1,
             for half in range(2 if e < WHOLE else 1):
                 round_w(e, half)
             if e == WHOLE:
-                weave(CHUNKS - 1, nc.scalar.copy, U32, f"w_raw{WHOLE}_0")
+                grouped[CHUNKS - 1] = behind(f"grouped{CHUNKS - 1}", 4 * CHUNK, BF16, f"w_raw{e}_0")
+                weave(CHUNKS - 1, nc.scalar.copy, U32, 0, CHUNK)
 
         w_codes, w_scales = {}, {}
 
         def quantize_w(first, count, half, scales=None):
             c, u = divmod(first, 2)
-            if (c, half) not in w_codes:
+            if u == 0:
                 w_codes[c, half] = sbuf.tile([P, 2 * HALF], U32, name=f"w_codes{c}_{half}", align_bytes=64)
                 if scales is None:
                     scales = sbuf.tile([P, 2 * HALF], U8, name=f"w_scales{c}_{half}", align_bytes=64)[:]
@@ -187,7 +171,7 @@ def tile_moe_loc_lin_silu_kernel(tc, x_words, x_scales, xo, w, gate, offs, pos1,
         held_scales = behind("held_scales", 2 * CHUNK, U8, f"w_raw{E - 1}_0")
         quantize_w(0, 2, 1, held_scales[:, 0:CHUNK])
         quantize_w(2, 1, 1, held_scales[:, CHUNK:])
-        gather_far_scales([1], behind("far_scales1", CHUNK, U8, "w_grouped0_1"))
+        gather_far_scales([1], "w_grouped0_1")
 
         def experts(c, nt, codes, scales, dest):
             bank = psum.tile([P, CHUNK], F32, name="bank", bufs=CHUNKS)
@@ -207,17 +191,13 @@ def tile_moe_loc_lin_silu_kernel(tc, x_words, x_scales, xo, w, gate, offs, pos1,
 
         y = {}
 
-        def own_tile(nt, tag, chunks=range(CHUNKS)):
-            if nt not in y:
-                y[nt] = behind(f"y{nt}", S, F32, tag)
+        def own_chunks(nt, chunks):
             for c in chunks:
                 slots = slice(c * CHUNK, (c + 1) * CHUNK)
                 experts(c, nt, own_codes[:, slots], own_scales[:, slots], y[nt][:, slots])
 
-        z_tags = ["xo_raw0_512", "w_raw4_256", "pairs1", "xo_raw1_0", "w_grouped2_1", "xo_raw1_512", "w_raw4_0", "w_grouped3_1"]
-
-        def far_part(nt, part):
-            z = sbuf.tile([P, 2 * CHUNK], F32, name=f"z{nt}{part}", tag=z_tags[2 * nt + part], align_bytes=64)
+        def far_part(nt, part, tag):
+            z = behind(f"z{nt}{part}", 2 * CHUNK, F32, tag)
             for u in range(2):
                 c = 2 * part + u
                 experts(c, nt, far_codes[c], far_scales[c], z[:, u * CHUNK : (u + 1) * CHUNK])
@@ -226,101 +206,111 @@ def tile_moe_loc_lin_silu_kernel(tc, x_words, x_scales, xo, w, gate, offs, pos1,
 
         identity = sbuf.tile([P, P], F32, name="identity")
         make_identity(nc, identity[:])
-        products = {}
 
-        def weigh(step, r, product, first=0):
-            nt, t0 = STEPS[step][:2]
-            width = product.shape[1]
-            for b0 in range(0, width, CHUNK):
-                products[step, r, first + b0] = product[:, b0 : min(b0 + CHUNK, width)]
-            t0 = t0 + first
+        def weigh(product, nt, r, t0, width):
             nc.vector.tensor_tensor(
                 product, y[nt][:].indirect(list_columns(pos_t[r], t0, width)), gate_t[r][:, t0 : t0 + width], MULT
             )
 
-        def kept(name, width, tag):
-            return behind(name, width, F32, tag)
-
-        def add_and_store(step):
-            nt, t0, width = STEPS[step]
-            tag = f"grouped{(0, 2, 3)[step - FIRST_VECTOR_STEP]}"
-            total = sbuf.tile([P, width], F32, name=f"total{step}", tag=tag, align_bytes=64)
-            nc.vector.tensor_tensor(total[:], products[step, 0, 0], products[step, 1, 0], ADD)
-            nc.sync.dma_start(out[nt * P : (nt + 1) * P, t0 : t0 + width], total[:])
-
-        own_tile(0, "w_raw6_0")
-        first_products = [kept(f"kept0_{r}", T, f"w_grouped{r}_0") for r in range(2)]
+        kept = {}
+        y[0] = behind("y0", S, F32, "w_raw6_0")
+        own_chunks(0, range(CHUNKS))
         for r in range(2):
-            weigh(0, r, first_products[r][:])
-        gather_far_scales([2, 3], behind("far_scales2", 2 * CHUNK, U8, "w_raw6_0"))
-        first_sum = kept("first_sum", T, "xo_raw0_0")
-        nc.gpsimd.tensor_tensor(first_sum[:], first_products[0][:], first_products[1][:], ADD)
+            kept[0, r] = behind(f"kept0_{r}", T, F32, f"w_grouped{r}_0")
+        for r in range(2):
+            weigh(kept[0, r][:], 0, r, 0, T)
+        gather_far_scales([2, 3], "w_raw6_0")
+        first_sum = behind("first_sum", T, F32, "xo_raw0")
+        nc.gpsimd.tensor_tensor(first_sum[:], kept[0, 0][:], kept[0, 1][:], ADD)
         nc.sync.dma_start(out[0:P, 0:T], first_sum[:])
-        own_tile(1, "w_raw2_0")
-        far_part(0, 0)
+
+        y[1] = behind("y1", S, F32, "w_raw2_0")
+        own_chunks(1, range(CHUNKS))
+        far_part(0, 0, "w_raw5_0")
         for e in range(WHOLE, E):
             round_w(e, 1)
         quantize_w(3, 1, 1)
         quantize_w(4, 2, 1)
-        weigh(1, 0, kept("kept1_0", T, f"w_raw5_{HALF}")[:])
+        kept[1, 0] = behind("kept1_0", T, F32, f"w_raw5_{HALF}")
+        weigh(kept[1, 0][:], 1, 0, 0, T)
         quantize_w(6, 2, 1)
-        weigh(1, 1, kept("kept1_1", T, f"w_raw7_{HALF}")[:])
-        far_part(1, 0)
-        own_tile(2, "w_raw0_0", range(2))
-        far_part(0, 1)
-        own_tile(2, None, range(2, CHUNKS))
-        far_part(1, 1)
-        far_part(2, 0)
-        own_tile(3, "w_raw1_0")
-        last_kept = [kept("kept2_0", T, "w_grouped3_0"), kept("kept2_1", T, "w_grouped2_0")]
-        for b0 in range(0, T, CHUNK):
-            for r in range(2):
-                weigh(2, r, last_kept[r][:, b0 : b0 + CHUNK], b0)
+        kept[1, 1] = behind("kept1_1", T, F32, f"w_raw7_{HALF}")
+        weigh(kept[1, 1][:], 1, 1, 0, T)
 
-        spans = [(step, b0) for step in TENSOR_STEPS for b0 in range(0, STEPS[step][2], CHUNK)]
+        far_part(1, 0, "pairs1")
+        y[2] = behind("y2", S, F32, "w_raw0_0")
+        own_chunks(2, range(2))
+        far_part(0, 1, f"w_raw4_{HALF}")
+        own_chunks(2, range(2, CHUNKS))
+        far_part(1, 1, "z11")
+        far_part(2, 0, "w_grouped2_1")
+        y[3] = behind("y3", S, F32, "w_raw1_0")
+        own_chunks(3, range(CHUNKS))
+        kept[2, 0] = behind("kept2_0", T, F32, "w_grouped3_0")
+        kept[2, 1] = behind("kept2_1", T, F32, "w_grouped2_0")
+        for t0 in range(0, T, CHUNK):
+            for r in range(2):
+                weigh(kept[2, r][:, t0 : t0 + CHUNK], 2, r, t0, CHUNK)
+
+        spans = [(nt, t0) for nt in (1, 2) for t0 in range(0, T, CHUNK)]
         turned = {}
-        summed_tags = ["summed0", "summed1", "picked0", "summed3"]
 
         def turn(index):
-            step, b0 = spans[index]
+            nt, t0 = spans[index]
             bank = psum.tile([P, CHUNK], F32, name="bank", bufs=CHUNKS)
             for b in range(0, CHUNK, P):
                 for r in range(2):
                     nc.tensor.matmul(
                         bank[:, b : b + P],
-                        products[step, r, b0][:, b : b + P],
+                        kept[nt, r][:, t0 + b : t0 + b + P],
                         identity[:],
                         start=r == 0,
                         stop=r == 1,
                         is_transpose=True,
                     )
-            turned[index] = sbuf.tile([P, CHUNK], F32, name=f"turned{index}", tag=f"grouped{index}", align_bytes=64)
+            turned[index] = behind(f"turned{index}", CHUNK, F32, f"grouped{index}")
             nc.scalar.copy(turned[index][:], bank[:])
 
-        def turn_back(index):
-            step, b0 = spans[index]
-            nt, t0 = STEPS[step][:2]
+        def turn_back(index, tag, pieces=1):
+            nt, t0 = spans[index]
             bank = psum.tile([P, CHUNK], F32, name="back_bank", bufs=CHUNKS)
             for b in range(0, CHUNK, P):
                 nc.tensor.transpose(bank[:, b : b + P], turned[index][:, b : b + P], identity[:])
-            summed = sbuf.tile([P, CHUNK], F32, name=f"summed{index}", tag=summed_tags[index], align_bytes=64)
-            nc.scalar.copy(summed[:], bank[:])
-            nc.sync.dma_start(out[nt * P : (nt + 1) * P, t0 + b0 : t0 + b0 + CHUNK], summed[:])
+            summed = behind(f"summed{index}", CHUNK, F32, tag)
+            width = CHUNK // pieces
+            for b in range(0, CHUNK, width):
+                nc.scalar.copy(summed[:, b : b + width], bank[:, b : b + width])
+                nc.sync.dma_start(out[nt * P : (nt + 1) * P, t0 + b : t0 + b + width], summed[:, b : b + width])
 
-        far_part(2, 1)
-        far_part(3, 0)
+        far_part(2, 1, "xo_raw1")
+        far_part(3, 0, "w_raw4_0")
+        far_part(3, 1, "w_grouped3_1")
         turn(0)
         turn(1)
-        far_part(3, 1)
         turn(2)
-        turn_back(0)
+        turn_back(0, "summed0")
         turn(3)
-        for index in range(1, len(spans)):
-            turn_back(index)
+        turn_back(1, "summed1")
+        turn_back(2, "picked0")
+        turn_back(3, "summed3", pieces=2)
 
-        for step in range(FIRST_VECTOR_STEP, len(STEPS)):
-            weigh(step, 0, sbuf.tile([P, STEPS[step][2]], F32, name="product0", bufs=2)[:])
-            if step > FIRST_VECTOR_STEP:
+        total_tags = ["grouped0", "grouped2", "grouped3"]
+        products = {}
+
+        def weigh_step(step, r):
+            t0, width = LAST_STEPS[step]
+            products[step, r] = sbuf.tile([P, width], F32, name=f"product{r}", bufs=2)
+            weigh(products[step, r][:], 3, r, t0, width)
+
+        def add_and_store(step):
+            t0, width = LAST_STEPS[step]
+            total = behind(f"total{step}", width, F32, total_tags[step])
+            nc.vector.tensor_tensor(total[:], products[step, 0][:], products[step, 1][:], ADD)
+            nc.sync.dma_start(out[3 * P : 4 * P, t0 : t0 + width], total[:])
+
+        for step in range(len(LAST_STEPS)):
+            weigh_step(step, 0)
+            if step > 0:
                 add_and_store(step - 1)
-            weigh(step, 1, sbuf.tile([P, STEPS[step][2]], F32, name="product1", bufs=2)[:])
-        add_and_store(len(STEPS) - 1)
+            weigh_step(step, 1)
+        add_and_store(len(LAST_STEPS) - 1)

@@ -24,6 +24,7 @@ CHUNK = 512
 CHUNKS = S // CHUNK
 HALF = N // 2
 
+PADDED = 1376
 WHOLE = 3
 LAST_STEPS = [(0, 512), (512, 256), (768, 256)]
 
@@ -45,13 +46,14 @@ def tile_moe_loc_lin_silu_kernel(tc, x_words, x_scales, xo, w, gate, offs, pos1,
         offs_t = sbuf.tile([P, S // PER_COLUMN], U16, name="offs_t")
         pos_t = [sbuf.tile([P, T // PER_COLUMN], U16, name=f"pos_t{r}") for r in range(2)]
         gate_t = [sbuf.tile([P, T], F32, name=f"gate_t{r}") for r in range(2)]
-        token_words = sbuf.tile([P, Q], I32, name="token_words")
-        token_scales = sbuf.tile([P, Q // 4], I32, name="token_scales", align_bytes=64)
+        token_words = sbuf.tile([P, PADDED], I32, name="token_words")
+        token_scales = sbuf.tile([P, PADDED // 4], I32, name="token_scales", align_bytes=64)
         xo_raw = [sbuf.tile([P, 2, T], F32, name=f"xo_raw{a}", align_bytes=64) for a in range(2)]
 
         nc.vector.memset(token_scales[:], 0)
         nc.sync.dma_start(offs2_t[:], offs2)
-        nc.sync.dma_start(token_words[:], x_words[0].rearrange("p t d -> p (t d)").bitcast(I32))
+        nc.vector.memset(token_words[:, Q:PADDED], 0)
+        nc.sync.dma_start(token_words[:, 0:Q], x_words[0].rearrange("p t d -> p (t d)").bitcast(I32))
 
         warm = sbuf.tile([P, 16], F32, name="warm")
         nc.vector.memset(warm[:, 0:8], 0.0)
@@ -61,8 +63,6 @@ def tile_moe_loc_lin_silu_kernel(tc, x_words, x_scales, xo, w, gate, offs, pos1,
         nc.sync.dma_start(xo_raw[0][:], xo_rows[:, 0:2, :])
         nc.sync.dma_start(offs_t[:], offs)
         nc.sync.dma_start(xo_raw[1][:], xo_rows[:, 2:4, :])
-        for q in range(4):
-            nc.sync.dma_start(token_scales[32 * q : 32 * q + 4, :], x_scales[0, 4 * q : 4 * q + 4, :].bitcast(I32))
 
         w_raw = {}
 
@@ -72,6 +72,9 @@ def tile_moe_loc_lin_silu_kernel(tc, x_words, x_scales, xo, w, gate, offs, pos1,
 
         for e in range(E):
             load_w(e, 0, N if e < WHOLE else HALF)
+            if e == WHOLE - 1:
+                for q in range(4):
+                    nc.sync.dma_start(token_scales[32 * q : 32 * q + 4, 0 : Q // 4], x_scales[0, 4 * q : 4 * q + 4, :].bitcast(I32))
         for r, pos in enumerate((pos1, pos2)):
             nc.sync.dma_start(pos_t[r][:], pos)
             nc.sync.dma_start(gate_t[r][:], gate[r])
@@ -92,14 +95,15 @@ def tile_moe_loc_lin_silu_kernel(tc, x_words, x_scales, xo, w, gate, offs, pos1,
         def gather_far(chunks, gathered, table, found):
             for place, c in enumerate(chunks):
                 found[c] = gathered[:, place * CHUNK : (place + 1) * CHUNK]
-                nc.vector.tensor_copy(found[c], table.indirect(list_columns(offs2_t, c * CHUNK, CHUNK)))
+            nc.vector.tensor_copy(gathered, table.indirect(list_columns(offs2_t, chunks[0] * CHUNK, len(chunks) * CHUNK)))
 
         def gather_far_scales(chunks, tag):
             gathered = behind(f"far_scales{chunks[0]}", len(chunks) * CHUNK, U8, tag)
-            gather_far(chunks, gathered, token_scales[:].bitcast(U8), far_scales)
+            gather_far(chunks, gathered[:], token_scales[:].bitcast(U8), far_scales)
 
         far_words = sbuf.tile([P, S], U32, name="far_words", align_bytes=64)
-        gather_far(range(CHUNKS), far_words, token_words[:].bitcast(U32), far_codes)
+        for c in range(0, CHUNKS, 2):
+            gather_far([c, c + 1], far_words[:, c * CHUNK : (c + 2) * CHUNK], token_words[:].bitcast(U32), far_codes)
 
         two_chunks = [behind("picked0", 4 * CHUNK, I32, "picked0"), behind("picked1", 4 * CHUNK, I32, "xo_raw1")]
         picked = [two_chunks[c // 2][:, c % 2 * 2 * CHUNK : (c % 2 + 1) * 2 * CHUNK] for c in range(CHUNKS)]
@@ -248,9 +252,9 @@ def tile_moe_loc_lin_silu_kernel(tc, x_words, x_scales, xo, w, gate, offs, pos1,
         own_chunks(3, range(CHUNKS))
         kept[2, 0] = behind("kept2_0", T, F32, "w_grouped3_0")
         kept[2, 1] = behind("kept2_1", T, F32, "w_grouped2_0")
+        weigh(kept[2, 0][:], 2, 0, 0, T)
         for t0 in range(0, T, CHUNK):
-            for r in range(2):
-                weigh(kept[2, r][:, t0 : t0 + CHUNK], 2, r, t0, CHUNK)
+            weigh(kept[2, 1][:, t0 : t0 + CHUNK], 2, 1, t0, CHUNK)
 
         spans = [(nt, t0) for nt in (1, 2) for t0 in range(0, T, CHUNK)]
         turned = {}
@@ -294,7 +298,7 @@ def tile_moe_loc_lin_silu_kernel(tc, x_words, x_scales, xo, w, gate, offs, pos1,
         turn_back(2, "picked0")
         turn_back(3, "summed3", pieces=2)
 
-        total_tags = ["grouped0", "grouped2", "grouped3"]
+        totals = [behind("total0", CHUNK, F32, "grouped0"), behind("total1", CHUNK, F32, "grouped3")]
         products = {}
 
         def weigh_step(step, r):
@@ -304,13 +308,16 @@ def tile_moe_loc_lin_silu_kernel(tc, x_words, x_scales, xo, w, gate, offs, pos1,
 
         def add_and_store(step):
             t0, width = LAST_STEPS[step]
-            total = behind(f"total{step}", width, F32, total_tags[step])
-            nc.vector.tensor_tensor(total[:], products[step, 0][:], products[step, 1][:], ADD)
-            nc.sync.dma_start(out[3 * P : 4 * P, t0 : t0 + width], total[:])
+            total = totals[t0 // CHUNK][:, t0 % CHUNK : t0 % CHUNK + width]
+            nc.vector.tensor_tensor(total, products[step, 0][:], products[step, 1][:], ADD)
+            nc.sync.dma_start(out[3 * P : 4 * P, t0 : t0 + width], total)
 
-        for step in range(len(LAST_STEPS)):
-            weigh_step(step, 0)
-            if step > 0:
-                add_and_store(step - 1)
-            weigh_step(step, 1)
-        add_and_store(len(LAST_STEPS) - 1)
+        weigh_step(0, 0)
+        weigh_step(0, 1)
+        weigh_step(1, 0)
+        add_and_store(0)
+        weigh_step(1, 1)
+        weigh_step(2, 0)
+        weigh_step(2, 1)
+        add_and_store(1)
+        add_and_store(2)

@@ -50,9 +50,11 @@ def tile_moe_loc_lin_silu_kernel(tc, x_words, x_scales, xo, w, gate, offs, pos1,
         token_scales = sbuf.tile([P, PADDED // 4], I32, name="token_scales", align_bytes=64)
         xo_raw = [sbuf.tile([P, 2, T], F32, name=f"xo_raw{a}", align_bytes=64) for a in range(2)]
 
-        nc.vector.memset(token_scales[:], 0)
+        for c0 in range(0, PADDED // 4, PADDED // 16):
+            nc.vector.memset(token_scales[:, c0 : c0 + PADDED // 16], 0)
         nc.sync.dma_start(offs2_t[:], offs2)
-        nc.vector.memset(token_words[:, Q:PADDED], 0)
+        for c0 in range(Q, PADDED, (PADDED - Q) // 4):
+            nc.vector.memset(token_words[:, c0 : c0 + (PADDED - Q) // 4], 0)
         nc.sync.dma_start(token_words[:, 0:Q], x_words[0].rearrange("p t d -> p (t d)").bitcast(I32))
 
         warm = sbuf.tile([P, 16], F32, name="warm")
@@ -63,6 +65,8 @@ def tile_moe_loc_lin_silu_kernel(tc, x_words, x_scales, xo, w, gate, offs, pos1,
         nc.sync.dma_start(xo_raw[0][:], xo_rows[:, 0:2, :])
         nc.sync.dma_start(offs_t[:], offs)
         nc.sync.dma_start(xo_raw[1][:], xo_rows[:, 2:4, :])
+        for q in range(4):
+            nc.sync.dma_start(token_scales[32 * q : 32 * q + 4, 0 : Q // 4], x_scales[0, 4 * q : 4 * q + 4, :].bitcast(I32))
 
         w_raw = {}
 
@@ -72,9 +76,6 @@ def tile_moe_loc_lin_silu_kernel(tc, x_words, x_scales, xo, w, gate, offs, pos1,
 
         for e in range(E):
             load_w(e, 0, N if e < WHOLE else HALF)
-            if e == WHOLE - 1:
-                for q in range(4):
-                    nc.sync.dma_start(token_scales[32 * q : 32 * q + 4, 0 : Q // 4], x_scales[0, 4 * q : 4 * q + 4, :].bitcast(I32))
         for r, pos in enumerate((pos1, pos2)):
             nc.sync.dma_start(pos_t[r][:], pos)
             nc.sync.dma_start(gate_t[r][:], gate[r])

from contextlib import ExitStack

import concourse.mybir as mybir
from concourse.masks import make_identity

K, T, Q, E, C, N = 512, 1024, 768, 8, 256, 512
S = E * C
FLOPS = 2 * 2 * K * N * S

F32 = mybir.dt.float32
BF16 = mybir.dt.bfloat16
I32 = mybir.dt.int32
U32 = mybir.dt.uint32
U16 = mybir.dt.uint16
U8 = mybir.dt.uint8
FP8X4 = mybir.dt.float8_e4m3fn_x4
MULT = mybir.AluOpType.mult
ADD = mybir.AluOpType.add
SILU = mybir.ActivationFunctionType.Silu

P = 128
PER_COLUMN = 16
CHUNK = 512
CHUNKS = S // CHUNK
HALF = N // 2

PADDED = 1376
WHOLE = 3
LAST_STEPS = [(0, 512), (512, 256), (768, 256)]


def list_columns(list_tile, first, count):
    return list_tile[:, first // PER_COLUMN : (first + count) // PER_COLUMN]


def tile_moe_loc_lin_silu_kernel(tc, x_words, x_scales, xo, w, gate, offs, pos1, pos2, offs2, out):
    nc = tc.nc
    with ExitStack() as ctx:
        sbuf = ctx.enter_context(tc.tile_pool(name="sbuf", bufs=1))
        psum = ctx.enter_context(tc.psum_pool(name="psum", bufs=1))

        def behind(name, width, dtype, tag):
            return sbuf.tile([P, width], dtype, name=name, tag=tag, align_bytes=64)

        offs2_t = sbuf.tile([P, S // PER_COLUMN], U16, name="offs2_t")
        offs_t = sbuf.tile([P, S // PER_COLUMN], U16, name="offs_t")
        pos_t = [sbuf.tile([P, T // PER_COLUMN], U16, name=f"pos_t{r}") for r in range(2)]
        gate_t = [sbuf.tile([P, T], F32, name=f"gate_t{r}") for r in range(2)]
        token_words = sbuf.tile([P, PADDED], I32, name="token_words")
        token_scales = sbuf.tile([P, PADDED // 4], I32, name="token_scales", align_bytes=64)
        xo_raw = [sbuf.tile([P, 2, T], F32, name=f"xo_raw{a}", align_bytes=64) for a in range(2)]

        for c0 in range(0, PADDED // 4, PADDED // 16):
            nc.vector.memset(token_scales[:, c0 : c0 + PADDED // 16], 0)
        nc.sync.dma_start(offs2_t[:], offs2)
        for c0 in range(Q, PADDED, (PADDED - Q) // 4):
            nc.vector.memset(token_words[:, c0 : c0 + (PADDED - Q) // 4], 0)
        nc.sync.dma_start(token_words[:, 0:Q], x_words[0].rearrange("p t d -> p (t d)").bitcast(I32))

        warm = sbuf.tile([P, 16], F32, name="warm")
        nc.vector.memset(warm[:, 0:8], 0.0)
        nc.scalar.activation(warm[:, 8:16], warm[:, 0:8], SILU)

        xo_rows = xo.rearrange("(p j) t -> p j t", j=4)
        nc.sync.dma_start(xo_raw[0][:], xo_rows[:, 0:2, :])
        nc.sync.dma_start(offs_t[:], offs)
        nc.sync.dma_start(xo_raw[1][:], xo_rows[:, 2:4, :])
        for q in range(4):
            nc.sync.dma_start(token_scales[32 * q : 32 * q + 4, 0 : Q // 4], x_scales[0, 4 * q : 4 * q + 4, :].bitcast(I32))

        w_raw = {}

        def load_w(e, n0, width):
            w_raw[e, n0] = sbuf.tile([P, 4, width], F32, name=f"w_raw{e}_{n0}", align_bytes=64)
            nc.sync.dma_start(w_raw[e, n0][:], w[e].rearrange("(p j) n -> p j n", j=4)[:, :, n0 : n0 + width])

        for e in range(E):
            load_w(e, 0, N if e < WHOLE else HALF)
        for r, pos in enumerate((pos1, pos2)):
            nc.sync.dma_start(pos_t[r][:], pos)
            nc.sync.dma_start(gate_t[r][:], gate[r])
        for e in range(WHOLE, E):
            load_w(e, HALF, HALF)

        pairs = [sbuf.tile([P, 2 * T], BF16, name=f"pairs{a}", align_bytes=64) for a in range(2)]
        for a in range(2):
            nc.scalar.copy(
                pairs[a][:].rearrange("p (g t i) -> p g i t", t=4, i=2),
                xo_raw[a][:].rearrange("p i (g t) -> p g i t", t=4),
            )

        own_codes = sbuf.tile([P, S], U32, name="own_codes", align_bytes=64)
        own_scales = sbuf.tile([P, S], U8, name="own_scales", align_bytes=64)
        far_codes, far_scales = {}, {}

        def gather_far(chunks, gathered, table, found):
            for place, c in enumerate(chunks):
                found[c] = gathered[:, place * CHUNK : (place + 1) * CHUNK]
            nc.vector.tensor_copy(gathered, table.indirect(list_columns(offs2_t, chunks[0] * CHUNK, len(chunks) * CHUNK)))

        def gather_far_scales(chunks, tag):
            gathered = behind(f"far_scales{chunks[0]}", len(chunks) * CHUNK, U8, tag)
            gather_far(chunks, gathered[:], token_scales[:].bitcast(U8), far_scales)

        far_words = sbuf.tile([P, S], U32, name="far_words", align_bytes=64)
        for c in range(0, CHUNKS, 2):
            gather_far([c, c + 1], far_words[:, c * CHUNK : (c + 2) * CHUNK], token_words[:].bitcast(U32), far_codes)

        two_chunks = [behind("picked0", 4 * CHUNK, I32, "picked0"), behind("picked1", 4 * CHUNK, I32, "xo_raw1")]
        picked = [two_chunks[c // 2][:, c % 2 * 2 * CHUNK : (c % 2 + 1) * 2 * CHUNK] for c in range(CHUNKS)]
        grouped = {}

        def gather_own(c):
            for a in range(2):
                nc.vector.tensor_copy(
                    picked[c][:, a * CHUNK : (a + 1) * CHUNK].bitcast(U32),
                    pairs[a][:].bitcast(U32).indirect(list_columns(offs_t, c * CHUNK, CHUNK)),
                )

        def weave(c, copy, dtype, first, count):
            copy(
                grouped[c][:].bitcast(dtype).rearrange("p (s a) -> p s a", a=2)[:, first : first + count, :],
                picked[c].bitcast(dtype).rearrange("p (a s) -> p s a", a=2)[:, first : first + count, :],
            )

        for c in range(CHUNKS):
            gather_own(c)
            if c < CHUNKS - 1:
                grouped[c] = behind(f"grouped{c}", 4 * CHUNK, BF16, f"grouped{c}")
                weave(c, nc.gpsimd.tensor_copy, I32, 0, CHUNK if c < 2 else CHUNK // 2)
        gather_far_scales([0], "pairs0")
        weave(2, nc.vector.tensor_copy, I32, CHUNK // 2, CHUNK // 2)

        w_grouped = {}

        def round_w(e, half):
            c, u = divmod(e, 2)
            if u == 0:
                w_grouped[c, half] = sbuf.tile([P, 8 * HALF], BF16, name=f"w_grouped{c}_{half}", align_bytes=64)
            raw = w_raw[e, 0][:, :, half * HALF : (half + 1) * HALF] if e < WHOLE else w_raw[e, half * HALF][:]
            nc.scalar.copy(
                w_grouped[c, half][:, u * 4 * HALF : (u + 1) * 4 * HALF].rearrange("p (g i j) -> p g j i", i=2, j=4),
                raw.rearrange("p j (g i) -> p g j i", i=2),
            )

        for e in range(E):
            for half in range(2 if e < WHOLE else 1):
                round_w(e, half)
            if e == WHOLE:
                grouped[CHUNKS - 1] = behind(f"grouped{CHUNKS - 1}", 4 * CHUNK, BF16, f"w_raw{e}_0")
                weave(CHUNKS - 1, nc.scalar.copy, U32, 0, CHUNK)

        w_codes, w_scales = {}, {}

        def quantize_w(first, count, half, scales=None):
            c, u = divmod(first, 2)
            if u == 0:
                w_codes[c, half] = sbuf.tile([P, 2 * HALF], U32, name=f"w_codes{c}_{half}", align_bytes=64)
                if scales is None:
                    scales = sbuf.tile([P, 2 * HALF], U8, name=f"w_scales{c}_{half}", align_bytes=64)[:]
                w_scales[c, half] = scales
            cols = slice(u * HALF, (u + count) * HALF)
            nc.vector.quantize_mx(
                out=w_codes[c, half][:, cols].bitcast(FP8X4),
                scales=w_scales[c, half][:, cols],
                in_=w_grouped[c, half][:, 4 * u * HALF : 4 * (u + count) * HALF],
            )

        for c in range(CHUNKS):
            slots = slice(c * CHUNK, (c + 1) * CHUNK)
            nc.vector.quantize_mx(out=own_codes[:, slots].bitcast(FP8X4), scales=own_scales[:, slots], in_=grouped[c][:])
            if c < CHUNKS - 1:
                quantize_w(2 * c, 2, 0)
        quantize_w(E - 2, 1, 0)
        quantize_w(E - 1, 1, 0)
        held_scales = behind("held_scales", 2 * CHUNK, U8, f"w_raw{E - 1}_0")
        quantize_w(0, 2, 1, held_scales[:, 0:CHUNK])
        quantize_w(2, 1, 1, held_scales[:, CHUNK:])
        gather_far_scales([1], "w_grouped0_1")

        def experts(c, nt, codes, scales, dest):
            bank = psum.tile([P, CHUNK], F32, name="bank", bufs=CHUNKS)
            half, row0 = divmod(nt * P, HALF)
            for u in range(2):
                rows = slice(u * HALF + row0, u * HALF + row0 + P)
                nc.tensor.matmul_mx(
                    out=bank[:, u * C : (u + 1) * C],
                    lhsT=w_codes[c, half][:, rows].bitcast(FP8X4),
                    lhsT_scale=w_scales[c, half][:, rows],
                    rhs=codes[:, u * C : (u + 1) * C].bitcast(FP8X4),
                    rhs_scale=scales[:, u * C : (u + 1) * C],
                    start=True,
                    stop=True,
                )
            nc.scalar.activation(dest, bank[:], SILU)

        y = {}

        def own_chunks(nt, chunks):
            for c in chunks:
                slots = slice(c * CHUNK, (c + 1) * CHUNK)
                experts(c, nt, own_codes[:, slots], own_scales[:, slots], y[nt][:, slots])

        def far_part(nt, part, tag):
            z = behind(f"z{nt}{part}", 2 * CHUNK, F32, tag)
            for u in range(2):
                c = 2 * part + u
                experts(c, nt, far_codes[c], far_scales[c], z[:, u * CHUNK : (u + 1) * CHUNK])
            s0 = T + 2 * part * CHUNK
            nc.sync.dma_start(out[nt * P : (nt + 1) * P, s0 : s0 + 2 * CHUNK], z[:])

        identity = sbuf.tile([P, P], F32, name="identity")
        make_identity(nc, identity[:])

        def weigh(product, nt, r, t0, width):
            nc.vector.tensor_tensor(
                product, y[nt][:].indirect(list_columns(pos_t[r], t0, width)), gate_t[r][:, t0 : t0 + width], MULT
            )

        kept = {}
        y[0] = behind("y0", S, F32, "w_raw6_0")
        own_chunks(0, range(CHUNKS))
        for r in range(2):
            kept[0, r] = behind(f"kept0_{r}", T, F32, f"w_grouped{r}_0")
        for r in range(2):
            weigh(kept[0, r][:], 0, r, 0, T)
        gather_far_scales([2, 3], "w_raw6_0")
        first_sum = behind("first_sum", T, F32, "xo_raw0")
        nc.gpsimd.tensor_tensor(first_sum[:], kept[0, 0][:], kept[0, 1][:], ADD)
        nc.sync.dma_start(out[0:P, 0:T], first_sum[:])

        y[1] = behind("y1", S, F32, "w_raw2_0")
        own_chunks(1, range(CHUNKS))
        far_part(0, 0, "w_raw5_0")
        for e in range(WHOLE, E):
            round_w(e, 1)
        quantize_w(3, 1, 1)
        quantize_w(4, 2, 1)
        kept[1, 0] = behind("kept1_0", T, F32, f"w_raw5_{HALF}")
        weigh(kept[1, 0][:], 1, 0, 0, T)
        quantize_w(6, 2, 1)
        kept[1, 1] = behind("kept1_1", T, F32, f"w_raw7_{HALF}")
        weigh(kept[1, 1][:], 1, 1, 0, T)

        far_part(1, 0, "pairs1")
        y[2] = behind("y2", S, F32, "w_raw0_0")
        own_chunks(2, range(2))
        far_part(0, 1, f"w_raw4_{HALF}")
        own_chunks(2, range(2, CHUNKS))
        far_part(1, 1, "z11")
        far_part(2, 0, "w_grouped2_1")
        y[3] = behind("y3", S, F32, "w_raw1_0")
        own_chunks(3, range(CHUNKS))
        kept[2, 0] = behind("kept2_0", T, F32, "w_grouped3_0")
        kept[2, 1] = behind("kept2_1", T, F32, "w_grouped2_0")
        weigh(kept[2, 0][:], 2, 0, 0, T)
        for t0 in range(0, T, CHUNK):
            weigh(kept[2, 1][:, t0 : t0 + CHUNK], 2, 1, t0, CHUNK)

        spans = [(nt, t0) for nt in (1, 2) for t0 in range(0, T, CHUNK)]
        turned = {}

        def turn(index):
            nt, t0 = spans[index]
            bank = psum.tile([P, CHUNK], F32, name="bank", bufs=CHUNKS)
            for b in range(0, CHUNK, P):
                for r in range(2):
                    nc.tensor.matmul(
                        bank[:, b : b + P],
                        kept[nt, r][:, t0 + b : t0 + b + P],
                        identity[:],
                        start=r == 0,
                        stop=r == 1,
                        is_transpose=True,
                    )
            turned[index] = behind(f"turned{index}", CHUNK, F32, f"grouped{index}")
            nc.scalar.copy(turned[index][:], bank[:])

        def turn_back(index, tag, pieces=1):
            nt, t0 = spans[index]
            bank = psum.tile([P, CHUNK], F32, name="back_bank", bufs=CHUNKS)
            for b in range(0, CHUNK, P):
                nc.tensor.transpose(bank[:, b : b + P], turned[index][:, b : b + P], identity[:])
            summed = behind(f"summed{index}", CHUNK, F32, tag)
            width = CHUNK // pieces
            for b in range(0, CHUNK, width):
                nc.scalar.copy(summed[:, b : b + width], bank[:, b : b + width])
                nc.sync.dma_start(out[nt * P : (nt + 1) * P, t0 + b : t0 + b + width], summed[:, b : b + width])

        far_part(2, 1, "xo_raw1")
        far_part(3, 0, "w_raw4_0")
        far_part(3, 1, "w_grouped3_1")
        turn(0)
        turn(1)
        turn(2)
        turn_back(0, "summed0")
        turn(3)
        turn_back(1, "summed1")
        turn_back(2, "picked0")
        turn_back(3, "summed3", pieces=2)

        totals = [behind("total0", CHUNK, F32, "grouped0"), behind("total1", CHUNK, F32, "grouped3")]
        products = {}

        def weigh_step(step, r):
            t0, width = LAST_STEPS[step]
            products[step, r] = sbuf.tile([P, width], F32, name=f"product{r}", bufs=2)
            weigh(products[step, r][:], 3, r, t0, width)

        def add_and_store(step):
            t0, width = LAST_STEPS[step]
            total = totals[t0 // CHUNK][:, t0 % CHUNK : t0 % CHUNK + width]
            nc.vector.tensor_tensor(total, products[step, 0][:], products[step, 1][:], ADD)
            nc.sync.dma_start(out[3 * P : 4 * P, t0 : t0 + width], total)

        weigh_step(0, 0)
        weigh_step(0, 1)
        weigh_step(1, 0)
        add_and_store(0)
        weigh_step(1, 1)
        weigh_step(2, 0)
        weigh_step(2, 1)
        add_and_store(1)
        add_and_store(2)
